import numpy as np
import ml_dtypes


def mxq(x, axis, fmt="e4m3"):
    dtype, down = {"e4m3": (ml_dtypes.float8_e4m3fn, 7), "e5m2": (ml_dtypes.float8_e5m2, 14)}[fmt]
    v = np.moveaxis(np.asarray(x, np.float32).astype(ml_dtypes.bfloat16).astype(np.float64), axis, -1)
    blocks = v.reshape(v.shape[:-1] + (-1, 32))
    amax = np.abs(blocks).max(-1, keepdims=True)
    byte = np.maximum(np.where(amax > 0, np.frexp(amax)[1] - 1 + 127, 0) - down, 1)
    scale = np.exp2(byte - 127.0)
    codes = (blocks / scale).astype(np.float32).astype(dtype).astype(np.float64)
    return np.moveaxis((codes * scale).reshape(v.shape), -1, axis)


WIDE = False


def mx_kscale(k):
    if not WIDE:
        return np.ones(k)
    levels = np.array([10, -10, 5, -5, 0])
    if k % 512:
        return np.exp2(np.random.permutation(np.resize(levels, k // 32))).repeat(32)
    a = np.empty((k // 512, 16))
    for p in range(k // 512):
        a[p, :8] = np.random.permutation(np.resize(levels, 8))
        for g in range(8):
            far = levels[np.abs(levels - a[p, g]) >= 10]
            a[p, g + 8] = far[np.random.randint(len(far))]
    return np.exp2(a.ravel()).repeat(32)


def f64(x):
    return np.asarray(x).astype(np.float64)


def striped(idx):
    return np.tile(idx.reshape(-1, 16).T, (8, 1)).astype(np.uint16)


def unstriped(offs):
    return offs[:16].T.reshape(-1).astype(np.int64)


E2M1 = np.array([0.0, 0.5, 1.0, 1.5, 2.0, 3.0, 4.0, 6.0, -0.0, -0.5, -1.0, -1.5, -2.0, -3.0, -4.0, -6.0])


def pack_weight(w, fmt):
    k, n = w.shape
    w = f64(np.asarray(w, np.float32).astype(ml_dtypes.bfloat16)).reshape(k // 32, 32, n)
    amax = np.abs(w).max(1)
    if fmt == "e4m3":
        byte = np.frexp(amax)[1] - 1 + 127 - 7
    else:
        mant, ex = np.frexp(amax / 6.0)
        byte = np.where(mant > 0.5, ex, ex - 1) + 127
    byte = np.clip(np.where(amax > 0, byte, 1), 1, 254)
    scaled = (w * np.exp2(127.0 - byte)[:, None, :]).reshape(k, n).astype(np.float32)
    by_word = np.ascontiguousarray(scaled.reshape(k // 512, 128, 4, n).transpose(0, 1, 3, 2))
    if fmt == "e4m3":
        words = by_word.astype(ml_dtypes.float8_e4m3fn).view(np.uint8)
    else:
        c = by_word.astype(ml_dtypes.float4_e2m1fn).view(np.uint8) & 0xF
        words = (c[..., 0::2] | (c[..., 1::2] << 4)).reshape(k // 512, 128, 2 * n)
    return np.ascontiguousarray(words), np.ascontiguousarray(byte.astype(np.uint8).reshape(k // 512, 16, n))


def unpack_weight(words, scales, fmt):
    g, _, n = scales.shape
    words = np.ascontiguousarray(words).reshape(g, 128, n, -1)
    if fmt == "e4m3":
        vals = words.view(ml_dtypes.float8_e4m3fn).astype(np.float64)
    else:
        nib = np.empty((g, 128, n, 4), np.uint8)
        nib[..., 0::2] = words & 0xF
        nib[..., 1::2] = words >> 4
        vals = E2M1[nib]
    vals = vals * np.repeat(np.exp2(scales.astype(np.float64) - 127.0), 8, axis=1)[..., None]
    return vals.transpose(0, 1, 3, 2).reshape(g * 512, n)


def d_silu(v):
    s = 1.0 / (1.0 + np.exp(-np.maximum(v, -700.0)))
    return s * (1.0 + v * (1.0 - s))


K, T, E, C, H, N, TOP = 128, 512, 6, 256, 512, 1024, 3


def by_expert(wq, xq):
    return np.concatenate([wq[e].T @ xq[:, e * C:(e + 1) * C] for e in range(E)], axis=1)


def setup_inputs():
    n = np.random.standard_normal
    v = mx_kscale(N)
    u = mx_kscale(H)
    deal = np.repeat(np.arange(E), C).reshape(TOP, T)[:, np.random.permutation(T)]
    deal = np.take_along_axis(deal, np.argsort(np.random.rand(TOP, T), axis=0), axis=0)
    for _ in range(8):
        s_, t_ = np.random.permutation(T).reshape(2, -1); r = np.random.randint(TOP, size=T // 2); x, y = deal[r, s_].copy(), deal[r, t_].copy()
        ok = ~((deal[:, s_] == y).any(0) | (deal[:, t_] == x).any(0)); deal[r[ok], s_[ok]] = y[ok]; deal[r[ok], t_[ok]] = x[ok]
    order = np.lexsort((np.random.rand(TOP * T), deal.reshape(-1)))
    slot_token = order % T; pos = np.empty(TOP * T, np.int64); pos[order] = np.arange(TOP * T); pos = pos.reshape(TOP, T)
    g = np.random.uniform(0.5, 1.5, (TOP, T)); g = g / g.sum(0)
    dy = pack_weight(n((N, T)) * v[:, None], "e4m3")
    w2t = [pack_weight(m, "e2m1") for m in n((E, N, H)) / np.sqrt(N) / v[None, :, None] * u]
    w1t = pack_weight(n((H, K)) / np.sqrt(H) / u[:, None], "e2m1")
    return {
        "dy_words": dy[0],
        "dy_scales": dy[1],
        "w2t_words": np.stack([m[0] for m in w2t]),
        "w2t_scales": np.stack([m[1] for m in w2t]),
        "w1t_words": w1t[0],
        "w1t_scales": w1t[1],
        "a": (n((H, T))).astype(np.float32),
        "gate": np.stack([np.tile(r, (128, 1)) for r in g]).astype(np.float32),
        "offs": striped(slot_token),
        "pos1": striped(pos[0]),
        "pos2": striped(pos[1]),
        "pos3": striped(pos[2]),
    }


def reference(dy_words, dy_scales, w2t_words, w2t_scales, w1t_words, w1t_scales, a, gate, offs, pos1, pos2, pos3):
    w2t = np.stack([unpack_weight(w2t_words[e], w2t_scales[e], "e2m1") for e in range(E)])
    w1t = unpack_weight(w1t_words, w1t_scales, "e2m1")
    idx = unstriped(offs)
    gq = unpack_weight(dy_words, dy_scales, "e4m3")[:, idx]
    y = by_expert(w2t, gq)
    dh = sum(f64(gate[r, :1]) * y[:, unstriped(p)] for r, p in enumerate((pos1, pos2, pos3)))
    return w1t.T @ mxq(dh * d_silu(f64(a)), 0, "e4m3")

@@ -1,0 +1,227 @@
+from contextlib import ExitStack
+
+import concourse.mybir as mybir
+from concourse.masks import make_identity
+
+K, T, E, C, H, N, TOP = 128, 512, 6, 256, 512, 1024, 3
+SLOTS = E * C
+FLOPS = 2 * N * H * SLOTS + 2 * H * K * T
+
+F32 = mybir.dt.float32
+BF16 = mybir.dt.bfloat16
+I32 = mybir.dt.int32
+U32 = mybir.dt.uint32
+U16 = mybir.dt.uint16
+U8 = mybir.dt.uint8
+FP8X4 = mybir.dt.float8_e4m3fn_x4
+FP4X4 = mybir.dt.float4_e2m1fn_x4
+ACT = mybir.ActivationFunctionType
+ALU = mybir.AluOpType
+
+P = 128
+PACK = 4
+PASSES = N // (P * PACK)
+QUADS = 4
+HT = H // P
+BLOCKS = T // P
+PER_COL = 16
+BANK = 512
+BYTE_PIECE = 768
+BYTE_GATHER = 384
+CHUNKS = ((0, 2), (2, 1), (3, 1))
+
+
+def tile_moe_sub_silu_kernel(
+    tc, dy_words, dy_scales, w2t_words, w2t_scales, w1t_words, w1t_scales, a, gate, offs, pos1, pos2, pos3, out
+):
+    nc = tc.nc
+    with ExitStack() as ctx:
+        keep = ctx.enter_context(tc.tile_pool(name="keep", bufs=1))
+        ring = ctx.enter_context(tc.tile_pool(name="ring", bufs=6))
+        psum = ctx.enter_context(tc.psum_pool(name="psum", bufs=8))
+
+        offs_sb = keep.tile([P, SLOTS // PER_COL], U16, name="offs_sb")
+        pos_sb = [keep.tile([P, T // PER_COL], U16, name="pos_sb%d" % r) for r in range(TOP)]
+        dy_w = keep.tile([P, PASSES, T], I32, name="dy_w", align_bytes=64)
+        dy_s = keep.tile([P, T], U8, name="dy_s", align_bytes=64)
+        w2_w = keep.tile([P, E * PASSES, 2 * H], U8, name="w2_w", align_bytes=64)
+        w2_s = keep.tile([P, E * PASSES, H], U8, name="w2_s", align_bytes=64)
+        w1_w = keep.tile([P, 2 * K], U8, name="w1_w", align_bytes=64)
+        w1_s = keep.tile([P, K], U8, name="w1_s", align_bytes=64)
+        pieces = SLOTS // BYTE_PIECE
+        slot_w = [keep.tile([P, PASSES, C], I32, name="slot_w%d" % e, align_bytes=64) for e in range(E)]
+        slot_s0 = [keep.tile([P, BYTE_PIECE], U8, name="slot_s0_%d" % i, align_bytes=64) for i in range(pieces)]
+        slot_s1 = [keep.tile([P, BYTE_PIECE], U8, name="slot_s1_%d" % i, align_bytes=64) for i in range(pieces)]
+        y = [keep.tile([P, SLOTS], F32, name="y%d" % j, align_bytes=64) for j in range(HT)]
+        a_sb = keep.tile([P, HT, T], F32, name="a_sb")
+        sig = keep.tile([P, HT, T], F32, name="sig")
+        silu_neg = keep.tile([P, T, PACK], F32, name="silu_neg")
+        gate_rows = keep.tile([P, P], F32, name="gate_rows")
+        gate_neg = keep.tile([P, TOP * BLOCKS], F32, name="gate_neg")
+        ident = keep.tile([P, P], F32, name="ident")
+
+        nc.gpsimd.memset(dy_s[:].bitcast(I32), 0)
+        nc.vector.memset(w2_s[:].rearrange("p a i -> p (a i)").bitcast(I32), 0)
+        for i in range(pieces):
+            nc.vector.memset(slot_s1[i][:].bitcast(I32), 0)
+        nc.vector.memset(w1_s[:].bitcast(I32), 0)
+        nc.gpsimd.memset(gate_rows[:], 0.0)
+        make_identity(nc, ident[:])
+
+        def load_w2(e0, e1):
+            nc.sync.dma_start(
+                w2_w[:, e0 * PASSES : e1 * PASSES, :].bitcast(I32),
+                w2t_words[e0:e1].rearrange("e s p b -> p (e s) b").bitcast(I32),
+            )
+
+        def gather_bytes(i):
+            for off in range(0, BYTE_PIECE, BYTE_GATHER):
+                col = (i * BYTE_PIECE + off) // PER_COL
+                nc.vector.tensor_copy(
+                    slot_s0[i][:, off : off + BYTE_GATHER],
+                    dy_s[:].indirect(offs_sb[:, col : col + BYTE_GATHER // PER_COL]),
+                )
+            for q in range(QUADS):
+                nc.sync.dma_start(
+                    slot_s1[i][32 * q : 32 * q + 4, :].bitcast(I32),
+                    slot_s0[i][32 * q + 4 : 32 * q + 8, :].bitcast(I32),
+                )
+
+        def gather_words(e):
+            cols = C // PER_COL
+            for s in range(PASSES):
+                nc.vector.tensor_copy(
+                    slot_w[e][:, s, :].bitcast(U32),
+                    dy_w[:, s, :].bitcast(U32).indirect(offs_sb[:, e * cols : (e + 1) * cols]),
+                )
+
+        def expert(e):
+            for j in range(HT):
+                y_bank = psum.tile([P, C], F32, name="bank")
+                for u in range(C // P):
+                    slot0 = e * C + u * P
+                    i, off = divmod(slot0, BYTE_PIECE)
+                    for s in range(PASSES):
+                        nc.tensor.matmul_mx(
+                            out=y_bank[:, u * P : (u + 1) * P],
+                            lhsT=w2_w[:, e * PASSES + s, 2 * P * j : 2 * P * (j + 1)].bitcast(FP4X4),
+                            lhsT_scale=w2_s[:, e * PASSES + s, P * j : P * (j + 1)],
+                            rhs=slot_w[e][:, s, u * P : (u + 1) * P].bitcast(FP8X4),
+                            rhs_scale=(slot_s0, slot_s1)[s][i][:, off : off + P],
+                            start=(s == 0),
+                            stop=(s == PASSES - 1),
+                        )
+                nc.scalar.copy(y[j][:, e * C : (e + 1) * C], y_bank[:])
+
+        nc.sync.dma_start(offs_sb[:], offs)
+        for q in range(QUADS):
+            nc.sync.dma_start(
+                dy_s[32 * q : 32 * q + 4 * PASSES, 0:T].bitcast(I32),
+                dy_scales[:, 4 * q : 4 * q + 4, :].bitcast(I32),
+            )
+        nc.sync.dma_start(dy_w[:], dy_words.rearrange("s p t d -> p s (t d)").bitcast(I32))
+        for r, pos in enumerate((pos1, pos2, pos3)):
+            nc.sync.dma_start(pos_sb[r][:], pos)
+        for q in range(QUADS):
+            nc.sync.dma_start(
+                w2_s[32 * q : 32 * q + 4, :, :].bitcast(I32),
+                w2t_scales[:, :, 4 * q : 4 * q + 4, :].rearrange("e s b i -> b (e s) i").bitcast(I32),
+            )
+        load_w2(0, 1)
+        gather_bytes(0)
+        load_w2(1, 3)
+        a_rows = a.rearrange("(j p) t -> p j t", p=P)
+        first = CHUNKS[0][1] * P
+        nc.gpsimd.dma_start(a_sb[:, :, 0:first], a_rows[:, :, 0:first])
+        gather_words(0)
+        gather_words(1)
+        gather_bytes(1)
+        load_w2(3, E)
+        nc.gpsimd.dma_start(gate_rows[0 : TOP * BLOCKS, :], gate[:, 0, :].rearrange("r (b p) -> r b p", p=P))
+        nc.gpsimd.dma_start(a_sb[:, :, first:T], a_rows[:, :, first:T])
+        nc.gpsimd.dma_start(w1_w[:].bitcast(I32), w1t_words[0].bitcast(I32))
+        for q in range(QUADS):
+            nc.gpsimd.dma_start(
+                w1_s[32 * q : 32 * q + 4, :].bitcast(I32), w1t_scales[0, 4 * q : 4 * q + 4, :].bitcast(I32)
+            )
+
+        nc.scalar.activation(sig[:, :, 0:first], a_sb[:, :, 0:first], ACT.Sigmoid)
+
+        for e in range(E):
+            if e >= 2:
+                gather_words(e)
+            expert(e)
+
+        gate_bank = psum.tile([P, BANK], F32, name="bank")
+        nc.tensor.transpose(gate_bank[:, 0:P], gate_rows[:], ident[:])
+        nc.scalar.activation(gate_neg[:], gate_bank[:, 0 : TOP * BLOCKS], ACT.Copy, scale=-1.0)
+
+        nc.scalar.activation(sig[:, :, first:T], a_sb[:, :, first:T], ACT.Sigmoid)
+        a_packed = keep.tile([P, PACK, T], F32, name="a_sb")
+        nc.sync.dma_start(a_packed[:], a.rearrange("(p d) t -> p d t", d=PACK))
+
+        for b0, nb in CHUNKS:
+            toks = slice(b0 * P, (b0 + nb) * P)
+            cols = slice(b0 * P // PER_COL, (b0 + nb) * P // PER_COL)
+            sums = [psum.tile([P, BANK], F32, name="bank") for b in range(nb)]
+            for r in range(TOP):
+                turned = [psum.tile([P, BANK], F32, name="bank") for b in range(nb)]
+                for j in range(HT):
+                    picked = ring.tile([P, nb * P], F32, name="picked")
+                    nc.vector.tensor_tensor(
+                        picked[:], y[j][:].indirect(pos_sb[r][:, cols]), sig[:, j, toks], ALU.mult
+                    )
+                    for b in range(nb):
+                        nc.tensor.transpose(
+                            turned[b][:, j * P : (j + 1) * P], picked[:, b * P : (b + 1) * P], ident[:]
+                        )
+                for b in range(nb):
+                    gated = ring.tile([P, PACK, P], F32, name="gated")
+                    col = r * BLOCKS + b0 + b
+                    nc.scalar.activation(
+                        gated[:],
+                        turned[b][:].rearrange("t (m d) -> t d m", d=PACK),
+                        ACT.Copy,
+                        scale=gate_neg[:, col : col + 1],
+                    )
+                    for d in range(PACK):
+                        nc.tensor.matmul(
+                            sums[b][:, d * P : (d + 1) * P],
+                            lhsT=gated[:, d, :],
+                            rhs=ident[:],
+                            is_transpose=True,
+                            start=(r == 0 and d == 0),
+                            stop=(r == TOP - 1 and d == PACK - 1),
+                        )
+            da = ring.tile([P, nb * P, PACK], BF16, name="da", align_bytes=64)
+            for b in range(nb):
+                blk = slice((b0 + b) * P, (b0 + b + 1) * P)
+                nc.scalar.activation(
+                    silu_neg[:, blk, :], a_packed[:, :, blk].rearrange("p d t -> p t d"), ACT.Silu, scale=-1.0
+                )
+                nc.vector.scalar_tensor_tensor(
+                    da[:, b * P : (b + 1) * P, :],
+                    silu_neg[:, blk, :],
+                    1.0,
+                    sums[b][:].rearrange("p (d t) -> p t d", d=PACK),
+                    ALU.subtract,
+                    ALU.mult,
+                )
+            da_w = ring.tile([P, nb * P], U32, name="da_w", align_bytes=64)
+            da_s = ring.tile([P, nb * P], U8, name="da_s", align_bytes=64)
+            nc.vector.quantize_mx(
+                out=da_w[:].bitcast(FP8X4), scales=da_s[:], in_=da[:].rearrange("p t d -> p (t d)")
+            )
+            res_bank = psum.tile([P, BANK], F32, name="bank")
+            nc.tensor.matmul_mx(
+                out=res_bank[:, 0 : nb * P],
+                lhsT=w1_w[:].bitcast(FP4X4),
+                lhsT_scale=w1_s[:],
+                rhs=da_w[:].bitcast(FP8X4),
+                rhs_scale=da_s[:],
+                start=True,
+                stop=True,
+            )
+            res = ring.tile([P, nb * P], F32, name="res")
+            nc.scalar.copy(res[:], res_bank[:, 0 : nb * P])
+            nc.sync.dma_start(out[:, toks], res[:])

@@ -26,9 +26,12 @@ HT = H // P
 BLOCKS = T // P
 PER_COL = 16
 BANK = 512
-BYTE_PIECE = 768
+BYTE_PIECES = ((0, 384), (384, 384), (768, 768))
+W2_ZERO_SPLIT = 8
 BYTE_GATHER = 384
-CHUNKS = ((0, 2), (2, 1), (3, 1))
+W2_BUFS = 3
+LAST_CHUNK = 2
+GATE_STEP = TOP * BLOCKS
 
 
 def tile_moe_sub_silu_kernel(
@@ -37,6 +40,7 @@ def tile_moe_sub_silu_kernel(
     nc = tc.nc
     with ExitStack() as ctx:
         keep = ctx.enter_context(tc.tile_pool(name="keep", bufs=1))
+        weights = ctx.enter_context(tc.tile_pool(name="weights", bufs=W2_BUFS))
         ring = ctx.enter_context(tc.tile_pool(name="ring", bufs=6))
         psum = ctx.enter_context(tc.psum_pool(name="psum", bufs=8))
 
@@ -44,39 +48,33 @@ def tile_moe_sub_silu_kernel(
         pos_sb = [keep.tile([P, T // PER_COL], U16, name="pos_sb%d" % r) for r in range(TOP)]
         dy_w = keep.tile([P, PASSES, T], I32, name="dy_w", align_bytes=64)
         dy_s = keep.tile([P, T], U8, name="dy_s", align_bytes=64)
-        w2_w = keep.tile([P, E * PASSES, 2 * H], U8, name="w2_w", align_bytes=64)
         w2_s = keep.tile([P, E * PASSES, H], U8, name="w2_s", align_bytes=64)
-        w1_w = keep.tile([P, 2 * K], U8, name="w1_w", align_bytes=64)
-        w1_s = keep.tile([P, K], U8, name="w1_s", align_bytes=64)
-        pieces = SLOTS // BYTE_PIECE
         slot_w = [keep.tile([P, PASSES, C], I32, name="slot_w%d" % e, align_bytes=64) for e in range(E)]
-        slot_s0 = [keep.tile([P, BYTE_PIECE], U8, name="slot_s0_%d" % i, align_bytes=64) for i in range(pieces)]
-        slot_s1 = [keep.tile([P, BYTE_PIECE], U8, name="slot_s1_%d" % i, align_bytes=64) for i in range(pieces)]
+        slot_s0 = [keep.tile([P, n], U8, name="slot_s0_%d" % first, align_bytes=64) for first, n in BYTE_PIECES]
+        slot_s1 = [keep.tile([P, n], U8, name="slot_s1_%d" % first, align_bytes=64) for first, n in BYTE_PIECES]
         y = [keep.tile([P, SLOTS], F32, name="y%d" % j, align_bytes=64) for j in range(HT)]
-        a_sb = keep.tile([P, HT, T], F32, name="a_sb")
         sig = keep.tile([P, HT, T], F32, name="sig")
         silu_neg = keep.tile([P, T, PACK], F32, name="silu_neg")
-        gate_rows = keep.tile([P, P], F32, name="gate_rows")
-        gate_neg = keep.tile([P, TOP * BLOCKS], F32, name="gate_neg")
+        gate_neg = keep.tile([P, P], F32, name="gate_neg")
         ident = keep.tile([P, P], F32, name="ident")
 
         nc.gpsimd.memset(dy_s[:].bitcast(I32), 0)
-        nc.vector.memset(w2_s[:].rearrange("p a i -> p (a i)").bitcast(I32), 0)
-        for i in range(pieces):
-            nc.vector.memset(slot_s1[i][:].bitcast(I32), 0)
-        nc.vector.memset(w1_s[:].bitcast(I32), 0)
-        nc.gpsimd.memset(gate_rows[:], 0.0)
+        nc.vector.memset(w2_s[:, 0:W2_ZERO_SPLIT, :].bitcast(I32), 0)
+        nc.gpsimd.memset(w2_s[:, W2_ZERO_SPLIT:, :].bitcast(I32), 0)
+        for plane in slot_s1:
+            nc.gpsimd.memset(plane[:].bitcast(I32), 0)
         make_identity(nc, ident[:])
 
-        def load_w2(e0, e1):
-            nc.sync.dma_start(
-                w2_w[:, e0 * PASSES : e1 * PASSES, :].bitcast(I32),
-                w2t_words[e0:e1].rearrange("e s p b -> p (e s) b").bitcast(I32),
-            )
+        w2_w = {}
+
+        def load_w2(e):
+            w2_w[e] = weights.tile([P, PASSES, 2 * H], U8, name="w2_w", align_bytes=64)
+            nc.sync.dma_start(w2_w[e][:].bitcast(I32), w2t_words[e].rearrange("s p b -> p s b").bitcast(I32))
 
         def gather_bytes(i):
-            for off in range(0, BYTE_PIECE, BYTE_GATHER):
-                col = (i * BYTE_PIECE + off) // PER_COL
+            first, n = BYTE_PIECES[i]
+            for off in range(0, n, BYTE_GATHER):
+                col = (first + off) // PER_COL
                 nc.vector.tensor_copy(
                     slot_s0[i][:, off : off + BYTE_GATHER],
                     dy_s[:].indirect(offs_sb[:, col : col + BYTE_GATHER // PER_COL]),
@@ -95,23 +93,27 @@ def tile_moe_sub_silu_kernel(
                     dy_w[:, s, :].bitcast(U32).indirect(offs_sb[:, e * cols : (e + 1) * cols]),
                 )
 
-        def expert(e):
-            for j in range(HT):
+        def expert(e, tiles):
+            for j in tiles:
                 y_bank = psum.tile([P, C], F32, name="bank")
                 for u in range(C // P):
                     slot0 = e * C + u * P
-                    i, off = divmod(slot0, BYTE_PIECE)
+                    i = max(i for i, (first, n) in enumerate(BYTE_PIECES) if first <= slot0)
+                    off = slot0 - BYTE_PIECES[i][0]
                     for s in range(PASSES):
                         nc.tensor.matmul_mx(
                             out=y_bank[:, u * P : (u + 1) * P],
-                            lhsT=w2_w[:, e * PASSES + s, 2 * P * j : 2 * P * (j + 1)].bitcast(FP4X4),
+                            lhsT=w2_w[e][:, s, 2 * P * j : 2 * P * (j + 1)].bitcast(FP4X4),
                             lhsT_scale=w2_s[:, e * PASSES + s, P * j : P * (j + 1)],
                             rhs=slot_w[e][:, s, u * P : (u + 1) * P].bitcast(FP8X4),
                             rhs_scale=(slot_s0, slot_s1)[s][i][:, off : off + P],
                             start=(s == 0),
                             stop=(s == PASSES - 1),
                         )
-                nc.scalar.copy(y[j][:, e * C : (e + 1) * C], y_bank[:])
+                if (e, j) == (E - 1, 0):
+                    nc.vector.tensor_copy(y[j][:, e * C : (e + 1) * C], y_bank[:])
+                else:
+                    nc.scalar.copy(y[j][:, e * C : (e + 1) * C], y_bank[:])
 
         nc.sync.dma_start(offs_sb[:], offs)
         for q in range(QUADS):
@@ -127,94 +129,100 @@ def tile_moe_sub_silu_kernel(
                 w2_s[32 * q : 32 * q + 4, :, :].bitcast(I32),
                 w2t_scales[:, :, 4 * q : 4 * q + 4, :].rearrange("e s b i -> b (e s) i").bitcast(I32),
             )
-        load_w2(0, 1)
+        load_w2(0)
         gather_bytes(0)
-        load_w2(1, 3)
-        a_rows = a.rearrange("(j p) t -> p j t", p=P)
-        first = CHUNKS[0][1] * P
-        nc.gpsimd.dma_start(a_sb[:, :, 0:first], a_rows[:, :, 0:first])
+        for e in range(1, W2_BUFS):
+            load_w2(e)
         gather_words(0)
-        gather_words(1)
         gather_bytes(1)
-        load_w2(3, E)
-        nc.gpsimd.dma_start(gate_rows[0 : TOP * BLOCKS, :], gate[:, 0, :].rearrange("r (b p) -> r b p", p=P))
-        nc.gpsimd.dma_start(a_sb[:, :, first:T], a_rows[:, :, first:T])
-        nc.gpsimd.dma_start(w1_w[:].bitcast(I32), w1t_words[0].bitcast(I32))
+        gather_words(1)
+        gather_bytes(2)
+        for e in range(2, E):
+            gather_words(e)
+
+        for e in range(E - 2):
+            expert(e, range(HT))
+            if e + W2_BUFS < E:
+                load_w2(e + W2_BUFS)
+        a_sb = keep.tile([P, HT, T], F32, name="slot_w1", align_bytes=64)
+        nc.sync.dma_start(a_sb[:], a.rearrange("(j p) t -> p j t", p=P))
+        for j in range(HT):
+            nc.scalar.activation(sig[:, j, :], a_sb[:, j, :], ACT.Sigmoid)
+            expert(E - 2, [j])
+            expert(E - 1, [j])
+
+        gate_rows = keep.tile([P, P], F32, name="slot_w0", align_bytes=64)
+        gate_some = gate.rearrange("r q t -> (r q) t")[0 : TOP * P : GATE_STEP, :]
+        nc.sync.dma_start(gate_rows[:], gate_some.rearrange("i (b p) -> i b p", p=P))
+        gate_bank = psum.tile([P, P], F32, name="bank")
+        nc.tensor.transpose(gate_bank[:], gate_rows[:], ident[:])
+        nc.scalar.activation(gate_neg[:], gate_bank[:], ACT.Copy, scale=-1.0)
+
+        w1_w = keep.tile([P, 2 * K], U8, name="slot_w2", align_bytes=64)
+        nc.sync.dma_start(w1_w[:].bitcast(I32), w1t_words[0].bitcast(I32))
+        w1_s = keep.tile([P, K], U8, name="dy_s", align_bytes=64)
+        nc.vector.memset(w1_s[:].bitcast(I32), 0)
         for q in range(QUADS):
-            nc.gpsimd.dma_start(
+            nc.sync.dma_start(
                 w1_s[32 * q : 32 * q + 4, :].bitcast(I32), w1t_scales[0, 4 * q : 4 * q + 4, :].bitcast(I32)
             )
-
-        nc.scalar.activation(sig[:, :, 0:first], a_sb[:, :, 0:first], ACT.Sigmoid)
-
-        for e in range(E):
-            if e >= 2:
-                gather_words(e)
-            expert(e)
-
-        gate_bank = psum.tile([P, BANK], F32, name="bank")
-        nc.tensor.transpose(gate_bank[:, 0:P], gate_rows[:], ident[:])
-        nc.scalar.activation(gate_neg[:], gate_bank[:, 0 : TOP * BLOCKS], ACT.Copy, scale=-1.0)
-
-        nc.scalar.activation(sig[:, :, first:T], a_sb[:, :, first:T], ACT.Sigmoid)
-        a_packed = keep.tile([P, PACK, T], F32, name="a_sb")
+        a_packed = keep.tile([P, PACK, T], F32, name="slot_w%d" % (E - 2), align_bytes=64)
         nc.sync.dma_start(a_packed[:], a.rearrange("(p d) t -> p d t", d=PACK))
 
-        for b0, nb in CHUNKS:
+        sums = {}
+
+        def combine(r, b0, nb):
             toks = slice(b0 * P, (b0 + nb) * P)
             cols = slice(b0 * P // PER_COL, (b0 + nb) * P // PER_COL)
-            sums = [psum.tile([P, BANK], F32, name="bank") for b in range(nb)]
-            for r in range(TOP):
-                turned = [psum.tile([P, BANK], F32, name="bank") for b in range(nb)]
-                for j in range(HT):
-                    picked = ring.tile([P, nb * P], F32, name="picked")
-                    nc.vector.tensor_tensor(
-                        picked[:], y[j][:].indirect(pos_sb[r][:, cols]), sig[:, j, toks], ALU.mult
-                    )
-                    for b in range(nb):
-                        nc.tensor.transpose(
-                            turned[b][:, j * P : (j + 1) * P], picked[:, b * P : (b + 1) * P], ident[:]
-                        )
+            turned = [psum.tile([P, BANK], F32, name="bank") for b in range(nb)]
+            for j in range(HT):
+                picked = ring.tile([P, nb * P], F32, name="picked")
+                nc.vector.tensor_tensor(picked[:], y[j][:].indirect(pos_sb[r][:, cols]), sig[:, j, toks], ALU.mult)
                 for b in range(nb):
-                    gated = ring.tile([P, PACK, P], F32, name="gated")
-                    col = r * BLOCKS + b0 + b
-                    nc.scalar.activation(
-                        gated[:],
-                        turned[b][:].rearrange("t (m d) -> t d m", d=PACK),
-                        ACT.Copy,
-                        scale=gate_neg[:, col : col + 1],
-                    )
-                    for d in range(PACK):
-                        nc.tensor.matmul(
-                            sums[b][:, d * P : (d + 1) * P],
-                            lhsT=gated[:, d, :],
-                            rhs=ident[:],
-                            is_transpose=True,
-                            start=(r == 0 and d == 0),
-                            stop=(r == TOP - 1 and d == PACK - 1),
-                        )
-            da = ring.tile([P, nb * P, PACK], BF16, name="da", align_bytes=64)
-            for b in range(nb):
-                blk = slice((b0 + b) * P, (b0 + b + 1) * P)
+                    nc.tensor.transpose(turned[b][:, j * P : (j + 1) * P], picked[:, b * P : (b + 1) * P], ident[:])
+            for b in range(b0, b0 + nb):
+                gated = ring.tile([P, PACK, P], F32, name="gated")
+                col = -(-r * P // GATE_STEP) * BLOCKS + b
                 nc.scalar.activation(
-                    silu_neg[:, blk, :], a_packed[:, :, blk].rearrange("p d t -> p t d"), ACT.Silu, scale=-1.0
+                    gated[:],
+                    turned[b - b0][:].rearrange("t (m d) -> t d m", d=PACK),
+                    ACT.Copy,
+                    scale=gate_neg[:, col : col + 1],
                 )
-                nc.vector.scalar_tensor_tensor(
-                    da[:, b * P : (b + 1) * P, :],
-                    silu_neg[:, blk, :],
-                    1.0,
-                    sums[b][:].rearrange("p (d t) -> p t d", d=PACK),
-                    ALU.subtract,
-                    ALU.mult,
-                )
-            da_w = ring.tile([P, nb * P], U32, name="da_w", align_bytes=64)
-            da_s = ring.tile([P, nb * P], U8, name="da_s", align_bytes=64)
+                if r == 0:
+                    sums[b] = psum.tile([P, BANK], F32, name="bank")
+                for d in range(PACK):
+                    nc.tensor.matmul(
+                        sums[b][:, d * P : (d + 1) * P],
+                        lhsT=gated[:, d, :],
+                        rhs=ident[:],
+                        is_transpose=True,
+                        start=(r == 0 and d == 0),
+                        stop=(r == TOP - 1 and d == PACK - 1),
+                    )
+
+        def project(b):
+            toks = slice(b * P, (b + 1) * P)
+            nc.scalar.activation(
+                silu_neg[:, toks, :], a_packed[:, :, toks].rearrange("p d t -> p t d"), ACT.Silu, scale=-1.0
+            )
+            da = ring.tile([P, P, PACK], BF16, name="da", align_bytes=64)
+            nc.vector.scalar_tensor_tensor(
+                da[:],
+                silu_neg[:, toks, :],
+                1.0,
+                sums[b][:].rearrange("p (d t) -> p t d", d=PACK),
+                ALU.subtract,
+                ALU.mult,
+            )
+            da_w = ring.tile([P, P], U32, name="da_w", align_bytes=64)
+            da_s = ring.tile([P, P], U8, name="da_s", align_bytes=64)
             nc.vector.quantize_mx(
                 out=da_w[:].bitcast(FP8X4), scales=da_s[:], in_=da[:].rearrange("p t d -> p (t d)")
             )
-            res_bank = psum.tile([P, BANK], F32, name="bank")
+            res_bank = psum.tile([P, P], F32, name="bank")
             nc.tensor.matmul_mx(
-                out=res_bank[:, 0 : nb * P],
+                out=res_bank[:],
                 lhsT=w1_w[:].bitcast(FP4X4),
                 lhsT_scale=w1_s[:],
                 rhs=da_w[:].bitcast(FP8X4),
@@ -222,6 +230,13 @@ def tile_moe_sub_silu_kernel(
                 start=True,
                 stop=True,
             )
-            res = ring.tile([P, nb * P], F32, name="res")
-            nc.scalar.copy(res[:], res_bank[:, 0 : nb * P])
+            res = ring.tile([P, P], F32, name="res")
+            nc.scalar.copy(res[:], res_bank[:])
             nc.sync.dma_start(out[:, toks], res[:])
+
+        for r in range(TOP - 1):
+            combine(r, 0, BLOCKS)
+        for b0 in range(0, BLOCKS, LAST_CHUNK):
+            combine(TOP - 1, b0, LAST_CHUNK)
+        for b in range(BLOCKS):
+            project(b)

@@ -26,11 +26,12 @@ HT = H // P
 BLOCKS = T // P
 PER_COL = 16
 BANK = 512
-BYTE_PIECES = ((0, 384), (384, 384), (768, 768))
+BYTE_PIECES = ((0, 768), (768, 768))
 W2_ZERO_SPLIT = 8
 BYTE_GATHER = 384
-W2_BUFS = 3
-LAST_CHUNK = 2
+W2_LOADS = ((0, 1, "w2_first"), (1, 3, "w2_next"), (3, E, "dy_s"))
+LAST_CHUNKS = ((0, 3), (3, 1))
+WORD_PIECES = ((0, 384), (384, 384), (768, 384), (1152, 256), (1408, 128))
 GATE_STEP = TOP * BLOCKS
 
 
@@ -40,7 +41,6 @@ def tile_moe_sub_silu_kernel(
     nc = tc.nc
     with ExitStack() as ctx:
         keep = ctx.enter_context(tc.tile_pool(name="keep", bufs=1))
-        weights = ctx.enter_context(tc.tile_pool(name="weights", bufs=W2_BUFS))
         ring = ctx.enter_context(tc.tile_pool(name="ring", bufs=6))
         psum = ctx.enter_context(tc.psum_pool(name="psum", bufs=8))
 
@@ -49,7 +49,9 @@ def tile_moe_sub_silu_kernel(
         dy_w = keep.tile([P, PASSES, T], I32, name="dy_w", align_bytes=64)
         dy_s = keep.tile([P, T], U8, name="dy_s", align_bytes=64)
         w2_s = keep.tile([P, E * PASSES, H], U8, name="w2_s", align_bytes=64)
-        slot_w = [keep.tile([P, PASSES, C], I32, name="slot_w%d" % e, align_bytes=64) for e in range(E)]
+        slot_w = [
+            keep.tile([P, PASSES, n], I32, name="slot_w%d" % i, align_bytes=64) for i, (first, n) in enumerate(WORD_PIECES)
+        ]
         slot_s0 = [keep.tile([P, n], U8, name="slot_s0_%d" % first, align_bytes=64) for first, n in BYTE_PIECES]
         slot_s1 = [keep.tile([P, n], U8, name="slot_s1_%d" % first, align_bytes=64) for first, n in BYTE_PIECES]
         y = [keep.tile([P, SLOTS], F32, name="y%d" % j, align_bytes=64) for j in range(HT)]
@@ -67,9 +69,11 @@ def tile_moe_sub_silu_kernel(
 
         w2_w = {}
 
-        def load_w2(e):
-            w2_w[e] = weights.tile([P, PASSES, 2 * H], U8, name="w2_w", align_bytes=64)
-            nc.sync.dma_start(w2_w[e][:].bitcast(I32), w2t_words[e].rearrange("s p b -> p s b").bitcast(I32))
+        def load_w2(e0, e1, name):
+            words = keep.tile([P, (e1 - e0) * PASSES, 2 * H], U8, name=name, align_bytes=64)
+            nc.sync.dma_start(words[:].bitcast(I32), w2t_words[e0:e1].rearrange("e s p b -> p (e s) b").bitcast(I32))
+            for e in range(e0, e1):
+                w2_w[e] = words[:, (e - e0) * PASSES : (e - e0 + 1) * PASSES, :]
 
         def gather_bytes(i):
             first, n = BYTE_PIECES[i]
@@ -85,35 +89,35 @@ def tile_moe_sub_silu_kernel(
                     slot_s0[i][32 * q + 4 : 32 * q + 8, :].bitcast(I32),
                 )
 
-        def gather_words(e):
-            cols = C // PER_COL
+        def gather_words(i):
+            first, n = WORD_PIECES[i]
             for s in range(PASSES):
                 nc.vector.tensor_copy(
-                    slot_w[e][:, s, :].bitcast(U32),
-                    dy_w[:, s, :].bitcast(U32).indirect(offs_sb[:, e * cols : (e + 1) * cols]),
+                    slot_w[i][:, s, :].bitcast(U32),
+                    dy_w[:, s, :].bitcast(U32).indirect(offs_sb[:, first // PER_COL : (first + n) // PER_COL]),
                 )
 
-        def expert(e, tiles):
-            for j in tiles:
-                y_bank = psum.tile([P, C], F32, name="bank")
-                for u in range(C // P):
-                    slot0 = e * C + u * P
-                    i = max(i for i, (first, n) in enumerate(BYTE_PIECES) if first <= slot0)
-                    off = slot0 - BYTE_PIECES[i][0]
-                    for s in range(PASSES):
-                        nc.tensor.matmul_mx(
-                            out=y_bank[:, u * P : (u + 1) * P],
-                            lhsT=w2_w[e][:, s, 2 * P * j : 2 * P * (j + 1)].bitcast(FP4X4),
-                            lhsT_scale=w2_s[:, e * PASSES + s, P * j : P * (j + 1)],
-                            rhs=slot_w[e][:, s, u * P : (u + 1) * P].bitcast(FP8X4),
-                            rhs_scale=(slot_s0, slot_s1)[s][i][:, off : off + P],
-                            start=(s == 0),
-                            stop=(s == PASSES - 1),
-                        )
-                if (e, j) == (E - 1, 0):
-                    nc.vector.tensor_copy(y[j][:, e * C : (e + 1) * C], y_bank[:])
-                else:
-                    nc.scalar.copy(y[j][:, e * C : (e + 1) * C], y_bank[:])
+        def find(pieces, slot):
+            i = max(i for i, (first, n) in enumerate(pieces) if first <= slot)
+            return i, slot - pieces[i][0]
+
+        def product(j, first, n, copy):
+            e = first // C
+            y_bank = psum.tile([P, n], F32, name="bank")
+            for u in range(0, n, P):
+                wi, woff = find(WORD_PIECES, first + u)
+                bi, boff = find(BYTE_PIECES, first + u)
+                for s in range(PASSES):
+                    nc.tensor.matmul_mx(
+                        out=y_bank[:, u : u + P],
+                        lhsT=w2_w[e][:, s, 2 * P * j : 2 * P * (j + 1)].bitcast(FP4X4),
+                        lhsT_scale=w2_s[:, e * PASSES + s, P * j : P * (j + 1)],
+                        rhs=slot_w[wi][:, s, woff : woff + P].bitcast(FP8X4),
+                        rhs_scale=(slot_s0, slot_s1)[s][bi][:, boff : boff + P],
+                        start=(s == 0),
+                        stop=(s == PASSES - 1),
+                    )
+            copy(y[j][:, first : first + n], y_bank[:])
 
         nc.sync.dma_start(offs_sb[:], offs)
         for q in range(QUADS):
@@ -129,44 +133,45 @@ def tile_moe_sub_silu_kernel(
                 w2_s[32 * q : 32 * q + 4, :, :].bitcast(I32),
                 w2t_scales[:, :, 4 * q : 4 * q + 4, :].rearrange("e s b i -> b (e s) i").bitcast(I32),
             )
-        load_w2(0)
+        load_w2(*W2_LOADS[0])
         gather_bytes(0)
-        for e in range(1, W2_BUFS):
-            load_w2(e)
+        load_w2(*W2_LOADS[1])
         gather_words(0)
-        gather_bytes(1)
         gather_words(1)
-        gather_bytes(2)
-        for e in range(2, E):
-            gather_words(e)
+        gather_bytes(1)
+        load_w2(*W2_LOADS[2])
+        for i in range(2, len(WORD_PIECES)):
+            gather_words(i)
 
-        for e in range(E - 2):
-            expert(e, range(HT))
-            if e + W2_BUFS < E:
-                load_w2(e + W2_BUFS)
-        a_sb = keep.tile([P, HT, T], F32, name="slot_w1", align_bytes=64)
-        nc.sync.dma_start(a_sb[:], a.rearrange("(j p) t -> p j t", p=P))
+        a_sb = keep.tile([P, HT, T], F32, name="a_sb")
+        nc.gpsimd.dma_start(a_sb[:], a.rearrange("(j p) t -> p j t", p=P))
+        nc.scalar.activation(sig[:], a_sb[:], ACT.Sigmoid)
         for j in range(HT):
-            nc.scalar.activation(sig[:, j, :], a_sb[:, j, :], ACT.Sigmoid)
-            expert(E - 2, [j])
-            expert(E - 1, [j])
+            product(j, 0, C, nc.scalar.copy)
+        for j in range(HT):
+            for e in range(1, E):
+                if (j, e) == (0, E - 1):
+                    product(j, SLOTS - C, P, nc.scalar.copy)
+                    product(j, SLOTS - P, P, nc.vector.tensor_copy)
+                else:
+                    product(j, e * C, C, nc.scalar.copy)
 
-        gate_rows = keep.tile([P, P], F32, name="slot_w0", align_bytes=64)
+        gate_rows = keep.tile([P, P], F32, name="w2_first", align_bytes=64)
         gate_some = gate.rearrange("r q t -> (r q) t")[0 : TOP * P : GATE_STEP, :]
         nc.sync.dma_start(gate_rows[:], gate_some.rearrange("i (b p) -> i b p", p=P))
         gate_bank = psum.tile([P, P], F32, name="bank")
         nc.tensor.transpose(gate_bank[:], gate_rows[:], ident[:])
         nc.scalar.activation(gate_neg[:], gate_bank[:], ACT.Copy, scale=-1.0)
 
-        w1_w = keep.tile([P, 2 * K], U8, name="slot_w2", align_bytes=64)
+        w1_w = keep.tile([P, 2 * K], U8, name="slot_w0", align_bytes=64)
         nc.sync.dma_start(w1_w[:].bitcast(I32), w1t_words[0].bitcast(I32))
-        w1_s = keep.tile([P, K], U8, name="dy_s", align_bytes=64)
+        w1_s = keep.tile([P, K], U8, name="slot_w1", align_bytes=64)
         nc.vector.memset(w1_s[:].bitcast(I32), 0)
         for q in range(QUADS):
             nc.sync.dma_start(
                 w1_s[32 * q : 32 * q + 4, :].bitcast(I32), w1t_scales[0, 4 * q : 4 * q + 4, :].bitcast(I32)
             )
-        a_packed = keep.tile([P, PACK, T], F32, name="slot_w%d" % (E - 2), align_bytes=64)
+        a_packed = keep.tile([P, PACK, T], F32, name="slot_w%d" % (len(WORD_PIECES) - 1), align_bytes=64)
         nc.sync.dma_start(a_packed[:], a.rearrange("(p d) t -> p d t", d=PACK))
 
         sums = {}
@@ -236,7 +241,7 @@ def tile_moe_sub_silu_kernel(
 
         for r in range(TOP - 1):
             combine(r, 0, BLOCKS)
-        for b0 in range(0, BLOCKS, LAST_CHUNK):
-            combine(TOP - 1, b0, LAST_CHUNK)
+        for b0, nb in LAST_CHUNKS:
+            combine(TOP - 1, b0, nb)
         for b in range(BLOCKS):
             project(b)

@@ -31,7 +31,7 @@ W2_ZERO_SPLIT = 8
 BYTE_GATHER = 384
 W2_LOADS = ((0, 1, "w2_first"), (1, 3, "w2_next"), (3, E, "dy_s"))
 LAST_CHUNKS = ((0, 3), (3, 1))
-WORD_PIECES = ((0, 384), (384, 384), (768, 384), (1152, 256), (1408, 128))
+WORD_PIECES = ((0, 256), (256, 256), (512, 256), (768, 384), (1152, 256), (1408, 128))
 GATE_STEP = TOP * BLOCKS
 
 
@@ -66,6 +66,8 @@ def tile_moe_sub_silu_kernel(
         for plane in slot_s1:
             nc.gpsimd.memset(plane[:].bitcast(I32), 0)
         make_identity(nc, ident[:])
+        a_sb = keep.tile([P, HT, T], F32, name="a_sb")
+        nc.gpsimd.dma_start(a_sb[:], a.rearrange("(j p) t -> p j t", p=P))
 
         w2_w = {}
 
@@ -137,14 +139,11 @@ def tile_moe_sub_silu_kernel(
         gather_bytes(0)
         load_w2(*W2_LOADS[1])
         gather_words(0)
-        gather_words(1)
         gather_bytes(1)
         load_w2(*W2_LOADS[2])
-        for i in range(2, len(WORD_PIECES)):
+        for i in range(1, len(WORD_PIECES)):
             gather_words(i)
 
-        a_sb = keep.tile([P, HT, T], F32, name="a_sb")
-        nc.gpsimd.dma_start(a_sb[:], a.rearrange("(j p) t -> p j t", p=P))
         nc.scalar.activation(sig[:], a_sb[:], ACT.Sigmoid)
         for j in range(HT):
             product(j, 0, C, nc.scalar.copy)
@@ -206,7 +205,7 @@ def tile_moe_sub_silu_kernel(
                         stop=(r == TOP - 1 and d == PACK - 1),
                     )
 
-        def project(b):
+        def finish_gradient(b):
             toks = slice(b * P, (b + 1) * P)
             nc.scalar.activation(
                 silu_neg[:, toks, :], a_packed[:, :, toks].rearrange("p d t -> p t d"), ACT.Silu, scale=-1.0
@@ -220,6 +219,10 @@ def tile_moe_sub_silu_kernel(
                 ALU.subtract,
                 ALU.mult,
             )
+            return da
+
+        def project(b, da):
+            toks = slice(b * P, (b + 1) * P)
             da_w = ring.tile([P, P], U32, name="da_w", align_bytes=64)
             da_s = ring.tile([P, P], U8, name="da_s", align_bytes=64)
             nc.vector.quantize_mx(
@@ -243,5 +246,8 @@ def tile_moe_sub_silu_kernel(
             combine(r, 0, BLOCKS)
         for b0, nb in LAST_CHUNKS:
             combine(TOP - 1, b0, nb)
-        for b in range(BLOCKS):
-            project(b)
+        das = [finish_gradient(0)]
+        for b in range(1, BLOCKS):
+            das.append(finish_gradient(b))
+            project(b - 1, das[b - 1])
+        project(BLOCKS - 1, das[-1])

@@ -25,14 +25,13 @@ QUADS = 4
 HT = H // P
 BLOCKS = T // P
 PER_COL = 16
-BANK = 512
-BYTE_PIECES = ((0, 768), (768, 768))
-W2_ZERO_SPLIT = 8
-BYTE_GATHER = 384
-W2_LOADS = ((0, 1, "w2_first"), (1, 3, "w2_next"), (3, E, "dy_s"))
-LAST_CHUNKS = ((0, 3), (3, 1))
-WORD_PIECES = ((0, 256), (256, 256), (512, 256), (768, 384), (1152, 256), (1408, 128))
-GATE_STEP = TOP * BLOCKS
+WORD_PIECES = ((0, 768), (768, 384), (1152, 384))
+WORD_WINDOW = 1024
+BYTE_WINDOW = 2048
+HALF = T // 2
+PART = 384
+W2_EARLY = 4
+LAST_CHUNKS = ((0, 2), (2, 1), (3, 1))
 
 
 def tile_moe_sub_silu_kernel(
@@ -41,85 +40,36 @@ def tile_moe_sub_silu_kernel(
     nc = tc.nc
     with ExitStack() as ctx:
         keep = ctx.enter_context(tc.tile_pool(name="keep", bufs=1))
+        placed = ctx.enter_context(tc.tile_pool(name="placed", bufs=1))
         ring = ctx.enter_context(tc.tile_pool(name="ring", bufs=6))
-        psum = ctx.enter_context(tc.psum_pool(name="psum", bufs=8))
+        psum = ctx.enter_context(tc.psum_pool(name="psum", bufs=6))
+        psum_last = ctx.enter_context(tc.psum_pool(name="psum_last", bufs=2))
 
+        late_bytes = (E - W2_EARLY) * PASSES * 2 * H
         offs_sb = keep.tile([P, SLOTS // PER_COL], U16, name="offs_sb")
         pos_sb = [keep.tile([P, T // PER_COL], U16, name="pos_sb%d" % r) for r in range(TOP)]
-        dy_w = keep.tile([P, PASSES, T], I32, name="dy_w", align_bytes=64)
-        dy_s = keep.tile([P, T], U8, name="dy_s", align_bytes=64)
+        dy_s = placed.tile([P, BYTE_WINDOW], U8, name="dy_s", align_bytes=64, offset=late_bytes - T // 2)
+        dy_w_at = late_bytes + TOP * T * 4
+        dy_w = placed.tile([P, T + WORD_WINDOW], I32, name="dy_w", align_bytes=64, offset=dy_w_at)
         w2_s = keep.tile([P, E * PASSES, H], U8, name="w2_s", align_bytes=64)
         slot_w = [
-            keep.tile([P, PASSES, n], I32, name="slot_w%d" % i, align_bytes=64) for i, (first, n) in enumerate(WORD_PIECES)
+            keep.tile([P, PASSES, n], I32, name="slot_w%d" % first, align_bytes=64) for first, n in WORD_PIECES
         ]
-        slot_s0 = [keep.tile([P, n], U8, name="slot_s0_%d" % first, align_bytes=64) for first, n in BYTE_PIECES]
-        slot_s1 = [keep.tile([P, n], U8, name="slot_s1_%d" % first, align_bytes=64) for first, n in BYTE_PIECES]
+        slot_s = [keep.tile([P, SLOTS], U8, name="slot_s%d" % s, align_bytes=64) for s in range(PASSES)]
         y = [keep.tile([P, SLOTS], F32, name="y%d" % j, align_bytes=64) for j in range(HT)]
-        sig = keep.tile([P, HT, T], F32, name="sig")
-        silu_neg = keep.tile([P, T, PACK], F32, name="silu_neg")
-        gate_neg = keep.tile([P, P], F32, name="gate_neg")
+        a_sb = keep.tile([P, PACK, T], F32, name="a_sb", align_bytes=64)
+        sig = keep.tile([P, T, PACK], F32, name="sig", align_bytes=64)
+        silu_neg = [keep.tile([P, HALF, PACK], F32, name="silu_neg%d" % h, align_bytes=64) for h in range(2)]
+        slope_neg = keep.tile([P, T, PACK], F32, name="slope_neg", align_bytes=64)
+        dh_t = keep.tile([P, BLOCKS, PACK, P], F32, name="dh_t", align_bytes=64)
         ident = keep.tile([P, P], F32, name="ident")
 
-        nc.gpsimd.memset(dy_s[:].bitcast(I32), 0)
-        nc.vector.memset(w2_s[:, 0:W2_ZERO_SPLIT, :].bitcast(I32), 0)
-        nc.gpsimd.memset(w2_s[:, W2_ZERO_SPLIT:, :].bitcast(I32), 0)
-        for plane in slot_s1:
-            nc.gpsimd.memset(plane[:].bitcast(I32), 0)
+        nc.gpsimd.memset(dy_s[:, 0:T].bitcast(I32), 0)
+        nc.vector.memset(w2_s[:].bitcast(I32), 0)
+        nc.gpsimd.memset(dy_s[:, T:].bitcast(I32), 0)
+        nc.gpsimd.memset(dy_w[:, PASSES * T :], 0)
+        nc.gpsimd.memset(slot_s[1][:].bitcast(I32), 0)
         make_identity(nc, ident[:])
-        a_sb = keep.tile([P, HT, T], F32, name="a_sb")
-        nc.gpsimd.dma_start(a_sb[:], a.rearrange("(j p) t -> p j t", p=P))
-
-        w2_w = {}
-
-        def load_w2(e0, e1, name):
-            words = keep.tile([P, (e1 - e0) * PASSES, 2 * H], U8, name=name, align_bytes=64)
-            nc.sync.dma_start(words[:].bitcast(I32), w2t_words[e0:e1].rearrange("e s p b -> p (e s) b").bitcast(I32))
-            for e in range(e0, e1):
-                w2_w[e] = words[:, (e - e0) * PASSES : (e - e0 + 1) * PASSES, :]
-
-        def gather_bytes(i):
-            first, n = BYTE_PIECES[i]
-            for off in range(0, n, BYTE_GATHER):
-                col = (first + off) // PER_COL
-                nc.vector.tensor_copy(
-                    slot_s0[i][:, off : off + BYTE_GATHER],
-                    dy_s[:].indirect(offs_sb[:, col : col + BYTE_GATHER // PER_COL]),
-                )
-            for q in range(QUADS):
-                nc.sync.dma_start(
-                    slot_s1[i][32 * q : 32 * q + 4, :].bitcast(I32),
-                    slot_s0[i][32 * q + 4 : 32 * q + 8, :].bitcast(I32),
-                )
-
-        def gather_words(i):
-            first, n = WORD_PIECES[i]
-            for s in range(PASSES):
-                nc.vector.tensor_copy(
-                    slot_w[i][:, s, :].bitcast(U32),
-                    dy_w[:, s, :].bitcast(U32).indirect(offs_sb[:, first // PER_COL : (first + n) // PER_COL]),
-                )
-
-        def find(pieces, slot):
-            i = max(i for i, (first, n) in enumerate(pieces) if first <= slot)
-            return i, slot - pieces[i][0]
-
-        def product(j, first, n, copy):
-            e = first // C
-            y_bank = psum.tile([P, n], F32, name="bank")
-            for u in range(0, n, P):
-                wi, woff = find(WORD_PIECES, first + u)
-                bi, boff = find(BYTE_PIECES, first + u)
-                for s in range(PASSES):
-                    nc.tensor.matmul_mx(
-                        out=y_bank[:, u : u + P],
-                        lhsT=w2_w[e][:, s, 2 * P * j : 2 * P * (j + 1)].bitcast(FP4X4),
-                        lhsT_scale=w2_s[:, e * PASSES + s, P * j : P * (j + 1)],
-                        rhs=slot_w[wi][:, s, woff : woff + P].bitcast(FP8X4),
-                        rhs_scale=(slot_s0, slot_s1)[s][bi][:, boff : boff + P],
-                        start=(s == 0),
-                        stop=(s == PASSES - 1),
-                    )
-            copy(y[j][:, first : first + n], y_bank[:])
 
         nc.sync.dma_start(offs_sb[:], offs)
         for q in range(QUADS):
@@ -127,108 +77,126 @@ def tile_moe_sub_silu_kernel(
                 dy_s[32 * q : 32 * q + 4 * PASSES, 0:T].bitcast(I32),
                 dy_scales[:, 4 * q : 4 * q + 4, :].bitcast(I32),
             )
-        nc.sync.dma_start(dy_w[:], dy_words.rearrange("s p t d -> p s (t d)").bitcast(I32))
-        for r, pos in enumerate((pos1, pos2, pos3)):
-            nc.sync.dma_start(pos_sb[r][:], pos)
+        nc.sync.dma_start(
+            dy_w[:, 0 : PASSES * T].rearrange("p (s t) -> p s t", s=PASSES),
+            dy_words.rearrange("s p t d -> p s (t d)").bitcast(I32),
+        )
+        nc.sync.dma_start(a_sb[:], a.rearrange("(p d) t -> p d t", d=PACK))
         for q in range(QUADS):
             nc.sync.dma_start(
                 w2_s[32 * q : 32 * q + 4, :, :].bitcast(I32),
                 w2t_scales[:, :, 4 * q : 4 * q + 4, :].rearrange("e s b i -> b (e s) i").bitcast(I32),
             )
-        load_w2(*W2_LOADS[0])
-        gather_bytes(0)
-        load_w2(*W2_LOADS[1])
-        gather_words(0)
-        gather_bytes(1)
-        load_w2(*W2_LOADS[2])
-        for i in range(1, len(WORD_PIECES)):
-            gather_words(i)
+        w2_early = keep.tile([P, W2_EARLY * PASSES, 2 * H], U8, name="w2_early", align_bytes=64)
+        nc.sync.dma_start(
+            w2_early[:].bitcast(I32), w2t_words[0:W2_EARLY].rearrange("e s p b -> p (e s) b").bitcast(I32)
+        )
 
-        nc.scalar.activation(sig[:], a_sb[:], ACT.Sigmoid)
-        for j in range(HT):
-            product(j, 0, C, nc.scalar.copy)
-        for j in range(HT):
-            for e in range(1, E):
-                if (j, e) == (0, E - 1):
-                    product(j, SLOTS - C, P, nc.scalar.copy)
-                    product(j, SLOTS - P, P, nc.vector.tensor_copy)
-                else:
-                    product(j, e * C, C, nc.scalar.copy)
+        nc.vector.tensor_copy(slot_s[0][:], dy_s[:].indirect(offs_sb[:]))
+        for q in range(QUADS):
+            nc.sync.dma_start(
+                slot_s[1][32 * q : 32 * q + 4, :].bitcast(I32),
+                slot_s[0][32 * q + 4 : 32 * q + 8, :].bitcast(I32),
+            )
+        w2_late = placed.tile([P, (E - W2_EARLY) * PASSES, 2 * H], U8, name="w2_late", align_bytes=64, offset=0)
+        nc.sync.dma_start(
+            w2_late[:].bitcast(I32), w2t_words[W2_EARLY:E].rearrange("e s p b -> p (e s) b").bitcast(I32)
+        )
+        gate_sb = placed.tile([P, TOP, T], F32, name="gate_sb", align_bytes=64, offset=late_bytes)
+        nc.sync.dma_start(gate_sb[:], gate.rearrange("r p t -> p r t"))
+        for r, pos in enumerate((pos1, pos2, pos3)):
+            nc.sync.dma_start(pos_sb[r][:], pos)
+        for i, (first, n) in enumerate(WORD_PIECES):
+            listed = offs_sb[:, first // PER_COL : (first + n) // PER_COL]
+            for s in range(PASSES):
+                window = dy_w[:, s * T : s * T + WORD_WINDOW].bitcast(U32)
+                nc.vector.tensor_copy(slot_w[i][:, s, :].bitcast(U32), window.indirect(listed))
 
-        gate_rows = keep.tile([P, P], F32, name="w2_first", align_bytes=64)
-        gate_some = gate.rearrange("r q t -> (r q) t")[0 : TOP * P : GATE_STEP, :]
-        nc.sync.dma_start(gate_rows[:], gate_some.rearrange("i (b p) -> i b p", p=P))
-        gate_bank = psum.tile([P, P], F32, name="bank")
-        nc.tensor.transpose(gate_bank[:], gate_rows[:], ident[:])
-        nc.scalar.activation(gate_neg[:], gate_bank[:], ACT.Copy, scale=-1.0)
+        def woven(tile):
+            return tile.rearrange("p (c i) d -> p c d i", i=PACK)
 
-        w1_w = keep.tile([P, 2 * K], U8, name="slot_w0", align_bytes=64)
+        def unwoven(tile):
+            return tile.rearrange("p d (c i) -> p c d i", i=PACK)
+
+        nc.scalar.activation(woven(sig[:]), unwoven(a_sb[:]), ACT.Sigmoid)
+        for h in range(2):
+            toks = slice(h * HALF, (h + 1) * HALF)
+            nc.scalar.activation(woven(silu_neg[h][:]), unwoven(a_sb[:, :, toks]), ACT.Silu, scale=-1.0)
+            nc.vector.scalar_tensor_tensor(
+                slope_neg[:, toks, :], silu_neg[h][:], 1.0, sig[:, toks, :], ALU.subtract, ALU.mult
+            )
+
+        w1_w = placed.tile([P, 2 * K], U8, name="w1_w", align_bytes=64, offset=dy_w_at)
         nc.sync.dma_start(w1_w[:].bitcast(I32), w1t_words[0].bitcast(I32))
-        w1_s = keep.tile([P, K], U8, name="slot_w1", align_bytes=64)
-        nc.vector.memset(w1_s[:].bitcast(I32), 0)
+        w1_s = placed.tile([P, K], U8, name="w1_s", align_bytes=64, offset=dy_w_at + 2 * K)
+        nc.gpsimd.memset(w1_s[:].bitcast(I32), 0)
         for q in range(QUADS):
             nc.sync.dma_start(
                 w1_s[32 * q : 32 * q + 4, :].bitcast(I32), w1t_scales[0, 4 * q : 4 * q + 4, :].bitcast(I32)
             )
-        a_packed = keep.tile([P, PACK, T], F32, name="slot_w%d" % (len(WORD_PIECES) - 1), align_bytes=64)
-        nc.sync.dma_start(a_packed[:], a.rearrange("(p d) t -> p d t", d=PACK))
 
-        sums = {}
+        def product(j, part):
+            y_bank = psum.tile([P, PART], F32, name="bank")
+            for u in range(0, PART, P):
+                slot = part * PART + u
+                e = slot // C
+                piece = max(i for i, (first, n) in enumerate(WORD_PIECES) if first <= slot)
+                at = slot - WORD_PIECES[piece][0]
+                words = w2_early if e < W2_EARLY else w2_late
+                for s in range(PASSES):
+                    nc.tensor.matmul_mx(
+                        out=y_bank[:, u : u + P],
+                        lhsT=words[:, (e % W2_EARLY) * PASSES + s, 2 * P * j : 2 * P * (j + 1)].bitcast(FP4X4),
+                        lhsT_scale=w2_s[:, e * PASSES + s, P * j : P * (j + 1)],
+                        rhs=slot_w[piece][:, s, at : at + P].bitcast(FP8X4),
+                        rhs_scale=slot_s[s][:, slot : slot + P],
+                        start=(s == 0),
+                        stop=(s == PASSES - 1),
+                    )
+            nc.scalar.copy(y[j][:, part * PART : (part + 1) * PART], y_bank[:])
 
-        def combine(r, b0, nb):
+        def combine(j, b0, nb, banks):
             toks = slice(b0 * P, (b0 + nb) * P)
             cols = slice(b0 * P // PER_COL, (b0 + nb) * P // PER_COL)
-            turned = [psum.tile([P, BANK], F32, name="bank") for b in range(nb)]
-            for j in range(HT):
+            turned = banks.tile([P, nb, P], F32, name="bank")
+            for r in range(TOP):
                 picked = ring.tile([P, nb * P], F32, name="picked")
-                nc.vector.tensor_tensor(picked[:], y[j][:].indirect(pos_sb[r][:, cols]), sig[:, j, toks], ALU.mult)
+                nc.vector.tensor_tensor(picked[:], y[j][:].indirect(pos_sb[r][:, cols]), gate_sb[:, r, toks], ALU.mult)
                 for b in range(nb):
-                    nc.tensor.transpose(turned[b][:, j * P : (j + 1) * P], picked[:, b * P : (b + 1) * P], ident[:])
-            for b in range(b0, b0 + nb):
-                gated = ring.tile([P, PACK, P], F32, name="gated")
-                col = -(-r * P // GATE_STEP) * BLOCKS + b
-                nc.scalar.activation(
-                    gated[:],
-                    turned[b - b0][:].rearrange("t (m d) -> t d m", d=PACK),
-                    ACT.Copy,
-                    scale=gate_neg[:, col : col + 1],
-                )
-                if r == 0:
-                    sums[b] = psum.tile([P, BANK], F32, name="bank")
-                for d in range(PACK):
                     nc.tensor.matmul(
-                        sums[b][:, d * P : (d + 1) * P],
-                        lhsT=gated[:, d, :],
+                        turned[:, b, :],
+                        lhsT=picked[:, b * P : (b + 1) * P],
                         rhs=ident[:],
                         is_transpose=True,
-                        start=(r == 0 and d == 0),
-                        stop=(r == TOP - 1 and d == PACK - 1),
+                        start=(r == 0 and b == 0),
+                        stop=(r == TOP - 1 and b == nb - 1),
                     )
+            rows = slice(j * P // PACK, (j + 1) * P // PACK)
+            nc.scalar.copy(dh_t[:, b0 : b0 + nb, :, rows], turned[:].rearrange("t b (m d) -> t b d m", d=PACK))
 
-        def finish_gradient(b):
-            toks = slice(b * P, (b + 1) * P)
-            nc.scalar.activation(
-                silu_neg[:, toks, :], a_packed[:, :, toks].rearrange("p d t -> p t d"), ACT.Silu, scale=-1.0
-            )
-            da = ring.tile([P, P, PACK], BF16, name="da", align_bytes=64)
-            nc.vector.scalar_tensor_tensor(
-                da[:],
-                silu_neg[:, toks, :],
-                1.0,
-                sums[b][:].rearrange("p (d t) -> p t d", d=PACK),
-                ALU.subtract,
-                ALU.mult,
-            )
+        def finish_gradient(b0, nb):
+            da = ring.tile([P, nb * P, PACK], BF16, name="da", align_bytes=64)
+            for b in range(b0, b0 + nb):
+                back = psum.tile([P, PACK, P], F32, name="bank")
+                for d in range(PACK):
+                    nc.tensor.transpose(back[:, d, :], dh_t[:, b, d, :], ident[:])
+                nc.vector.scalar_tensor_tensor(
+                    da[:, (b - b0) * P : (b - b0 + 1) * P, :],
+                    back[:].rearrange("p d t -> p t d"),
+                    -1.0,
+                    slope_neg[:, b * P : (b + 1) * P, :],
+                    ALU.mult,
+                    ALU.mult,
+                )
             return da
 
-        def project(b, da):
-            toks = slice(b * P, (b + 1) * P)
-            da_w = ring.tile([P, P], U32, name="da_w", align_bytes=64)
-            da_s = ring.tile([P, P], U8, name="da_s", align_bytes=64)
+        def project(b0, nb, da):
+            da_w = ring.tile([P, nb * P], U32, name="da_w", align_bytes=64)
+            da_s = ring.tile([P, nb * P], U8, name="da_s", align_bytes=64)
             nc.vector.quantize_mx(
                 out=da_w[:].bitcast(FP8X4), scales=da_s[:], in_=da[:].rearrange("p t d -> p (t d)")
             )
-            res_bank = psum.tile([P, P], F32, name="bank")
+            res_bank = psum.tile([P, nb * P], F32, name="bank")
             nc.tensor.matmul_mx(
                 out=res_bank[:],
                 lhsT=w1_w[:].bitcast(FP4X4),
@@ -238,16 +206,24 @@ def tile_moe_sub_silu_kernel(
                 start=True,
                 stop=True,
             )
-            res = ring.tile([P, P], F32, name="res")
+            res = ring.tile([P, nb * P], F32, name="res")
             nc.scalar.copy(res[:], res_bank[:])
-            nc.sync.dma_start(out[:, toks], res[:])
+            nc.sync.dma_start(out[:, b0 * P : (b0 + nb) * P], res[:])
 
-        for r in range(TOP - 1):
-            combine(r, 0, BLOCKS)
-        for b0, nb in LAST_CHUNKS:
-            combine(TOP - 1, b0, nb)
-        das = [finish_gradient(0)]
-        for b in range(1, BLOCKS):
-            das.append(finish_gradient(b))
-            project(b - 1, das[b - 1])
-        project(BLOCKS - 1, das[-1])
+        for j, part in ((0, 0), (0, 1), (1, 0), (1, 1), (0, 2), (1, 2), (0, 3), (1, 3)):
+            product(j, part)
+        for j in range(HT - 1):
+            if j + 2 < HT:
+                for part in range(SLOTS // PART):
+                    product(j + 2, part)
+            combine(j, 0, BLOCKS, psum)
+        first, second, third = LAST_CHUNKS
+        combine(HT - 1, *first, psum_last)
+        combine(HT - 1, *second, psum_last)
+        da_first = finish_gradient(*first)
+        combine(HT - 1, *third, psum_last)
+        da_second = finish_gradient(*second)
+        project(*first, da_first)
+        da_third = finish_gradient(*third)
+        project(*second, da_second)
+        project(*third, da_third)

@@ -30,7 +30,7 @@ WORD_WINDOW = 1024
 BYTE_WINDOW = 2048
 HALF = T // 2
 PART = 384
-W2_EARLY = 4
+W2_EARLY = 3
 LAST_CHUNKS = ((0, 2), (2, 1), (3, 1))
 
 
@@ -41,7 +41,8 @@ def tile_moe_sub_silu_kernel(
     with ExitStack() as ctx:
         keep = ctx.enter_context(tc.tile_pool(name="keep", bufs=1))
         placed = ctx.enter_context(tc.tile_pool(name="placed", bufs=1))
-        ring = ctx.enter_context(tc.tile_pool(name="ring", bufs=6))
+        ring = ctx.enter_context(tc.tile_pool(name="ring", bufs=3))
+        picks = ctx.enter_context(tc.tile_pool(name="picks", bufs=21))
         psum = ctx.enter_context(tc.psum_pool(name="psum", bufs=6))
         psum_last = ctx.enter_context(tc.psum_pool(name="psum_last", bufs=2))
 
@@ -77,11 +78,11 @@ def tile_moe_sub_silu_kernel(
                 dy_s[32 * q : 32 * q + 4 * PASSES, 0:T].bitcast(I32),
                 dy_scales[:, 4 * q : 4 * q + 4, :].bitcast(I32),
             )
+        nc.sync.dma_start(a_sb[:], a.rearrange("(p d) t -> p d t", d=PACK))
         nc.sync.dma_start(
             dy_w[:, 0 : PASSES * T].rearrange("p (s t) -> p s t", s=PASSES),
             dy_words.rearrange("s p t d -> p s (t d)").bitcast(I32),
         )
-        nc.sync.dma_start(a_sb[:], a.rearrange("(p d) t -> p d t", d=PACK))
         for q in range(QUADS):
             nc.sync.dma_start(
                 w2_s[32 * q : 32 * q + 4, :, :].bitcast(I32),
@@ -160,7 +161,7 @@ def tile_moe_sub_silu_kernel(
             cols = slice(b0 * P // PER_COL, (b0 + nb) * P // PER_COL)
             turned = banks.tile([P, nb, P], F32, name="bank")
             for r in range(TOP):
-                picked = ring.tile([P, nb * P], F32, name="picked")
+                picked = picks.tile([P, nb * P], F32, name="picked")
                 nc.vector.tensor_tensor(picked[:], y[j][:].indirect(pos_sb[r][:, cols]), gate_sb[:, r, toks], ALU.mult)
                 for b in range(nb):
                     nc.tensor.matmul(
@@ -174,15 +175,20 @@ def tile_moe_sub_silu_kernel(
             rows = slice(j * P // PACK, (j + 1) * P // PACK)
             nc.scalar.copy(dh_t[:, b0 : b0 + nb, :, rows], turned[:].rearrange("t b (m d) -> t b d m", d=PACK))
 
+        backs = {}
+
+        def turn_back(b0, nb):
+            for b in range(b0, b0 + nb):
+                backs[b] = psum.tile([P, PACK, P], F32, name="bank")
+                for d in range(PACK):
+                    nc.tensor.transpose(backs[b][:, d, :], dh_t[:, b, d, :], ident[:])
+
         def finish_gradient(b0, nb):
             da = ring.tile([P, nb * P, PACK], BF16, name="da", align_bytes=64)
             for b in range(b0, b0 + nb):
-                back = psum.tile([P, PACK, P], F32, name="bank")
-                for d in range(PACK):
-                    nc.tensor.transpose(back[:, d, :], dh_t[:, b, d, :], ident[:])
                 nc.vector.scalar_tensor_tensor(
                     da[:, (b - b0) * P : (b - b0 + 1) * P, :],
-                    back[:].rearrange("p d t -> p t d"),
+                    backs[b][:].rearrange("p d t -> p t d"),
                     -1.0,
                     slope_neg[:, b * P : (b + 1) * P, :],
                     ALU.mult,
@@ -210,18 +216,21 @@ def tile_moe_sub_silu_kernel(
             nc.scalar.copy(res[:], res_bank[:])
             nc.sync.dma_start(out[:, b0 * P : (b0 + nb) * P], res[:])
 
-        for j, part in ((0, 0), (0, 1), (1, 0), (1, 1), (0, 2), (1, 2), (0, 3), (1, 3)):
-            product(j, part)
-        for j in range(HT - 1):
-            if j + 2 < HT:
-                for part in range(SLOTS // PART):
-                    product(j + 2, part)
+        for j in range(HT):
+            for part in range(SLOTS // PART):
+                product(j, part)
+        for j in range(HT - 2):
             combine(j, 0, BLOCKS, psum)
         first, second, third = LAST_CHUNKS
+        combine(HT - 2, *first, psum_last)
         combine(HT - 1, *first, psum_last)
+        combine(HT - 2, second[0], second[1] + third[1], psum_last)
+        turn_back(*first)
         combine(HT - 1, *second, psum_last)
-        da_first = finish_gradient(*first)
         combine(HT - 1, *third, psum_last)
+        turn_back(*second)
+        turn_back(*third)
+        da_first = finish_gradient(*first)
         da_second = finish_gradient(*second)
         project(*first, da_first)
         da_third = finish_gradient(*third)

@@ -25,11 +25,11 @@ QUADS = 4
 HT = H // P
 BLOCKS = T // P
 PER_COL = 16
-WORD_PIECES = ((0, 768), (768, 384), (1152, 384))
+WORD_PIECES = ((0, 768), (768, 512), (1280, 256))
 WORD_WINDOW = 1024
 BYTE_WINDOW = 2048
 HALF = T // 2
-PART = 384
+PARTS = ((0, 384), (384, 384), (768, 512), (1280, 256))
 W2_EARLY = 3
 LAST_CHUNKS = ((0, 2), (2, 1), (3, 1))
 
@@ -88,6 +88,7 @@ def tile_moe_sub_silu_kernel(
                 w2_s[32 * q : 32 * q + 4, :, :].bitcast(I32),
                 w2t_scales[:, :, 4 * q : 4 * q + 4, :].rearrange("e s b i -> b (e s) i").bitcast(I32),
             )
+        nc.sync.dma_start(pos_sb[0][:], pos1)
         w2_early = keep.tile([P, W2_EARLY * PASSES, 2 * H], U8, name="w2_early", align_bytes=64)
         nc.sync.dma_start(
             w2_early[:].bitcast(I32), w2t_words[0:W2_EARLY].rearrange("e s p b -> p (e s) b").bitcast(I32)
@@ -105,8 +106,8 @@ def tile_moe_sub_silu_kernel(
         )
         gate_sb = placed.tile([P, TOP, T], F32, name="gate_sb", align_bytes=64, offset=late_bytes)
         nc.sync.dma_start(gate_sb[:], gate.rearrange("r p t -> p r t"))
-        for r, pos in enumerate((pos1, pos2, pos3)):
-            nc.sync.dma_start(pos_sb[r][:], pos)
+        nc.sync.dma_start(pos_sb[1][:], pos2)
+        nc.sync.dma_start(pos_sb[2][:], pos3)
         for i, (first, n) in enumerate(WORD_PIECES):
             listed = offs_sb[:, first // PER_COL : (first + n) // PER_COL]
             for s in range(PASSES):
@@ -119,27 +120,32 @@ def tile_moe_sub_silu_kernel(
         def unwoven(tile):
             return tile.rearrange("p d (c i) -> p c d i", i=PACK)
 
-        nc.scalar.activation(woven(sig[:]), unwoven(a_sb[:]), ACT.Sigmoid)
+        halves = [slice(h * HALF, (h + 1) * HALF) for h in range(2)]
         for h in range(2):
-            toks = slice(h * HALF, (h + 1) * HALF)
-            nc.scalar.activation(woven(silu_neg[h][:]), unwoven(a_sb[:, :, toks]), ACT.Silu, scale=-1.0)
-            nc.vector.scalar_tensor_tensor(
-                slope_neg[:, toks, :], silu_neg[h][:], 1.0, sig[:, toks, :], ALU.subtract, ALU.mult
-            )
+            nc.scalar.activation(woven(silu_neg[h][:]), unwoven(a_sb[:, :, halves[h]]), ACT.Silu, scale=-1.0)
+        shifted_at = dy_w_at + (T + WORD_WINDOW) * 4
+        shifted = placed.tile([P, HALF, PACK], F32, name="shifted", align_bytes=64, offset=shifted_at)
+        nc.gpsimd.tensor_scalar(shifted[:], silu_neg[0][:], 1.0, -1.0, ALU.mult, ALU.add)
+        for h in range(2):
+            nc.scalar.activation(woven(sig[:, halves[h], :]), unwoven(a_sb[:, :, halves[h]]), ACT.Sigmoid)
+        nc.gpsimd.tensor_tensor(slope_neg[:, halves[0], :], shifted[:], sig[:, halves[0], :], ALU.mult)
+        nc.vector.scalar_tensor_tensor(
+            slope_neg[:, halves[1], :], silu_neg[1][:], 1.0, sig[:, halves[1], :], ALU.subtract, ALU.mult
+        )
 
         w1_w = placed.tile([P, 2 * K], U8, name="w1_w", align_bytes=64, offset=dy_w_at)
         nc.sync.dma_start(w1_w[:].bitcast(I32), w1t_words[0].bitcast(I32))
-        w1_s = placed.tile([P, K], U8, name="w1_s", align_bytes=64, offset=dy_w_at + 2 * K)
+        w1_s = placed.tile([P, K], U8, name="w1_s", align_bytes=64, offset=shifted_at)
         nc.gpsimd.memset(w1_s[:].bitcast(I32), 0)
         for q in range(QUADS):
             nc.sync.dma_start(
                 w1_s[32 * q : 32 * q + 4, :].bitcast(I32), w1t_scales[0, 4 * q : 4 * q + 4, :].bitcast(I32)
             )
 
-        def product(j, part):
-            y_bank = psum.tile([P, PART], F32, name="bank")
-            for u in range(0, PART, P):
-                slot = part * PART + u
+        def product(j, start, width):
+            y_bank = psum.tile([P, width], F32, name="bank")
+            for u in range(0, width, P):
+                slot = start + u
                 e = slot // C
                 piece = max(i for i, (first, n) in enumerate(WORD_PIECES) if first <= slot)
                 at = slot - WORD_PIECES[piece][0]
@@ -154,7 +160,7 @@ def tile_moe_sub_silu_kernel(
                         start=(s == 0),
                         stop=(s == PASSES - 1),
                     )
-            nc.scalar.copy(y[j][:, part * PART : (part + 1) * PART], y_bank[:])
+            nc.scalar.copy(y[j][:, start : start + width], y_bank[:])
 
         def combine(j, b0, nb, banks):
             toks = slice(b0 * P, (b0 + nb) * P)
@@ -217,8 +223,8 @@ def tile_moe_sub_silu_kernel(
             nc.sync.dma_start(out[:, b0 * P : (b0 + nb) * P], res[:])
 
         for j in range(HT):
-            for part in range(SLOTS // PART):
-                product(j, part)
+            for part in PARTS:
+                product(j, *part)
         for j in range(HT - 2):
             combine(j, 0, BLOCKS, psum)
         first, second, third = LAST_CHUNKS

@@ -25,12 +25,12 @@ QUADS = 4
 HT = H // P
 BLOCKS = T // P
 PER_COL = 16
-WORD_PIECES = ((0, 768), (768, 512), (1280, 256))
+WORD_PIECES = ((0, 768), (768, 384), (1152, 256), (1408, 128))
 WORD_WINDOW = 1024
 BYTE_WINDOW = 2048
 HALF = T // 2
-PARTS = ((0, 384), (384, 384), (768, 512), (1280, 256))
-W2_EARLY = 3
+PARTS = ((0, 384), (384, 384), (768, 384), (1152, 384))
+HALF_H = H // 2
 LAST_CHUNKS = ((0, 2), (2, 1), (3, 1))
 
 
@@ -44,21 +44,32 @@ def tile_moe_sub_silu_kernel(
         ring = ctx.enter_context(tc.tile_pool(name="ring", bufs=3))
         picks = ctx.enter_context(tc.tile_pool(name="picks", bufs=21))
         psum = ctx.enter_context(tc.psum_pool(name="psum", bufs=6))
-        psum_last = ctx.enter_context(tc.psum_pool(name="psum_last", bufs=2))
+        psum_pair = ctx.enter_context(tc.psum_pool(name="psum_pair", bufs=1))
 
-        late_bytes = (E - W2_EARLY) * PASSES * 2 * H
+        plane_bytes = E * PASSES * HALF_H
+        dy_s_at = plane_bytes - T
+        gate_at = plane_bytes
+        dy_w_at = gate_at + TOP * T * 4
+        shifted_at = dy_w_at + (T + WORD_WINDOW) * 4
+        a_at = shifted_at + HALF * PACK * 4
         offs_sb = keep.tile([P, SLOTS // PER_COL], U16, name="offs_sb")
         pos_sb = [keep.tile([P, T // PER_COL], U16, name="pos_sb%d" % r) for r in range(TOP)]
-        dy_s = placed.tile([P, BYTE_WINDOW], U8, name="dy_s", align_bytes=64, offset=late_bytes - T // 2)
-        dy_w_at = late_bytes + TOP * T * 4
+        dy_s = placed.tile([P, BYTE_WINDOW], U8, name="dy_s", align_bytes=64, offset=dy_s_at)
         dy_w = placed.tile([P, T + WORD_WINDOW], I32, name="dy_w", align_bytes=64, offset=dy_w_at)
-        w2_s = keep.tile([P, E * PASSES, H], U8, name="w2_s", align_bytes=64)
+        w2_s = [
+            keep.tile([P, E * PASSES, HALF_H], U8, name="w2_s0", align_bytes=64),
+            placed.tile([P, E * PASSES, HALF_H], U8, name="w2_s1", align_bytes=64, offset=0),
+        ]
+        w2_w = [
+            keep.tile([P, E * PASSES, 2 * HALF_H], U8, name="w2_w0", align_bytes=64),
+            placed.tile([P, E * PASSES, 2 * HALF_H], U8, name="w2_w1", align_bytes=64, offset=a_at),
+        ]
         slot_w = [
             keep.tile([P, PASSES, n], I32, name="slot_w%d" % first, align_bytes=64) for first, n in WORD_PIECES
         ]
         slot_s = [keep.tile([P, SLOTS], U8, name="slot_s%d" % s, align_bytes=64) for s in range(PASSES)]
         y = [keep.tile([P, SLOTS], F32, name="y%d" % j, align_bytes=64) for j in range(HT)]
-        a_sb = keep.tile([P, PACK, T], F32, name="a_sb", align_bytes=64)
+        a_sb = placed.tile([P, PACK, T], F32, name="a_sb", align_bytes=64, offset=a_at)
         sig = keep.tile([P, T, PACK], F32, name="sig", align_bytes=64)
         silu_neg = [keep.tile([P, HALF, PACK], F32, name="silu_neg%d" % h, align_bytes=64) for h in range(2)]
         slope_neg = keep.tile([P, T, PACK], F32, name="slope_neg", align_bytes=64)
@@ -66,10 +77,11 @@ def tile_moe_sub_silu_kernel(
         ident = keep.tile([P, P], F32, name="ident")
 
         nc.gpsimd.memset(dy_s[:, 0:T].bitcast(I32), 0)
-        nc.vector.memset(w2_s[:].bitcast(I32), 0)
-        nc.gpsimd.memset(dy_s[:, T:].bitcast(I32), 0)
-        nc.gpsimd.memset(dy_w[:, PASSES * T :], 0)
-        nc.gpsimd.memset(slot_s[1][:].bitcast(I32), 0)
+        nc.gpsimd.memset(w2_s[0][:, 0:E, :].bitcast(I32), 0)
+        nc.vector.memset(w2_s[0][:, E:, :].bitcast(I32), 0)
+        nc.vector.memset(dy_s[:, T:].bitcast(I32), 0)
+        nc.vector.memset(dy_w[:, PASSES * T :], 0)
+        nc.vector.memset(slot_s[1][:].bitcast(I32), 0)
         make_identity(nc, ident[:])
 
         nc.sync.dma_start(offs_sb[:], offs)
@@ -83,16 +95,25 @@ def tile_moe_sub_silu_kernel(
             dy_w[:, 0 : PASSES * T].rearrange("p (s t) -> p s t", s=PASSES),
             dy_words.rearrange("s p t d -> p s (t d)").bitcast(I32),
         )
-        for q in range(QUADS):
+
+        def load_w2_scales(h):
+            cols = slice(h * HALF_H, (h + 1) * HALF_H)
+            for q in range(QUADS):
+                nc.sync.dma_start(
+                    w2_s[h][32 * q : 32 * q + 4, :, :].bitcast(I32),
+                    w2t_scales[:, :, 4 * q : 4 * q + 4, cols].rearrange("e s b i -> b (e s) i").bitcast(I32),
+                )
+
+        def load_w2_words(h):
+            cols = slice(2 * h * HALF_H, 2 * (h + 1) * HALF_H)
             nc.sync.dma_start(
-                w2_s[32 * q : 32 * q + 4, :, :].bitcast(I32),
-                w2t_scales[:, :, 4 * q : 4 * q + 4, :].rearrange("e s b i -> b (e s) i").bitcast(I32),
+                w2_w[h][:].bitcast(I32), w2t_words[:, :, :, cols].rearrange("e s p b -> p (e s) b").bitcast(I32)
             )
-        nc.sync.dma_start(pos_sb[0][:], pos1)
-        w2_early = keep.tile([P, W2_EARLY * PASSES, 2 * H], U8, name="w2_early", align_bytes=64)
-        nc.sync.dma_start(
-            w2_early[:].bitcast(I32), w2t_words[0:W2_EARLY].rearrange("e s p b -> p (e s) b").bitcast(I32)
-        )
+
+        load_w2_scales(0)
+        load_w2_words(0)
+        for r, pos in enumerate((pos1, pos2, pos3)):
+            nc.sync.dma_start(pos_sb[r][:], pos)
 
         nc.vector.tensor_copy(slot_s[0][:], dy_s[:].indirect(offs_sb[:]))
         for q in range(QUADS):
@@ -100,17 +121,13 @@ def tile_moe_sub_silu_kernel(
                 slot_s[1][32 * q : 32 * q + 4, :].bitcast(I32),
                 slot_s[0][32 * q + 4 : 32 * q + 8, :].bitcast(I32),
             )
-        w2_late = placed.tile([P, (E - W2_EARLY) * PASSES, 2 * H], U8, name="w2_late", align_bytes=64, offset=0)
-        nc.sync.dma_start(
-            w2_late[:].bitcast(I32), w2t_words[W2_EARLY:E].rearrange("e s p b -> p (e s) b").bitcast(I32)
-        )
-        gate_sb = placed.tile([P, TOP, T], F32, name="gate_sb", align_bytes=64, offset=late_bytes)
+        gate_sb = placed.tile([P, TOP, T], F32, name="gate_sb", align_bytes=64, offset=gate_at)
         nc.sync.dma_start(gate_sb[:], gate.rearrange("r p t -> p r t"))
-        nc.sync.dma_start(pos_sb[1][:], pos2)
-        nc.sync.dma_start(pos_sb[2][:], pos3)
+        nc.gpsimd.memset(w2_s[1][:].bitcast(I32), 0)
+        load_w2_scales(1)
         for i, (first, n) in enumerate(WORD_PIECES):
             listed = offs_sb[:, first // PER_COL : (first + n) // PER_COL]
-            for s in range(PASSES):
+            for s in reversed(range(PASSES)):
                 window = dy_w[:, s * T : s * T + WORD_WINDOW].bitcast(U32)
                 nc.vector.tensor_copy(slot_w[i][:, s, :].bitcast(U32), window.indirect(listed))
 
@@ -123,7 +140,6 @@ def tile_moe_sub_silu_kernel(
         halves = [slice(h * HALF, (h + 1) * HALF) for h in range(2)]
         for h in range(2):
             nc.scalar.activation(woven(silu_neg[h][:]), unwoven(a_sb[:, :, halves[h]]), ACT.Silu, scale=-1.0)
-        shifted_at = dy_w_at + (T + WORD_WINDOW) * 4
         shifted = placed.tile([P, HALF, PACK], F32, name="shifted", align_bytes=64, offset=shifted_at)
         nc.gpsimd.tensor_scalar(shifted[:], silu_neg[0][:], 1.0, -1.0, ALU.mult, ALU.add)
         for h in range(2):
@@ -133,6 +149,7 @@ def tile_moe_sub_silu_kernel(
             slope_neg[:, halves[1], :], silu_neg[1][:], 1.0, sig[:, halves[1], :], ALU.subtract, ALU.mult
         )
 
+        load_w2_words(1)
         w1_w = placed.tile([P, 2 * K], U8, name="w1_w", align_bytes=64, offset=dy_w_at)
         nc.sync.dma_start(w1_w[:].bitcast(I32), w1t_words[0].bitcast(I32))
         w1_s = placed.tile([P, K], U8, name="w1_s", align_bytes=64, offset=shifted_at)
@@ -142,30 +159,39 @@ def tile_moe_sub_silu_kernel(
                 w1_s[32 * q : 32 * q + 4, :].bitcast(I32), w1t_scales[0, 4 * q : 4 * q + 4, :].bitcast(I32)
             )
 
-        def product(j, start, width):
-            y_bank = psum.tile([P, width], F32, name="bank")
+        def any_bank(shape):
+            return psum.tile(shape, F32, name="bank")
+
+        def bank_x(shape):
+            return psum_pair.tile(shape, F32, name="bank_x")
+
+        def bank_y(shape):
+            return psum_pair.tile(shape, F32, name="bank_y")
+
+        def product(j, start, width, bank):
+            h, col = divmod(j * P, HALF_H)
+            y_bank = bank([P, width])
             for u in range(0, width, P):
                 slot = start + u
                 e = slot // C
                 piece = max(i for i, (first, n) in enumerate(WORD_PIECES) if first <= slot)
                 at = slot - WORD_PIECES[piece][0]
-                words = w2_early if e < W2_EARLY else w2_late
-                for s in range(PASSES):
+                for s in reversed(range(PASSES)):
                     nc.tensor.matmul_mx(
                         out=y_bank[:, u : u + P],
-                        lhsT=words[:, (e % W2_EARLY) * PASSES + s, 2 * P * j : 2 * P * (j + 1)].bitcast(FP4X4),
-                        lhsT_scale=w2_s[:, e * PASSES + s, P * j : P * (j + 1)],
+                        lhsT=w2_w[h][:, e * PASSES + s, 2 * col : 2 * (col + P)].bitcast(FP4X4),
+                        lhsT_scale=w2_s[h][:, e * PASSES + s, col : col + P],
                         rhs=slot_w[piece][:, s, at : at + P].bitcast(FP8X4),
                         rhs_scale=slot_s[s][:, slot : slot + P],
-                        start=(s == 0),
-                        stop=(s == PASSES - 1),
+                        start=(s == PASSES - 1),
+                        stop=(s == 0),
                     )
             nc.scalar.copy(y[j][:, start : start + width], y_bank[:])
 
-        def combine(j, b0, nb, banks):
+        def combine(j, b0, nb, bank):
             toks = slice(b0 * P, (b0 + nb) * P)
             cols = slice(b0 * P // PER_COL, (b0 + nb) * P // PER_COL)
-            turned = banks.tile([P, nb, P], F32, name="bank")
+            turned = bank([P, nb, P])
             for r in range(TOP):
                 picked = picks.tile([P, nb * P], F32, name="picked")
                 nc.vector.tensor_tensor(picked[:], y[j][:].indirect(pos_sb[r][:, cols]), gate_sb[:, r, toks], ALU.mult)
@@ -222,18 +248,22 @@ def tile_moe_sub_silu_kernel(
             nc.scalar.copy(res[:], res_bank[:])
             nc.sync.dma_start(out[:, b0 * P : (b0 + nb) * P], res[:])
 
-        for j in range(HT):
+        for part, bank in zip(PARTS, (any_bank, any_bank, bank_x, bank_y)):
+            product(0, *part, bank)
+        for part, bank in zip(PARTS, (bank_x, bank_y, bank_x, bank_y)):
+            product(1, *part, bank)
+        for j in range(2, HT):
             for part in PARTS:
-                product(j, *part)
+                product(j, *part, any_bank)
         for j in range(HT - 2):
-            combine(j, 0, BLOCKS, psum)
+            combine(j, 0, BLOCKS, any_bank)
         first, second, third = LAST_CHUNKS
-        combine(HT - 2, *first, psum_last)
-        combine(HT - 1, *first, psum_last)
-        combine(HT - 2, second[0], second[1] + third[1], psum_last)
+        combine(HT - 2, *first, bank_x)
+        combine(HT - 1, *first, bank_y)
+        combine(HT - 2, second[0], second[1] + third[1], bank_x)
         turn_back(*first)
-        combine(HT - 1, *second, psum_last)
-        combine(HT - 1, *third, psum_last)
+        combine(HT - 1, *second, bank_y)
+        combine(HT - 1, *third, bank_x)
         turn_back(*second)
         turn_back(*third)
         da_first = finish_gradient(*first)

@@ -25,11 +25,13 @@ QUADS = 4
 HT = H // P
 BLOCKS = T // P
 PER_COL = 16
-WORD_PIECES = ((0, 768), (768, 384), (1152, 256), (1408, 128))
+FIRST_PARTS = ((0, 384), (384, 384), (768, 384), (1152, 256), (1408, 128))
+WORD_PIECES = (((0, 768), (768, 768)), ((0, 768), (768, 384), (1152, 256), (1408, 128)))
 WORD_WINDOW = 1024
 BYTE_WINDOW = 2048
-HALF = T // 2
-PARTS = ((0, 384), (384, 384), (768, 384), (1152, 384))
+SHARE = 256
+SHARES = (SHARE, T - SHARE)
+PARTS = ((0, 512), (512, 512), (1024, 512))
 HALF_H = H // 2
 LAST_CHUNKS = ((0, 2), (2, 1), (3, 1))
 
@@ -51,7 +53,7 @@ def tile_moe_sub_silu_kernel(
         gate_at = plane_bytes
         dy_w_at = gate_at + TOP * T * 4
         shifted_at = dy_w_at + (T + WORD_WINDOW) * 4
-        a_at = shifted_at + HALF * PACK * 4
+        a_at = shifted_at + SHARE * PACK * 4
         offs_sb = keep.tile([P, SLOTS // PER_COL], U16, name="offs_sb")
         pos_sb = [keep.tile([P, T // PER_COL], U16, name="pos_sb%d" % r) for r in range(TOP)]
         dy_s = placed.tile([P, BYTE_WINDOW], U8, name="dy_s", align_bytes=64, offset=dy_s_at)
@@ -65,13 +67,20 @@ def tile_moe_sub_silu_kernel(
             placed.tile([P, E * PASSES, 2 * HALF_H], U8, name="w2_w1", align_bytes=64, offset=a_at),
         ]
         slot_w = [
-            keep.tile([P, PASSES, n], I32, name="slot_w%d" % first, align_bytes=64) for first, n in WORD_PIECES
+            [keep.tile([P, n], I32, name="slot_w%d_%d" % (s, first), align_bytes=64) for first, n in WORD_PIECES[s]]
+            for s in range(PASSES)
         ]
-        slot_s = [keep.tile([P, SLOTS], U8, name="slot_s%d" % s, align_bytes=64) for s in range(PASSES)]
+        picked_s = keep.tile([P, SLOTS], U8, name="picked_s", align_bytes=64)
+        slot_s = keep.tile([P, PASSES, SLOTS], U8, name="slot_s", align_bytes=64)
         y = [keep.tile([P, SLOTS], F32, name="y%d" % j, align_bytes=64) for j in range(HT)]
-        a_sb = placed.tile([P, PACK, T], F32, name="a_sb", align_bytes=64, offset=a_at)
+        a_sb = [
+            placed.tile(
+                [P, PACK, SHARES[h]], F32, name="a_sb%d" % h, align_bytes=64, offset=a_at + h * PACK * SHARE * 4
+            )
+            for h in range(2)
+        ]
         sig = keep.tile([P, T, PACK], F32, name="sig", align_bytes=64)
-        silu_neg = [keep.tile([P, HALF, PACK], F32, name="silu_neg%d" % h, align_bytes=64) for h in range(2)]
+        silu_neg = [keep.tile([P, SHARES[h], PACK], F32, name="silu_neg%d" % h, align_bytes=64) for h in range(2)]
         slope_neg = keep.tile([P, T, PACK], F32, name="slope_neg", align_bytes=64)
         dh_t = keep.tile([P, BLOCKS, PACK, P], F32, name="dh_t", align_bytes=64)
         ident = keep.tile([P, P], F32, name="ident")
@@ -80,25 +89,23 @@ def tile_moe_sub_silu_kernel(
         nc.gpsimd.memset(w2_s[0][:, 0:E, :].bitcast(I32), 0)
         nc.vector.memset(w2_s[0][:, E:, :].bitcast(I32), 0)
         nc.vector.memset(dy_s[:, T:].bitcast(I32), 0)
-        nc.vector.memset(dy_w[:, PASSES * T :], 0)
-        nc.vector.memset(slot_s[1][:].bitcast(I32), 0)
+        nc.vector.memset(slot_s[:].bitcast(I32), 0)
+        nc.gpsimd.memset(dy_w[:, PASSES * T :], 0)
         make_identity(nc, ident[:])
 
+        halves = [slice(0, SHARE), slice(SHARE, T)]
         nc.sync.dma_start(offs_sb[:], offs)
-        for q in range(QUADS):
-            nc.sync.dma_start(
-                dy_s[32 * q : 32 * q + 4 * PASSES, 0:T].bitcast(I32),
-                dy_scales[:, 4 * q : 4 * q + 4, :].bitcast(I32),
-            )
-        nc.sync.dma_start(a_sb[:], a.rearrange("(p d) t -> p d t", d=PACK))
+        nc.sync.dma_start(dy_s[0:P:PACK, 0:T].bitcast(I32), dy_scales.rearrange("s b t -> b s t").bitcast(I32))
+        for h in range(2):
+            nc.sync.dma_start(a_sb[h][:], a[:, halves[h]].rearrange("(p d) t -> p d t", d=PACK))
         nc.sync.dma_start(
             dy_w[:, 0 : PASSES * T].rearrange("p (s t) -> p s t", s=PASSES),
             dy_words.rearrange("s p t d -> p s (t d)").bitcast(I32),
         )
 
-        def load_w2_scales(h):
+        def load_w2_scales(h, quads):
             cols = slice(h * HALF_H, (h + 1) * HALF_H)
-            for q in range(QUADS):
+            for q in quads:
                 nc.sync.dma_start(
                     w2_s[h][32 * q : 32 * q + 4, :, :].bitcast(I32),
                     w2t_scales[:, :, 4 * q : 4 * q + 4, cols].rearrange("e s b i -> b (e s) i").bitcast(I32),
@@ -110,26 +117,33 @@ def tile_moe_sub_silu_kernel(
                 w2_w[h][:].bitcast(I32), w2t_words[:, :, :, cols].rearrange("e s p b -> p (e s) b").bitcast(I32)
             )
 
-        load_w2_scales(0)
-        load_w2_words(0)
         for r, pos in enumerate((pos1, pos2, pos3)):
             nc.sync.dma_start(pos_sb[r][:], pos)
+        load_w2_scales(0, range(1))
+        load_w2_words(0)
+        load_w2_scales(0, range(1, QUADS))
 
-        nc.vector.tensor_copy(slot_s[0][:], dy_s[:].indirect(offs_sb[:]))
+        def gather_words(s, i):
+            first, n = WORD_PIECES[s][i]
+            listed = offs_sb[:, first // PER_COL : (first + n) // PER_COL]
+            window = dy_w[:, s * T : s * T + WORD_WINDOW].bitcast(U32)
+            nc.vector.tensor_copy(slot_w[s][i][:].bitcast(U32), window.indirect(listed))
+
+        nc.vector.tensor_copy(picked_s[:], dy_s[:].indirect(offs_sb[:]))
         for q in range(QUADS):
             nc.sync.dma_start(
-                slot_s[1][32 * q : 32 * q + 4, :].bitcast(I32),
-                slot_s[0][32 * q + 4 : 32 * q + 8, :].bitcast(I32),
+                slot_s[32 * q : 32 * q + 4, :, :].bitcast(I32),
+                picked_s[32 * q : 32 * q + 32 : PACK, :].bitcast(I32),
             )
         gate_sb = placed.tile([P, TOP, T], F32, name="gate_sb", align_bytes=64, offset=gate_at)
         nc.sync.dma_start(gate_sb[:], gate.rearrange("r p t -> p r t"))
         nc.gpsimd.memset(w2_s[1][:].bitcast(I32), 0)
-        load_w2_scales(1)
-        for i, (first, n) in enumerate(WORD_PIECES):
-            listed = offs_sb[:, first // PER_COL : (first + n) // PER_COL]
-            for s in reversed(range(PASSES)):
-                window = dy_w[:, s * T : s * T + WORD_WINDOW].bitcast(U32)
-                nc.vector.tensor_copy(slot_w[i][:, s, :].bitcast(U32), window.indirect(listed))
+        load_w2_scales(1, range(QUADS))
+        gather_words(0, 0)
+        gather_words(1, 0)
+        gather_words(0, 1)
+        for i in range(1, len(WORD_PIECES[1])):
+            gather_words(1, i)
 
         def woven(tile):
             return tile.rearrange("p (c i) d -> p c d i", i=PACK)
@@ -137,13 +151,12 @@ def tile_moe_sub_silu_kernel(
         def unwoven(tile):
             return tile.rearrange("p d (c i) -> p c d i", i=PACK)
 
-        halves = [slice(h * HALF, (h + 1) * HALF) for h in range(2)]
         for h in range(2):
-            nc.scalar.activation(woven(silu_neg[h][:]), unwoven(a_sb[:, :, halves[h]]), ACT.Silu, scale=-1.0)
-        shifted = placed.tile([P, HALF, PACK], F32, name="shifted", align_bytes=64, offset=shifted_at)
+            nc.scalar.activation(woven(silu_neg[h][:]), unwoven(a_sb[h][:]), ACT.Silu, scale=-1.0)
+        shifted = placed.tile([P, SHARE, PACK], F32, name="shifted", align_bytes=64, offset=shifted_at)
         nc.gpsimd.tensor_scalar(shifted[:], silu_neg[0][:], 1.0, -1.0, ALU.mult, ALU.add)
         for h in range(2):
-            nc.scalar.activation(woven(sig[:, halves[h], :]), unwoven(a_sb[:, :, halves[h]]), ACT.Sigmoid)
+            nc.scalar.activation(woven(sig[:, halves[h], :]), unwoven(a_sb[h][:]), ACT.Sigmoid)
         nc.gpsimd.tensor_tensor(slope_neg[:, halves[0], :], shifted[:], sig[:, halves[0], :], ALU.mult)
         nc.vector.scalar_tensor_tensor(
             slope_neg[:, halves[1], :], silu_neg[1][:], 1.0, sig[:, halves[1], :], ALU.subtract, ALU.mult
@@ -168,24 +181,40 @@ def tile_moe_sub_silu_kernel(
         def bank_y(shape):
             return psum_pair.tile(shape, F32, name="bank_y")
 
-        def product(j, start, width, bank):
+        def one_pass(j, y_bank, start, u, s, opens, closes):
             h, col = divmod(j * P, HALF_H)
+            slot = start + u
+            e = slot // C
+            piece = max(i for i, (first, n) in enumerate(WORD_PIECES[s]) if first <= slot)
+            at = slot - WORD_PIECES[s][piece][0]
+            nc.tensor.matmul_mx(
+                out=y_bank[:, u : u + P],
+                lhsT=w2_w[h][:, e * PASSES + s, 2 * col : 2 * (col + P)].bitcast(FP4X4),
+                lhsT_scale=w2_s[h][:, e * PASSES + s, col : col + P],
+                rhs=slot_w[s][piece][:, at : at + P].bitcast(FP8X4),
+                rhs_scale=slot_s[:, s, slot : slot + P],
+                start=opens,
+                stop=closes,
+            )
+
+        def product(j, start, width, bank):
             y_bank = bank([P, width])
             for u in range(0, width, P):
-                slot = start + u
-                e = slot // C
-                piece = max(i for i, (first, n) in enumerate(WORD_PIECES) if first <= slot)
-                at = slot - WORD_PIECES[piece][0]
                 for s in reversed(range(PASSES)):
-                    nc.tensor.matmul_mx(
-                        out=y_bank[:, u : u + P],
-                        lhsT=w2_w[h][:, e * PASSES + s, 2 * col : 2 * (col + P)].bitcast(FP4X4),
-                        lhsT_scale=w2_s[h][:, e * PASSES + s, col : col + P],
-                        rhs=slot_w[piece][:, s, at : at + P].bitcast(FP8X4),
-                        rhs_scale=slot_s[s][:, slot : slot + P],
-                        start=(s == PASSES - 1),
-                        stop=(s == 0),
-                    )
+                    one_pass(j, y_bank, start, u, s, s == PASSES - 1, s == 0)
+            nc.scalar.copy(y[j][:, start : start + width], y_bank[:])
+
+        def early_pass(j, start, width, bank):
+            y_bank = bank([P, width])
+            for u in range(0, width, P):
+                one_pass(j, y_bank, start, u, 0, u == 0, False)
+            return y_bank
+
+        def late_pass(j, start, width, y_bank):
+            for u in range(0, width, P):
+                one_pass(j, y_bank, start, u, 1, False, u == width - P)
+
+        def copy_out(j, start, width, y_bank):
             nc.scalar.copy(y[j][:, start : start + width], y_bank[:])
 
         def combine(j, b0, nb, bank):
@@ -248,11 +277,13 @@ def tile_moe_sub_silu_kernel(
             nc.scalar.copy(res[:], res_bank[:])
             nc.sync.dma_start(out[:, b0 * P : (b0 + nb) * P], res[:])
 
-        for part, bank in zip(PARTS, (any_bank, any_bank, bank_x, bank_y)):
-            product(0, *part, bank)
-        for part, bank in zip(PARTS, (bank_x, bank_y, bank_x, bank_y)):
-            product(1, *part, bank)
-        for j in range(2, HT):
+        for part in FIRST_PARTS[:2]:
+            product(0, *part, any_bank)
+        open0 = [early_pass(0, *part, any_bank) for part in FIRST_PARTS[2:]]
+        for part, y_bank in zip(FIRST_PARTS[2:], open0):
+            late_pass(0, *part, y_bank)
+            copy_out(0, *part, y_bank)
+        for j in range(1, HT):
             for part in PARTS:
                 product(j, *part, any_bank)
         for j in range(HT - 2):

@@ -85,17 +85,18 @@ def tile_moe_sub_silu_kernel(
         dh_t = keep.tile([P, BLOCKS, PACK, P], F32, name="dh_t", align_bytes=64)
         ident = keep.tile([P, P], F32, name="ident")
 
-        nc.gpsimd.memset(dy_s[:, 0:T].bitcast(I32), 0)
+        nc.gpsimd.memset(slot_s[:].bitcast(I32), 0)
         nc.gpsimd.memset(w2_s[0][:, 0:E, :].bitcast(I32), 0)
         nc.vector.memset(w2_s[0][:, E:, :].bitcast(I32), 0)
         nc.vector.memset(dy_s[:, T:].bitcast(I32), 0)
-        nc.vector.memset(slot_s[:].bitcast(I32), 0)
+        nc.vector.memset(dy_s[32:64, 0:T].bitcast(I32), 0)
+        nc.vector.memset(dy_s[64:P, 0:T].bitcast(I32), 0)
         nc.gpsimd.memset(dy_w[:, PASSES * T :], 0)
         make_identity(nc, ident[:])
 
         halves = [slice(0, SHARE), slice(SHARE, T)]
+        nc.sync.dma_start(dy_s[0:32, 0:T].bitcast(I32), dy_scales.rearrange("s b t -> b s t").bitcast(I32))
         nc.sync.dma_start(offs_sb[:], offs)
-        nc.sync.dma_start(dy_s[0:P:PACK, 0:T].bitcast(I32), dy_scales.rearrange("s b t -> b s t").bitcast(I32))
         for h in range(2):
             nc.sync.dma_start(a_sb[h][:], a[:, halves[h]].rearrange("(p d) t -> p d t", d=PACK))
         nc.sync.dma_start(
@@ -133,7 +134,7 @@ def tile_moe_sub_silu_kernel(
         for q in range(QUADS):
             nc.sync.dma_start(
                 slot_s[32 * q : 32 * q + 4, :, :].bitcast(I32),
-                picked_s[32 * q : 32 * q + 32 : PACK, :].bitcast(I32),
+                picked_s[8 * q : 8 * q + 8, :].bitcast(I32),
             )
         gate_sb = placed.tile([P, TOP, T], F32, name="gate_sb", align_bytes=64, offset=gate_at)
         nc.sync.dma_start(gate_sb[:], gate.rearrange("r p t -> p r t"))

@@ -97,12 +97,12 @@ def tile_moe_sub_silu_kernel(
         halves = [slice(0, SHARE), slice(SHARE, T)]
         nc.sync.dma_start(dy_s[0:32, 0:T].bitcast(I32), dy_scales.rearrange("s b t -> b s t").bitcast(I32))
         nc.sync.dma_start(offs_sb[:], offs)
+        word_at = (T, 0)
         for h in range(2):
             nc.sync.dma_start(a_sb[h][:], a[:, halves[h]].rearrange("(p d) t -> p d t", d=PACK))
-        nc.sync.dma_start(
-            dy_w[:, 0 : PASSES * T].rearrange("p (s t) -> p s t", s=PASSES),
-            dy_words.rearrange("s p t d -> p s (t d)").bitcast(I32),
-        )
+            nc.sync.dma_start(
+                dy_w[:, word_at[h] : word_at[h] + T], dy_words[h].rearrange("p t d -> p (t d)").bitcast(I32)
+            )
 
         def load_w2_scales(h, quads):
             cols = slice(h * HALF_H, (h + 1) * HALF_H)
@@ -127,7 +127,7 @@ def tile_moe_sub_silu_kernel(
         def gather_words(s, i):
             first, n = WORD_PIECES[s][i]
             listed = offs_sb[:, first // PER_COL : (first + n) // PER_COL]
-            window = dy_w[:, s * T : s * T + WORD_WINDOW].bitcast(U32)
+            window = dy_w[:, word_at[s] : word_at[s] + WORD_WINDOW].bitcast(U32)
             nc.vector.tensor_copy(slot_w[s][i][:].bitcast(U32), window.indirect(listed))
 
         nc.vector.tensor_copy(picked_s[:], dy_s[:].indirect(offs_sb[:]))
@@ -140,11 +140,9 @@ def tile_moe_sub_silu_kernel(
         nc.sync.dma_start(gate_sb[:], gate.rearrange("r p t -> p r t"))
         nc.gpsimd.memset(w2_s[1][:].bitcast(I32), 0)
         load_w2_scales(1, range(QUADS))
-        gather_words(0, 0)
-        gather_words(1, 0)
-        gather_words(0, 1)
-        for i in range(1, len(WORD_PIECES[1])):
-            gather_words(1, i)
+        for s in range(PASSES):
+            for i in range(len(WORD_PIECES[s])):
+                gather_words(s, i)
 
         def woven(tile):
             return tile.rearrange("p (c i) d -> p c d i", i=PACK)
@@ -275,13 +273,14 @@ def tile_moe_sub_silu_kernel(
                 stop=True,
             )
             res = ring.tile([P, nb * P], F32, name="res")
-            nc.scalar.copy(res[:], res_bank[:])
+            if b0 + nb == BLOCKS:
+                nc.vector.tensor_copy(res[:], res_bank[:])
+            else:
+                nc.scalar.copy(res[:], res_bank[:])
             nc.sync.dma_start(out[:, b0 * P : (b0 + nb) * P], res[:])
 
-        for part in FIRST_PARTS[:2]:
-            product(0, *part, any_bank)
-        open0 = [early_pass(0, *part, any_bank) for part in FIRST_PARTS[2:]]
-        for part, y_bank in zip(FIRST_PARTS[2:], open0):
+        open0 = [early_pass(0, *part, any_bank) for part in FIRST_PARTS]
+        for part, y_bank in zip(FIRST_PARTS, open0):
             late_pass(0, *part, y_bank)
             copy_out(0, *part, y_bank)
         for j in range(1, HT):

@@ -26,7 +26,7 @@ HT = H // P
 BLOCKS = T // P
 PER_COL = 16
 FIRST_PARTS = ((0, 384), (384, 384), (768, 384), (1152, 256), (1408, 128))
-WORD_PIECES = (((0, 768), (768, 768)), ((0, 768), (768, 384), (1152, 256), (1408, 128)))
+WORD_PIECES = (((0, 768), (768, 768)), FIRST_PARTS)
 WORD_WINDOW = 1024
 BYTE_WINDOW = 2048
 SHARE = 256
@@ -154,9 +154,11 @@ def tile_moe_sub_silu_kernel(
             nc.scalar.activation(woven(silu_neg[h][:]), unwoven(a_sb[h][:]), ACT.Silu, scale=-1.0)
         shifted = placed.tile([P, SHARE, PACK], F32, name="shifted", align_bytes=64, offset=shifted_at)
         nc.gpsimd.tensor_scalar(shifted[:], silu_neg[0][:], 1.0, -1.0, ALU.mult, ALU.add)
-        for h in range(2):
-            nc.scalar.activation(woven(sig[:, halves[h], :]), unwoven(a_sb[h][:]), ACT.Sigmoid)
-        nc.gpsimd.tensor_tensor(slope_neg[:, halves[0], :], shifted[:], sig[:, halves[0], :], ALU.mult)
+        for first in range(0, SHARE, P):
+            toks = slice(first, first + P)
+            nc.scalar.activation(woven(sig[:, toks, :]), unwoven(a_sb[0][:, :, toks]), ACT.Sigmoid)
+            nc.gpsimd.tensor_tensor(slope_neg[:, toks, :], shifted[:, toks, :], sig[:, toks, :], ALU.mult)
+        nc.scalar.activation(woven(sig[:, halves[1], :]), unwoven(a_sb[1][:]), ACT.Sigmoid)
         nc.vector.scalar_tensor_tensor(
             slope_neg[:, halves[1], :], silu_neg[1][:], 1.0, sig[:, halves[1], :], ALU.subtract, ALU.mult
         )
@@ -279,10 +281,12 @@ def tile_moe_sub_silu_kernel(
                 nc.scalar.copy(res[:], res_bank[:])
             nc.sync.dma_start(out[:, b0 * P : (b0 + nb) * P], res[:])
 
-        open0 = [early_pass(0, *part, any_bank) for part in FIRST_PARTS]
-        for part, y_bank in zip(FIRST_PARTS, open0):
-            late_pass(0, *part, y_bank)
-            copy_out(0, *part, y_bank)
+        open0 = [early_pass(0, *FIRST_PARTS[0], any_bank)]
+        for k, part in enumerate(FIRST_PARTS):
+            if k + 1 < len(FIRST_PARTS):
+                open0.append(early_pass(0, *FIRST_PARTS[k + 1], any_bank))
+            late_pass(0, *part, open0[k])
+            copy_out(0, *part, open0[k])
         for j in range(1, HT):
             for part in PARTS:
                 product(j, *part, any_bank)

@@ -28,7 +28,8 @@ PER_COL = 16
 FIRST_PARTS = ((0, 384), (384, 384), (768, 384), (1152, 256), (1408, 128))
 WORD_PIECES = (((0, 768), (768, 768)), FIRST_PARTS)
 WORD_WINDOW = 1024
-BYTE_WINDOW = 2048
+BYTE_WINDOW = 2052
+ROWS_AT = 96
 SHARE = 256
 SHARES = (SHARE, T - SHARE)
 PARTS = ((0, 512), (512, 512), (1024, 512))
@@ -86,16 +87,14 @@ def tile_moe_sub_silu_kernel(
         ident = keep.tile([P, P], F32, name="ident")
 
         nc.gpsimd.memset(slot_s[:].bitcast(I32), 0)
-        nc.gpsimd.memset(w2_s[0][:, 0:E, :].bitcast(I32), 0)
-        nc.vector.memset(w2_s[0][:, E:, :].bitcast(I32), 0)
+        nc.gpsimd.memset(w2_s[0][:].bitcast(I32), 0)
         nc.vector.memset(dy_s[:, T:].bitcast(I32), 0)
-        nc.vector.memset(dy_s[32:64, 0:T].bitcast(I32), 0)
-        nc.vector.memset(dy_s[64:P, 0:T].bitcast(I32), 0)
+        nc.vector.memset(dy_s[0:ROWS_AT, 0 : T + 4].bitcast(I32), 0)
         nc.gpsimd.memset(dy_w[:, PASSES * T :], 0)
         make_identity(nc, ident[:])
 
         halves = [slice(0, SHARE), slice(SHARE, T)]
-        nc.sync.dma_start(dy_s[0:32, 0:T].bitcast(I32), dy_scales.rearrange("s b t -> b s t").bitcast(I32))
+        nc.sync.dma_start(dy_s[ROWS_AT:P, 0:T].bitcast(I32), dy_scales.rearrange("s b t -> b s t").bitcast(I32))
         nc.sync.dma_start(offs_sb[:], offs)
         word_at = (T, 0)
         for h in range(2):
@@ -134,7 +133,7 @@ def tile_moe_sub_silu_kernel(
         for q in range(QUADS):
             nc.sync.dma_start(
                 slot_s[32 * q : 32 * q + 4, :, :].bitcast(I32),
-                picked_s[8 * q : 8 * q + 8, :].bitcast(I32),
+                picked_s[ROWS_AT + 8 * q : ROWS_AT + 8 * q + 8, :].bitcast(I32),
             )
         gate_sb = placed.tile([P, TOP, T], F32, name="gate_sb", align_bytes=64, offset=gate_at)
         nc.sync.dma_start(gate_sb[:], gate.rearrange("r p t -> p r t"))

@@ -25,16 +25,17 @@ QUADS = 4
 HT = H // P
 BLOCKS = T // P
 PER_COL = 16
-FIRST_PARTS = ((0, 384), (384, 384), (768, 384), (1152, 256), (1408, 128))
+FIRST_PARTS = ((0, 512), (512, 512), (1024, 256), (1280, 256))
 WORD_PIECES = (((0, 768), (768, 768)), FIRST_PARTS)
 WORD_WINDOW = 1024
 BYTE_WINDOW = 2052
 ROWS_AT = 96
 SHARE = 256
 SHARES = (SHARE, T - SHARE)
-PARTS = ((0, 512), (512, 512), (1024, 512))
 HALF_H = H // 2
-LAST_CHUNKS = ((0, 2), (2, 1), (3, 1))
+BANK = 2048
+SHARED = BLOCKS - 1
+LONE = SHARED - 1
 
 
 def tile_moe_sub_silu_kernel(
@@ -45,14 +46,13 @@ def tile_moe_sub_silu_kernel(
         keep = ctx.enter_context(tc.tile_pool(name="keep", bufs=1))
         placed = ctx.enter_context(tc.tile_pool(name="placed", bufs=1))
         ring = ctx.enter_context(tc.tile_pool(name="ring", bufs=3))
-        picks = ctx.enter_context(tc.tile_pool(name="picks", bufs=21))
-        psum = ctx.enter_context(tc.psum_pool(name="psum", bufs=6))
-        psum_pair = ctx.enter_context(tc.psum_pool(name="psum_pair", bufs=1))
+        picks = ctx.enter_context(tc.tile_pool(name="picks", bufs=15))
+        psum = ctx.enter_context(tc.psum_pool(name="psum", bufs=1))
 
         plane_bytes = E * PASSES * HALF_H
         dy_s_at = plane_bytes - T
-        gate_at = plane_bytes
-        dy_w_at = gate_at + TOP * T * 4
+        gate_at = plane_bytes + 64
+        dy_w_at = gate_at + TOP * SHARED * P * 4
         shifted_at = dy_w_at + (T + WORD_WINDOW) * 4
         a_at = shifted_at + SHARE * PACK * 4
         offs_sb = keep.tile([P, SLOTS // PER_COL], U16, name="offs_sb")
@@ -83,7 +83,7 @@ def tile_moe_sub_silu_kernel(
         sig = keep.tile([P, T, PACK], F32, name="sig", align_bytes=64)
         silu_neg = [keep.tile([P, SHARES[h], PACK], F32, name="silu_neg%d" % h, align_bytes=64) for h in range(2)]
         slope_neg = keep.tile([P, T, PACK], F32, name="slope_neg", align_bytes=64)
-        dh_t = keep.tile([P, BLOCKS, PACK, P], F32, name="dh_t", align_bytes=64)
+        dh_t = keep.tile([P, SHARED, PACK, P], F32, name="dh_t", align_bytes=64)
         ident = keep.tile([P, P], F32, name="ident")
 
         nc.gpsimd.memset(slot_s[:].bitcast(I32), 0)
@@ -135,8 +135,8 @@ def tile_moe_sub_silu_kernel(
                 slot_s[32 * q : 32 * q + 4, :, :].bitcast(I32),
                 picked_s[ROWS_AT + 8 * q : ROWS_AT + 8 * q + 8, :].bitcast(I32),
             )
-        gate_sb = placed.tile([P, TOP, T], F32, name="gate_sb", align_bytes=64, offset=gate_at)
-        nc.sync.dma_start(gate_sb[:], gate.rearrange("r p t -> p r t"))
+        gate_sb = placed.tile([P, TOP, SHARED * P], F32, name="gate_sb", align_bytes=64, offset=gate_at)
+        nc.sync.dma_start(gate_sb[:], gate[:, :, 0 : SHARED * P].rearrange("r p t -> p r t"))
         nc.gpsimd.memset(w2_s[1][:].bitcast(I32), 0)
         load_w2_scales(1, range(QUADS))
         for s in range(PASSES):
@@ -163,6 +163,9 @@ def tile_moe_sub_silu_kernel(
         )
 
         load_w2_words(1)
+        gate_t = placed.tile([P, TOP], F32, name="gate_t", align_bytes=64, offset=dy_w_at + 2 * K)
+        with nc.allow_non_contiguous_dma(reason="one gate value a token and partition"):
+            nc.sync.dma_start(gate_t[:], gate[:, 0, SHARED * P : T].rearrange("r t -> t r"))
         w1_w = placed.tile([P, 2 * K], U8, name="w1_w", align_bytes=64, offset=dy_w_at)
         nc.sync.dma_start(w1_w[:].bitcast(I32), w1t_words[0].bitcast(I32))
         w1_s = placed.tile([P, K], U8, name="w1_s", align_bytes=64, offset=shifted_at)
@@ -172,98 +175,113 @@ def tile_moe_sub_silu_kernel(
                 w1_s[32 * q : 32 * q + 4, :].bitcast(I32), w1t_scales[0, 4 * q : 4 * q + 4, :].bitcast(I32)
             )
 
-        def any_bank(shape):
-            return psum.tile(shape, F32, name="bank")
+        banks_used = []
 
-        def bank_x(shape):
-            return psum_pair.tile(shape, F32, name="bank_x")
+        def bank(number, shape):
+            banks_used.append(number)
+            return psum.tile(shape, F32, name="bank%d" % len(banks_used), offset=number * BANK)
 
-        def bank_y(shape):
-            return psum_pair.tile(shape, F32, name="bank_y")
-
-        def one_pass(j, y_bank, start, u, s, opens, closes):
+        def one_pass(j, target, slot, width, s, opens, closes):
             h, col = divmod(j * P, HALF_H)
-            slot = start + u
             e = slot // C
             piece = max(i for i, (first, n) in enumerate(WORD_PIECES[s]) if first <= slot)
             at = slot - WORD_PIECES[s][piece][0]
             nc.tensor.matmul_mx(
-                out=y_bank[:, u : u + P],
+                out=target,
                 lhsT=w2_w[h][:, e * PASSES + s, 2 * col : 2 * (col + P)].bitcast(FP4X4),
                 lhsT_scale=w2_s[h][:, e * PASSES + s, col : col + P],
-                rhs=slot_w[s][piece][:, at : at + P].bitcast(FP8X4),
-                rhs_scale=slot_s[:, s, slot : slot + P],
+                rhs=slot_w[s][piece][:, at : at + width].bitcast(FP8X4),
+                rhs_scale=slot_s[:, s, slot : slot + width],
                 start=opens,
                 stop=closes,
             )
 
-        def product(j, start, width, bank):
-            y_bank = bank([P, width])
-            for u in range(0, width, P):
+        def product(j, first, number):
+            y_bank = bank(number, [P, 2 * C])
+            for u in range(0, 2 * C, C):
                 for s in reversed(range(PASSES)):
-                    one_pass(j, y_bank, start, u, s, s == PASSES - 1, s == 0)
-            nc.scalar.copy(y[j][:, start : start + width], y_bank[:])
+                    one_pass(j, y_bank[:, u : u + C], first * C + u, C, s, s == PASSES - 1, s == 0)
+            nc.scalar.copy(y[j][:, first * C : (first + 2) * C], y_bank[:])
 
-        def early_pass(j, start, width, bank):
-            y_bank = bank([P, width])
-            for u in range(0, width, P):
-                one_pass(j, y_bank, start, u, 0, u == 0, False)
+        def early_pass(k):
+            start, width = FIRST_PARTS[k]
+            y_bank = bank(k, [P, width])
+            for u in range(0, width, C):
+                one_pass(0, y_bank[:, u : u + C], start + u, C, 0, u == 0, False)
             return y_bank
 
-        def late_pass(j, start, width, y_bank):
-            for u in range(0, width, P):
-                one_pass(j, y_bank, start, u, 1, False, u == width - P)
+        def late_pass(k, y_bank):
+            start, width = FIRST_PARTS[k]
+            for u in range(0, width, C):
+                one_pass(0, y_bank[:, u : u + C], start + u, C, 1, False, u == width - C)
+            nc.scalar.copy(y[0][:, start : start + width], y_bank[:])
 
-        def copy_out(j, start, width, y_bank):
-            nc.scalar.copy(y[j][:, start : start + width], y_bank[:])
+        def listed(r, b0, nb):
+            return pos_sb[r][:, b0 * P // PER_COL : (b0 + nb) * P // PER_COL]
 
-        def combine(j, b0, nb, bank):
-            toks = slice(b0 * P, (b0 + nb) * P)
-            cols = slice(b0 * P // PER_COL, (b0 + nb) * P // PER_COL)
-            turned = bank([P, nb, P])
+        def combine(j, b0, nb, number):
+            turned = bank(number, [P, nb, P])
             for r in range(TOP):
-                picked = picks.tile([P, nb * P], F32, name="picked")
-                nc.vector.tensor_tensor(picked[:], y[j][:].indirect(pos_sb[r][:, cols]), gate_sb[:, r, toks], ALU.mult)
+                gated = picks.tile([P, nb * P], F32, name="gated")
+                nc.vector.tensor_tensor(
+                    gated[:], y[j][:].indirect(listed(r, b0, nb)), gate_sb[:, r, b0 * P : (b0 + nb) * P], ALU.mult
+                )
                 for b in range(nb):
                     nc.tensor.matmul(
                         turned[:, b, :],
-                        lhsT=picked[:, b * P : (b + 1) * P],
+                        lhsT=gated[:, b * P : (b + 1) * P],
                         rhs=ident[:],
                         is_transpose=True,
                         start=(r == 0 and b == 0),
                         stop=(r == TOP - 1 and b == nb - 1),
                     )
+            return turned
+
+        def sort_out(j, b0, nb, turned):
             rows = slice(j * P // PACK, (j + 1) * P // PACK)
             nc.scalar.copy(dh_t[:, b0 : b0 + nb, :, rows], turned[:].rearrange("t b (m d) -> t b d m", d=PACK))
 
-        backs = {}
+        plains = {}
 
-        def turn_back(b0, nb):
-            for b in range(b0, b0 + nb):
-                backs[b] = psum.tile([P, PACK, P], F32, name="bank")
+        def fetch_plain(j):
+            for r in range(TOP):
+                plains[j, r] = picks.tile([P, P], F32, name="plain")
+                nc.scalar.activation(plains[j, r][:], y[j][:].indirect(listed(r, SHARED, 1)), ACT.Copy)
+
+        def turn_back(terms, number):
+            back = bank(number, [P, PACK, P])
+            for r, term in enumerate(terms):
                 for d in range(PACK):
-                    nc.tensor.transpose(backs[b][:, d, :], dh_t[:, b, d, :], ident[:])
+                    nc.tensor.matmul(
+                        back[:, d, :],
+                        lhsT=term[:, d, :],
+                        rhs=ident[:],
+                        is_transpose=True,
+                        start=(r == 0 and d == 0),
+                        stop=(r == len(terms) - 1 and d == PACK - 1),
+                    )
+            return back
 
-        def finish_gradient(b0, nb):
-            da = ring.tile([P, nb * P, PACK], BF16, name="da", align_bytes=64)
-            for b in range(b0, b0 + nb):
+        def finish_gradient(b0, backs):
+            da = ring.tile([P, len(backs) * P, PACK], BF16, name="da", align_bytes=64)
+            for k, back in enumerate(backs):
                 nc.vector.scalar_tensor_tensor(
-                    da[:, (b - b0) * P : (b - b0 + 1) * P, :],
-                    backs[b][:].rearrange("p d t -> p t d"),
+                    da[:, k * P : (k + 1) * P, :],
+                    back[:].rearrange("p d t -> p t d"),
                     -1.0,
-                    slope_neg[:, b * P : (b + 1) * P, :],
+                    slope_neg[:, (b0 + k) * P : (b0 + k + 1) * P, :],
                     ALU.mult,
                     ALU.mult,
                 )
             return da
 
-        def project(b0, nb, da):
+        def project(b0, nb, da, number, copy):
             da_w = ring.tile([P, nb * P], U32, name="da_w", align_bytes=64)
             da_s = ring.tile([P, nb * P], U8, name="da_s", align_bytes=64)
             nc.vector.quantize_mx(
                 out=da_w[:].bitcast(FP8X4), scales=da_s[:], in_=da[:].rearrange("p t d -> p (t d)")
             )
-            res_bank = psum.tile([P, nb * P], F32, name="bank")
+            res_bank = bank(number, [P, nb * P])
             nc.tensor.matmul_mx(
                 out=res_bank[:],
                 lhsT=w1_w[:].bitcast(FP4X4),
@@ -274,35 +292,57 @@ def tile_moe_sub_silu_kernel(
                 stop=True,
             )
             res = ring.tile([P, nb * P], F32, name="res")
-            if b0 + nb == BLOCKS:
-                nc.vector.tensor_copy(res[:], res_bank[:])
-            else:
-                nc.scalar.copy(res[:], res_bank[:])
+            copy(res[:], res_bank[:])
             nc.sync.dma_start(out[:, b0 * P : (b0 + nb) * P], res[:])
 
-        open0 = [early_pass(0, *FIRST_PARTS[0], any_bank)]
-        for k, part in enumerate(FIRST_PARTS):
+        on_scalar, on_vector = nc.scalar.copy, nc.vector.tensor_copy
+        open0 = [early_pass(0)]
+        for k in range(len(FIRST_PARTS)):
             if k + 1 < len(FIRST_PARTS):
-                open0.append(early_pass(0, *FIRST_PARTS[k + 1], any_bank))
-            late_pass(0, *part, open0[k])
-            copy_out(0, *part, open0[k])
-        for j in range(1, HT):
-            for part in PARTS:
-                product(j, *part, any_bank)
-        for j in range(HT - 2):
-            combine(j, 0, BLOCKS, any_bank)
-        first, second, third = LAST_CHUNKS
-        combine(HT - 2, *first, bank_x)
-        combine(HT - 1, *first, bank_y)
-        combine(HT - 2, second[0], second[1] + third[1], bank_x)
-        turn_back(*first)
-        combine(HT - 1, *second, bank_y)
-        combine(HT - 1, *third, bank_x)
-        turn_back(*second)
-        turn_back(*third)
-        da_first = finish_gradient(*first)
-        da_second = finish_gradient(*second)
-        project(*first, da_first)
-        da_third = finish_gradient(*third)
-        project(*second, da_second)
-        project(*third, da_third)
+                open0.append(early_pass(k + 1))
+            late_pass(k, open0[k])
+        for j, numbers in ((1, (0, 1, 2)), (2, (3, 4, 0)), (3, (1, 2, 3))):
+            for pair, number in enumerate(numbers):
+                product(j, 2 * pair, number)
+
+        apart = [bank(number, [P, HT, P]) for number in (1, 2, 3)]
+
+        def turn_plain(j):
+            for r in range(TOP):
+                nc.tensor.transpose(apart[r][:, j, :], plains[j, r][:], ident[:])
+
+        weighed = [keep.tile([P, PACK, P], F32, name="weighed%d" % r, align_bytes=64) for r in range(TOP)]
+
+        def weigh(r):
+            nc.scalar.activation(
+                weighed[r][:],
+                apart[r][:].rearrange("t j (m d) -> t d (j m)", d=PACK),
+                ACT.Copy,
+                scale=gate_t[:, r : r + 1],
+            )
+
+        sort_out(0, 0, SHARED, combine(0, 0, SHARED, 0))
+        fetch_plain(0)
+        fetch_plain(1)
+        sort_out(1, 0, SHARED, combine(1, 0, SHARED, 4))
+        turn_plain(0)
+        turn_plain(1)
+        fetch_plain(2)
+        sort_out(2, 0, SHARED, combine(2, 0, SHARED, 5))
+        turn_plain(2)
+        sort_out(3, 0, 2, combine(3, 0, 2, 6))
+        fetch_plain(3)
+        lone_sum = combine(3, LONE, 1, 7)
+        back_pair = [turn_back([dh_t[:, b, :, :]], number) for b, number in enumerate((0, 4))]
+        turn_plain(3)
+        sort_out(3, LONE, 1, lone_sum)
+        back_lone = turn_back([dh_t[:, LONE, :, :]], 5)
+        for r in range(TOP):
+            weigh(r)
+        back_last = turn_back([tile[:] for tile in weighed], 6)
+        da_pair = finish_gradient(0, back_pair)
+        da_lone = finish_gradient(LONE, [back_lone])
+        project(0, 2, da_pair, 7, on_scalar)
+        project(LONE, 1, da_lone, 0, on_scalar)
+        da_last = finish_gradient(SHARED, [back_last])
+        project(SHARED, 1, da_last, 4, on_vector)

@@ -46,7 +46,7 @@ def tile_moe_sub_silu_kernel(
         keep = ctx.enter_context(tc.tile_pool(name="keep", bufs=1))
         placed = ctx.enter_context(tc.tile_pool(name="placed", bufs=1))
         ring = ctx.enter_context(tc.tile_pool(name="ring", bufs=3))
-        picks = ctx.enter_context(tc.tile_pool(name="picks", bufs=15))
+        picks = ctx.enter_context(tc.tile_pool(name="picks", bufs=17))
         psum = ctx.enter_context(tc.psum_pool(name="psum", bufs=1))
 
         plane_bytes = E * PASSES * HALF_H
@@ -222,9 +222,12 @@ def tile_moe_sub_silu_kernel(
         def combine(j, b0, nb, number):
             turned = bank(number, [P, nb, P])
             for r in range(TOP):
-                gated = picks.tile([P, nb * P], F32, name="gated")
+                if (j, b0, r) == (HT - 2, LONE, 0):
+                    gated = gate_sb[:, TOP - 1, 0:P]
+                else:
+                    gated = picks.tile([P, nb * P], F32, name="gated")[:]
                 nc.vector.tensor_tensor(
-                    gated[:], y[j][:].indirect(listed(r, b0, nb)), gate_sb[:, r, b0 * P : (b0 + nb) * P], ALU.mult
+                    gated, y[j][:].indirect(listed(r, b0, nb)), gate_sb[:, r, b0 * P : (b0 + nb) * P], ALU.mult
                 )
                 for b in range(nb):
                     nc.tensor.matmul(
@@ -327,22 +330,24 @@ def tile_moe_sub_silu_kernel(
         sort_out(1, 0, SHARED, combine(1, 0, SHARED, 4))
         turn_plain(0)
         turn_plain(1)
+        sort_out(2, 0, 2, combine(2, 0, 2, 5))
         fetch_plain(2)
-        sort_out(2, 0, SHARED, combine(2, 0, SHARED, 5))
         turn_plain(2)
-        sort_out(3, 0, 2, combine(3, 0, 2, 6))
+        pair_sum = combine(3, 0, 2, 6)
         fetch_plain(3)
-        lone_sum = combine(3, LONE, 1, 7)
-        back_pair = [turn_back([dh_t[:, b, :, :]], number) for b, number in enumerate((0, 4))]
+        sort_out(3, 0, 2, pair_sum)
         turn_plain(3)
+        back_pair = [turn_back([dh_t[:, b, :, :]], number) for b, number in enumerate((0, 4))]
+        sort_out(2, LONE, 1, combine(2, LONE, 1, 7))
+        weigh(0)
+        lone_sum = combine(3, LONE, 1, 1)
+        weigh(1)
+        weigh(2)
+        back_last = turn_back([tile[:] for tile in weighed], 5)
         sort_out(3, LONE, 1, lone_sum)
-        back_lone = turn_back([dh_t[:, LONE, :, :]], 5)
-        for r in range(TOP):
-            weigh(r)
-        back_last = turn_back([tile[:] for tile in weighed], 6)
-        da_pair = finish_gradient(0, back_pair)
-        da_lone = finish_gradient(LONE, [back_lone])
-        project(0, 2, da_pair, 7, on_scalar)
-        project(LONE, 1, da_lone, 0, on_scalar)
+        back_lone = turn_back([dh_t[:, LONE, :, :]], 7)
+        project(0, 2, finish_gradient(0, back_pair), 6, on_scalar)
         da_last = finish_gradient(SHARED, [back_last])
-        project(SHARED, 1, da_last, 4, on_vector)
+        da_lone = finish_gradient(LONE, [back_lone])
+        project(SHARED, 1, da_last, 2, on_scalar)
+        project(LONE, 1, da_lone, 3, on_vector)

@@ -30,12 +30,11 @@ WORD_PIECES = (((0, 768), (768, 768)), FIRST_PARTS)
 WORD_WINDOW = 1024
 BYTE_WINDOW = 2052
 ROWS_AT = 96
-SHARE = 256
-SHARES = (SHARE, T - SHARE)
 HALF_H = H // 2
 BANK = 2048
 SHARED = BLOCKS - 1
 LONE = SHARED - 1
+PAIRS = PACK // 2
 
 
 def tile_moe_sub_silu_kernel(
@@ -46,7 +45,7 @@ def tile_moe_sub_silu_kernel(
         keep = ctx.enter_context(tc.tile_pool(name="keep", bufs=1))
         placed = ctx.enter_context(tc.tile_pool(name="placed", bufs=1))
         ring = ctx.enter_context(tc.tile_pool(name="ring", bufs=3))
-        picks = ctx.enter_context(tc.tile_pool(name="picks", bufs=17))
+        picks = ctx.enter_context(tc.tile_pool(name="picks", bufs=15))
         psum = ctx.enter_context(tc.psum_pool(name="psum", bufs=1))
 
         plane_bytes = E * PASSES * HALF_H
@@ -54,7 +53,9 @@ def tile_moe_sub_silu_kernel(
         gate_at = plane_bytes + 64
         dy_w_at = gate_at + TOP * SHARED * P * 4
         shifted_at = dy_w_at + (T + WORD_WINDOW) * 4
-        a_at = shifted_at + SHARE * PACK * 4
+        a_at = shifted_at + SHARED * H * 4
+        picked_at = a_at + SHARED * H * 4
+        a_last_at = picked_at + 2 * plane_bytes
         offs_sb = keep.tile([P, SLOTS // PER_COL], U16, name="offs_sb")
         pos_sb = [keep.tile([P, T // PER_COL], U16, name="pos_sb%d" % r) for r in range(TOP)]
         dy_s = placed.tile([P, BYTE_WINDOW], U8, name="dy_s", align_bytes=64, offset=dy_s_at)
@@ -65,43 +66,50 @@ def tile_moe_sub_silu_kernel(
         ]
         w2_w = [
             keep.tile([P, E * PASSES, 2 * HALF_H], U8, name="w2_w0", align_bytes=64),
-            placed.tile([P, E * PASSES, 2 * HALF_H], U8, name="w2_w1", align_bytes=64, offset=a_at),
+            placed.tile([P, E * PASSES, 2 * HALF_H], U8, name="w2_w1", align_bytes=64, offset=picked_at),
         ]
         slot_w = [
             [keep.tile([P, n], I32, name="slot_w%d_%d" % (s, first), align_bytes=64) for first, n in WORD_PIECES[s]]
             for s in range(PASSES)
         ]
-        picked_s = keep.tile([P, SLOTS], U8, name="picked_s", align_bytes=64)
+        picked_s = placed.tile([P, SLOTS], U8, name="picked_s", align_bytes=64, offset=picked_at)
         slot_s = keep.tile([P, PASSES, SLOTS], U8, name="slot_s", align_bytes=64)
         y = [keep.tile([P, SLOTS], F32, name="y%d" % j, align_bytes=64) for j in range(HT)]
-        a_sb = [
-            placed.tile(
-                [P, PACK, SHARES[h]], F32, name="a_sb%d" % h, align_bytes=64, offset=a_at + h * PACK * SHARE * 4
-            )
-            for h in range(2)
+        a_rows = placed.tile([P, HT, SHARED * P], F32, name="a_rows", align_bytes=64, offset=a_at)
+        a_last = placed.tile([P, PACK, P], F32, name="a_last", align_bytes=64, offset=a_last_at)
+        sig_at = {0: a_at + 2 * H * 4, 1: a_at + H * 4, SHARED: a_at}
+        sig = [
+            placed.tile([P, H], F32, name="sig%d" % b, align_bytes=64, offset=sig_at[b])
+            if b in sig_at
+            else keep.tile([P, H], F32, name="sig%d" % b, align_bytes=64)
+            for b in range(BLOCKS)
         ]
-        sig = keep.tile([P, T, PACK], F32, name="sig", align_bytes=64)
-        silu_neg = [keep.tile([P, SHARES[h], PACK], F32, name="silu_neg%d" % h, align_bytes=64) for h in range(2)]
-        slope_neg = keep.tile([P, T, PACK], F32, name="slope_neg", align_bytes=64)
-        dh_t = keep.tile([P, SHARED, PACK, P], F32, name="dh_t", align_bytes=64)
+        silu_neg = [keep.tile([P, H], F32, name="silu_neg%d" % b, align_bytes=64) for b in range(BLOCKS)]
+        slope = [keep.tile([P, H], F32, name="slope%d" % b, align_bytes=64) for b in range(BLOCKS)]
         ident = keep.tile([P, P], F32, name="ident")
 
         nc.gpsimd.memset(slot_s[:].bitcast(I32), 0)
         nc.gpsimd.memset(w2_s[0][:].bitcast(I32), 0)
         nc.vector.memset(dy_s[:, T:].bitcast(I32), 0)
         nc.vector.memset(dy_s[0:ROWS_AT, 0 : T + 4].bitcast(I32), 0)
-        nc.gpsimd.memset(dy_w[:, PASSES * T :], 0)
         make_identity(nc, ident[:])
+        nc.gpsimd.memset(dy_w[:, PASSES * T :], 0)
 
-        halves = [slice(0, SHARE), slice(SHARE, T)]
         nc.sync.dma_start(dy_s[ROWS_AT:P, 0:T].bitcast(I32), dy_scales.rearrange("s b t -> b s t").bitcast(I32))
         nc.sync.dma_start(offs_sb[:], offs)
         word_at = (T, 0)
-        for h in range(2):
-            nc.sync.dma_start(a_sb[h][:], a[:, halves[h]].rearrange("(p d) t -> p d t", d=PACK))
+
+        def load_words(s):
             nc.sync.dma_start(
-                dy_w[:, word_at[h] : word_at[h] + T], dy_words[h].rearrange("p t d -> p (t d)").bitcast(I32)
+                dy_w[:, word_at[s] : word_at[s] + T], dy_words[s].rearrange("p t d -> p (t d)").bitcast(I32)
             )
+
+        a_by_tile = a[:, 0 : SHARED * P].rearrange("(j p) t -> p j t", p=P)
+        nc.sync.dma_start(a_rows[:, 0:2, :], a_by_tile[:, 0:2, :])
+        load_words(0)
+        nc.sync.dma_start(a_rows[:, 2:HT, :], a_by_tile[:, 2:HT, :])
+        nc.sync.dma_start(a_last[:], a[:, SHARED * P : T].rearrange("(p d) t -> p d t", d=PACK))
+        load_words(1)
 
         def load_w2_scales(h, quads):
             cols = slice(h * HALF_H, (h + 1) * HALF_H)
@@ -125,9 +133,9 @@ def tile_moe_sub_silu_kernel(
 
         def gather_words(s, i):
             first, n = WORD_PIECES[s][i]
-            listed = offs_sb[:, first // PER_COL : (first + n) // PER_COL]
+            entries = offs_sb[:, first // PER_COL : (first + n) // PER_COL]
             window = dy_w[:, word_at[s] : word_at[s] + WORD_WINDOW].bitcast(U32)
-            nc.vector.tensor_copy(slot_w[s][i][:].bitcast(U32), window.indirect(listed))
+            nc.vector.tensor_copy(slot_w[s][i][:].bitcast(U32), window.indirect(entries))
 
         nc.vector.tensor_copy(picked_s[:], dy_s[:].indirect(offs_sb[:]))
         for q in range(QUADS):
@@ -139,47 +147,66 @@ def tile_moe_sub_silu_kernel(
         nc.sync.dma_start(gate_sb[:], gate[:, :, 0 : SHARED * P].rearrange("r p t -> p r t"))
         nc.gpsimd.memset(w2_s[1][:].bitcast(I32), 0)
         load_w2_scales(1, range(QUADS))
+        load_w2_words(1)
         for s in range(PASSES):
             for i in range(len(WORD_PIECES[s])):
                 gather_words(s, i)
-
-        def woven(tile):
-            return tile.rearrange("p (c i) d -> p c d i", i=PACK)
-
-        def unwoven(tile):
-            return tile.rearrange("p d (c i) -> p c d i", i=PACK)
-
-        for h in range(2):
-            nc.scalar.activation(woven(silu_neg[h][:]), unwoven(a_sb[h][:]), ACT.Silu, scale=-1.0)
-        shifted = placed.tile([P, SHARE, PACK], F32, name="shifted", align_bytes=64, offset=shifted_at)
-        nc.gpsimd.tensor_scalar(shifted[:], silu_neg[0][:], 1.0, -1.0, ALU.mult, ALU.add)
-        for first in range(0, SHARE, P):
-            toks = slice(first, first + P)
-            nc.scalar.activation(woven(sig[:, toks, :]), unwoven(a_sb[0][:, :, toks]), ACT.Sigmoid)
-            nc.gpsimd.tensor_tensor(slope_neg[:, toks, :], shifted[:, toks, :], sig[:, toks, :], ALU.mult)
-        nc.scalar.activation(woven(sig[:, halves[1], :]), unwoven(a_sb[1][:]), ACT.Sigmoid)
-        nc.vector.scalar_tensor_tensor(
-            slope_neg[:, halves[1], :], silu_neg[1][:], 1.0, sig[:, halves[1], :], ALU.subtract, ALU.mult
-        )
-
-        load_w2_words(1)
-        gate_t = placed.tile([P, TOP], F32, name="gate_t", align_bytes=64, offset=dy_w_at + 2 * K)
-        with nc.allow_non_contiguous_dma(reason="one gate value a token and partition"):
-            nc.sync.dma_start(gate_t[:], gate[:, 0, SHARED * P : T].rearrange("r t -> t r"))
-        w1_w = placed.tile([P, 2 * K], U8, name="w1_w", align_bytes=64, offset=dy_w_at)
-        nc.sync.dma_start(w1_w[:].bitcast(I32), w1t_words[0].bitcast(I32))
-        w1_s = placed.tile([P, K], U8, name="w1_s", align_bytes=64, offset=shifted_at)
-        nc.gpsimd.memset(w1_s[:].bitcast(I32), 0)
-        for q in range(QUADS):
-            nc.sync.dma_start(
-                w1_s[32 * q : 32 * q + 4, :].bitcast(I32), w1t_scales[0, 4 * q : 4 * q + 4, :].bitcast(I32)
-            )
 
         banks_used = []
 
         def bank(number, shape):
             banks_used.append(number)
             return psum.tile(shape, F32, name="bank%d" % len(banks_used), offset=number * BANK)
+
+        def by_pairs(ap):
+            return ap.rearrange("t (p u e) -> t u p e", u=PAIRS, e=2)
+
+        def as_pairs(ap):
+            return ap.rearrange("t (u p e) -> t u p e", u=PAIRS, e=2)
+
+        a_turned = [bank(b, [P, H]) for b in range(SHARED)]
+        for b, j in [(b, j) for half in (0, 2) for b in range(SHARED) for j in (half, half + 1)]:
+            if True:
+                nc.tensor.transpose(a_turned[b][:, j * P : (j + 1) * P], a_rows[:, j, b * P : (b + 1) * P], ident[:])
+
+        def activate(b, target, func, scale):
+            if b < SHARED:
+                nc.scalar.activation(as_pairs(target[:]), by_pairs(a_turned[b][:]), func, scale=scale)
+            else:
+                nc.scalar.activation(
+                    target[:].rearrange("p (c i d) -> p c d i", i=PACK, d=PACK),
+                    a_last[:].rearrange("p d (c i) -> p c d i", i=PACK),
+                    func,
+                    scale=scale,
+                )
+
+        shifted = [
+            placed.tile([P, H], F32, name="shifted%d" % b, align_bytes=64, offset=shifted_at + b * H * 4)
+            for b in range(SHARED)
+        ]
+        for b in range(BLOCKS):
+            activate(b, silu_neg[b], ACT.Silu, -1.0)
+            if b < SHARED:
+                nc.gpsimd.tensor_scalar(shifted[b][:], silu_neg[b][:], -1.0, 1.0, ALU.mult, ALU.add)
+        for b in range(BLOCKS):
+            activate(b, sig[b], ACT.Sigmoid, 1.0)
+            if b < SHARED:
+                nc.gpsimd.tensor_tensor(slope[b][:], shifted[b][:], sig[b][:], ALU.mult)
+        nc.vector.scalar_tensor_tensor(
+            slope[SHARED][:], silu_neg[SHARED][:], 1.0, sig[SHARED][:], ALU.subtract, ALU.mult
+        )
+
+        gate_t = placed.tile([P, TOP], F32, name="gate_t", align_bytes=64, offset=a_last_at + 2 * K)
+        with nc.allow_non_contiguous_dma(reason="one gate value a token and partition"):
+            nc.sync.dma_start(gate_t[:], gate[:, 0, SHARED * P : T].rearrange("r t -> t r"))
+        w1_w = placed.tile([P, 2 * K], U8, name="w1_w", align_bytes=64, offset=a_last_at)
+        nc.sync.dma_start(w1_w[:].bitcast(I32), w1t_words[0].bitcast(I32))
+        w1_s = placed.tile([P, K], U8, name="w1_s", align_bytes=64, offset=shifted_at + LONE * H * 4)
+        nc.gpsimd.memset(w1_s[:].bitcast(I32), 0)
+        for q in range(QUADS):
+            nc.sync.dma_start(
+                w1_s[32 * q : 32 * q + 4, :].bitcast(I32), w1t_scales[0, 4 * q : 4 * q + 4, :].bitcast(I32)
+            )
 
         def one_pass(j, target, slot, width, s, opens, closes):
             h, col = divmod(j * P, HALF_H)
@@ -196,16 +223,17 @@ def tile_moe_sub_silu_kernel(
                 stop=closes,
             )
 
-        def product(j, first, number):
+        def product(j, pair, number):
+            first = 2 * pair * C
             y_bank = bank(number, [P, 2 * C])
             for u in range(0, 2 * C, C):
                 for s in reversed(range(PASSES)):
-                    one_pass(j, y_bank[:, u : u + C], first * C + u, C, s, s == PASSES - 1, s == 0)
-            nc.scalar.copy(y[j][:, first * C : (first + 2) * C], y_bank[:])
+                    one_pass(j, y_bank[:, u : u + C], first + u, C, s, s == PASSES - 1, s == 0)
+            nc.scalar.copy(y[j][:, first : first + 2 * C], y_bank[:])
 
         def early_pass(k):
             start, width = FIRST_PARTS[k]
-            y_bank = bank(k, [P, width])
+            y_bank = bank(QUADS + k, [P, width])
             for u in range(0, width, C):
                 one_pass(0, y_bank[:, u : u + C], start + u, C, 0, u == 0, False)
             return y_bank
@@ -214,76 +242,88 @@ def tile_moe_sub_silu_kernel(
             start, width = FIRST_PARTS[k]
             for u in range(0, width, C):
                 one_pass(0, y_bank[:, u : u + C], start + u, C, 1, False, u == width - C)
-            nc.scalar.copy(y[0][:, start : start + width], y_bank[:])
+            copy = nc.vector.tensor_copy if k == len(FIRST_PARTS) - 1 else nc.scalar.copy
+            copy(y[0][:, start : start + width], y_bank[:])
 
         def listed(r, b0, nb):
             return pos_sb[r][:, b0 * P // PER_COL : (b0 + nb) * P // PER_COL]
 
-        def combine(j, b0, nb, number):
-            turned = bank(number, [P, nb, P])
-            for r in range(TOP):
-                if (j, b0, r) == (HT - 2, LONE, 0):
-                    gated = gate_sb[:, TOP - 1, 0:P]
-                else:
-                    gated = picks.tile([P, nb * P], F32, name="gated")[:]
-                nc.vector.tensor_tensor(
-                    gated, y[j][:].indirect(listed(r, b0, nb)), gate_sb[:, r, b0 * P : (b0 + nb) * P], ALU.mult
-                )
-                for b in range(nb):
-                    nc.tensor.matmul(
-                        turned[:, b, :],
-                        lhsT=gated[:, b * P : (b + 1) * P],
-                        rhs=ident[:],
-                        is_transpose=True,
-                        start=(r == 0 and b == 0),
-                        stop=(r == TOP - 1 and b == nb - 1),
-                    )
-            return turned
+        gated = {}
 
-        def sort_out(j, b0, nb, turned):
-            rows = slice(j * P // PACK, (j + 1) * P // PACK)
-            nc.scalar.copy(dh_t[:, b0 : b0 + nb, :, rows], turned[:].rearrange("t b (m d) -> t b d m", d=PACK))
+        def fetch_gated(j, r, b0, nb):
+            picked = picks.tile([P, nb * P], F32, name="gated")
+            nc.vector.tensor_tensor(
+                picked[:], y[j][:].indirect(listed(r, b0, nb)), gate_sb[:, r, b0 * P : (b0 + nb) * P], ALU.mult
+            )
+            for b in range(nb):
+                gated[j, r, b0 + b] = picked[:, b * P : (b + 1) * P]
+
+        def turn_gated(j, r, b):
+            nc.tensor.matmul(
+                sums[b][:, j * P : (j + 1) * P],
+                lhsT=gated[j, r, b],
+                rhs=ident[:],
+                is_transpose=True,
+                start=(r == 0),
+                stop=(r == TOP - 1),
+            )
+
+        def combine(j, r, b0, nb):
+            fetch_gated(j, r, b0, nb)
+            for b in range(b0, b0 + nb):
+                turn_gated(j, r, b)
 
         plains = {}
 
-        def fetch_plain(j):
-            for r in range(TOP):
+        def fetch_plain(j, choices=range(TOP)):
+            for r in choices:
                 plains[j, r] = picks.tile([P, P], F32, name="plain")
                 nc.scalar.activation(plains[j, r][:], y[j][:].indirect(listed(r, SHARED, 1)), ACT.Copy)
 
-        def turn_back(terms, number):
-            back = bank(number, [P, PACK, P])
-            for r, term in enumerate(terms):
-                for d in range(PACK):
-                    nc.tensor.matmul(
-                        back[:, d, :],
-                        lhsT=term[:, d, :],
-                        rhs=ident[:],
-                        is_transpose=True,
-                        start=(r == 0 and d == 0),
-                        stop=(r == len(terms) - 1 and d == PACK - 1),
-                    )
+        def turn_plain(j, choices=range(TOP)):
+            for r in choices:
+                nc.tensor.transpose(apart[r][:, j, :], plains[j, r][:], ident[:])
+
+        weighed = [keep.tile([P, PACK, P], F32, name="weighed%d" % r, align_bytes=64) for r in range(TOP)]
+
+        def weigh(r):
+            nc.scalar.activation(
+                weighed[r][:],
+                apart[r][:].rearrange("t j (m d) -> t d (j m)", d=PACK),
+                ACT.Copy,
+                scale=gate_t[:, r : r + 1],
+            )
+
+        def add_back(r, back):
+            for d in range(PACK):
+                nc.tensor.matmul(
+                    back[:, d, :],
+                    lhsT=weighed[r][:, d, :],
+                    rhs=ident[:],
+                    is_transpose=True,
+                    start=(r == 0 and d == 0),
+                    stop=(r == TOP - 1 and d == PACK - 1),
+                )
+
+        def slope_times_sums(b):
+            da_t = ring.tile([P, H], BF16, name="da_t", align_bytes=64)
+            nc.vector.tensor_tensor(as_pairs(da_t[:]), by_pairs(sums[b][:]), as_pairs(slope[b][:]), ALU.mult)
+            return da_t
+
+        def turn_pairs(da_t, number):
+            back = bank(number, [P, PAIRS, P])
+            for u in range(PAIRS):
+                nc.tensor.transpose(back[:, u, :], da_t[:].bitcast(F32)[:, u * P : (u + 1) * P], ident[:])
             return back
 
-        def finish_gradient(b0, backs):
-            da = ring.tile([P, len(backs) * P, PACK], BF16, name="da", align_bytes=64)
-            for k, back in enumerate(backs):
-                nc.vector.scalar_tensor_tensor(
-                    da[:, k * P : (k + 1) * P, :],
-                    back[:].rearrange("p d t -> p t d"),
-                    -1.0,
-                    slope_neg[:, (b0 + k) * P : (b0 + k + 1) * P, :],
-                    ALU.mult,
-                    ALU.mult,
-                )
-            return da
+        def lay_pairs(da, k, back):
+            words = da[:].bitcast(F32)[:, k * P * PAIRS : (k + 1) * P * PAIRS]
+            nc.scalar.copy(words.rearrange("p (t u) -> p t u", u=PAIRS), back[:].rearrange("p u t -> p t u"))
 
         def project(b0, nb, da, number, copy):
             da_w = ring.tile([P, nb * P], U32, name="da_w", align_bytes=64)
             da_s = ring.tile([P, nb * P], U8, name="da_s", align_bytes=64)
-            nc.vector.quantize_mx(
-                out=da_w[:].bitcast(FP8X4), scales=da_s[:], in_=da[:].rearrange("p t d -> p (t d)")
-            )
+            nc.vector.quantize_mx(out=da_w[:].bitcast(FP8X4), scales=da_s[:], in_=da[:])
             res_bank = bank(number, [P, nb * P])
             nc.tensor.matmul_mx(
                 out=res_bank[:],
@@ -304,50 +344,61 @@ def tile_moe_sub_silu_kernel(
             if k + 1 < len(FIRST_PARTS):
                 open0.append(early_pass(k + 1))
             late_pass(k, open0[k])
-        for j, numbers in ((1, (0, 1, 2)), (2, (3, 4, 0)), (3, (1, 2, 3))):
-            for pair, number in enumerate(numbers):
-                product(j, 2 * pair, number)
-
-        apart = [bank(number, [P, HT, P]) for number in (1, 2, 3)]
-
-        def turn_plain(j):
-            for r in range(TOP):
-                nc.tensor.transpose(apart[r][:, j, :], plains[j, r][:], ident[:])
-
-        weighed = [keep.tile([P, PACK, P], F32, name="weighed%d" % r, align_bytes=64) for r in range(TOP)]
-
-        def weigh(r):
-            nc.scalar.activation(
-                weighed[r][:],
-                apart[r][:].rearrange("t j (m d) -> t d (j m)", d=PACK),
-                ACT.Copy,
-                scale=gate_t[:, r : r + 1],
-            )
-
-        sort_out(0, 0, SHARED, combine(0, 0, SHARED, 0))
+        for pair, number in enumerate((3, 4, 5)):
+            product(1, pair, number)
         fetch_plain(0)
-        fetch_plain(1)
-        sort_out(1, 0, SHARED, combine(1, 0, SHARED, 4))
+        for pair in range(E // 2):
+            product(2, pair, pair)
+        for pair, number in enumerate((6, 7, 5)):
+            product(3, pair, number)
+        sums = [bank(b, [P, H]) for b in range(SHARED)]
+        apart = [bank(number, [P, HT, P]) for number in (5, 6, 7)]
+        for r in range(TOP):
+            combine(0, r, 0, SHARED)
         turn_plain(0)
+        for r in range(TOP):
+            combine(1, r, 0, SHARED)
+        fetch_plain(1)
         turn_plain(1)
-        sort_out(2, 0, 2, combine(2, 0, 2, 5))
-        fetch_plain(2)
-        turn_plain(2)
-        pair_sum = combine(3, 0, 2, 6)
-        fetch_plain(3)
-        sort_out(3, 0, 2, pair_sum)
-        turn_plain(3)
-        back_pair = [turn_back([dh_t[:, b, :, :]], number) for b, number in enumerate((0, 4))]
-        sort_out(2, LONE, 1, combine(2, LONE, 1, 7))
+
+        def late_plain(r):
+            for j in (2, 3):
+                fetch_plain(j, [r])
+                turn_plain(j, [r])
+
+        combine(2, 0, 0, SHARED)
+        combine(2, 1, 0, SHARED)
+        late_plain(0)
+        combine(2, 2, 0, SHARED)
+        late_plain(1)
+        combine(3, 0, 0, LONE)
+        late_plain(2)
+        combine(3, 1, 0, LONE)
+        back_last = bank(4, [P, PACK, P])
         weigh(0)
-        lone_sum = combine(3, LONE, 1, 1)
+        combine(3, 2, 0, LONE)
+        add_back(0, back_last)
+        combine(3, 0, LONE, 1)
         weigh(1)
+        combine(3, 1, LONE, 1)
+        combine(3, 2, LONE, 1)
+        add_back(1, back_last)
         weigh(2)
-        back_last = turn_back([tile[:] for tile in weighed], 5)
-        sort_out(3, LONE, 1, lone_sum)
-        back_lone = turn_back([dh_t[:, LONE, :, :]], 7)
-        project(0, 2, finish_gradient(0, back_pair), 6, on_scalar)
-        da_last = finish_gradient(SHARED, [back_last])
-        da_lone = finish_gradient(LONE, [back_lone])
-        project(SHARED, 1, da_last, 2, on_scalar)
-        project(LONE, 1, da_lone, 3, on_vector)
+        da_pair = keep.tile([P, LONE * H], BF16, name="da_pair", align_bytes=64)
+        da_lone = keep.tile([P, H], BF16, name="da_lone", align_bytes=64)
+        da_last = keep.tile([P, H], BF16, name="da_last", align_bytes=64)
+        lay_pairs(da_pair, 0, turn_pairs(slope_times_sums(0), 3))
+        add_back(2, back_last)
+        lay_pairs(da_pair, 1, turn_pairs(slope_times_sums(1), 5))
+        lay_pairs(da_lone, 0, turn_pairs(slope_times_sums(LONE), 6))
+        nc.vector.scalar_tensor_tensor(
+            da_last[:].rearrange("p (t d) -> p t d", d=PACK),
+            back_last[:].rearrange("p d t -> p t d"),
+            -1.0,
+            slope[SHARED][:].rearrange("p (t d) -> p t d", d=PACK),
+            ALU.mult,
+            ALU.mult,
+        )
+        project(0, LONE, da_pair, 0, on_scalar)
+        project(SHARED, 1, da_last, 1, on_scalar)
+        project(LONE, 1, da_lone, 2, on_vector)

@@ -77,15 +77,17 @@ def tile_moe_sub_silu_kernel(
         y = [keep.tile([P, SLOTS], F32, name="y%d" % j, align_bytes=64) for j in range(HT)]
         a_rows = placed.tile([P, HT, SHARED * P], F32, name="a_rows", align_bytes=64, offset=a_at)
         a_last = placed.tile([P, PACK, P], F32, name="a_last", align_bytes=64, offset=a_last_at)
-        sig_at = {0: a_at + 2 * H * 4, 1: a_at + H * 4, SHARED: a_at}
-        sig = [
-            placed.tile([P, H], F32, name="sig%d" % b, align_bytes=64, offset=sig_at[b])
-            if b in sig_at
-            else keep.tile([P, H], F32, name="sig%d" % b, align_bytes=64)
-            for b in range(BLOCKS)
-        ]
-        silu_neg = [keep.tile([P, H], F32, name="silu_neg%d" % b, align_bytes=64) for b in range(BLOCKS)]
-        slope = [keep.tile([P, H], F32, name="slope%d" % b, align_bytes=64) for b in range(BLOCKS)]
+        early = BLOCKS // 2
+        sig_late = placed.tile([P, early * H], F32, name="sig_late", align_bytes=64, offset=a_at)
+        silu_late = keep.tile([P, early * H], F32, name="silu_late", align_bytes=64)
+        slope_late = keep.tile([P, early * H], F32, name="slope_late", align_bytes=64)
+        sig_first = placed.tile([P, H], F32, name="sig_first", align_bytes=64, offset=a_at + early * H * 4)
+        sig_second = keep.tile([P, H], F32, name="sig_second", align_bytes=64)
+        sig = [sig_first[:], sig_second[:], sig_late[:, 0:H], sig_late[:, H:]]
+        silu_early = [keep.tile([P, H], F32, name="silu_early%d" % b, align_bytes=64) for b in range(early)]
+        silu_neg = [silu_early[0][:], silu_early[1][:], silu_late[:, 0:H], silu_late[:, H:]]
+        slope_early = [keep.tile([P, H], F32, name="slope_early%d" % b, align_bytes=64) for b in range(early)]
+        slope = [slope_early[0][:], slope_early[1][:], slope_late[:, 0:H], slope_late[:, H:]]
         ident = keep.tile([P, P], F32, name="ident")
 
         nc.gpsimd.memset(slot_s[:].bitcast(I32), 0)
@@ -106,8 +108,8 @@ def tile_moe_sub_silu_kernel(
 
         a_by_tile = a[:, 0 : SHARED * P].rearrange("(j p) t -> p j t", p=P)
         nc.sync.dma_start(a_rows[:, 0:2, :], a_by_tile[:, 0:2, :])
-        load_words(0)
         nc.sync.dma_start(a_rows[:, 2:HT, :], a_by_tile[:, 2:HT, :])
+        load_words(0)
         nc.sync.dma_start(a_last[:], a[:, SHARED * P : T].rearrange("(p d) t -> p d t", d=PACK))
         load_words(1)
 
@@ -171,10 +173,10 @@ def tile_moe_sub_silu_kernel(
 
         def activate(b, target, func, scale):
             if b < SHARED:
-                nc.scalar.activation(as_pairs(target[:]), by_pairs(a_turned[b][:]), func, scale=scale)
+                nc.scalar.activation(as_pairs(target), by_pairs(a_turned[b][:]), func, scale=scale)
             else:
                 nc.scalar.activation(
-                    target[:].rearrange("p (c i d) -> p c d i", i=PACK, d=PACK),
+                    target.rearrange("p (c i d) -> p c d i", i=PACK, d=PACK),
                     a_last[:].rearrange("p d (c i) -> p c d i", i=PACK),
                     func,
                     scale=scale,
@@ -182,26 +184,24 @@ def tile_moe_sub_silu_kernel(
 
         shifted = [
             placed.tile([P, H], F32, name="shifted%d" % b, align_bytes=64, offset=shifted_at + b * H * 4)
-            for b in range(SHARED)
+            for b in range(early)
         ]
         for b in range(BLOCKS):
             activate(b, silu_neg[b], ACT.Silu, -1.0)
-            if b < SHARED:
-                nc.gpsimd.tensor_scalar(shifted[b][:], silu_neg[b][:], -1.0, 1.0, ALU.mult, ALU.add)
+            if b < early:
+                nc.gpsimd.tensor_scalar(shifted[b][:], silu_neg[b], -1.0, 1.0, ALU.mult, ALU.add)
         for b in range(BLOCKS):
             activate(b, sig[b], ACT.Sigmoid, 1.0)
-            if b < SHARED:
-                nc.gpsimd.tensor_tensor(slope[b][:], shifted[b][:], sig[b][:], ALU.mult)
-        nc.vector.scalar_tensor_tensor(
-            slope[SHARED][:], silu_neg[SHARED][:], 1.0, sig[SHARED][:], ALU.subtract, ALU.mult
-        )
+            if b < early:
+                nc.gpsimd.tensor_tensor(slope[b], shifted[b][:], sig[b], ALU.mult)
+        nc.vector.scalar_tensor_tensor(slope_late[:], silu_late[:], 1.0, sig_late[:], ALU.subtract, ALU.mult)
 
         gate_t = placed.tile([P, TOP], F32, name="gate_t", align_bytes=64, offset=a_last_at + 2 * K)
         with nc.allow_non_contiguous_dma(reason="one gate value a token and partition"):
             nc.sync.dma_start(gate_t[:], gate[:, 0, SHARED * P : T].rearrange("r t -> t r"))
         w1_w = placed.tile([P, 2 * K], U8, name="w1_w", align_bytes=64, offset=a_last_at)
         nc.sync.dma_start(w1_w[:].bitcast(I32), w1t_words[0].bitcast(I32))
-        w1_s = placed.tile([P, K], U8, name="w1_s", align_bytes=64, offset=shifted_at + LONE * H * 4)
+        w1_s = placed.tile([P, K], U8, name="w1_s", align_bytes=64, offset=shifted_at + H * 4)
         nc.gpsimd.memset(w1_s[:].bitcast(I32), 0)
         for q in range(QUADS):
             nc.sync.dma_start(
@@ -242,8 +242,7 @@ def tile_moe_sub_silu_kernel(
             start, width = FIRST_PARTS[k]
             for u in range(0, width, C):
                 one_pass(0, y_bank[:, u : u + C], start + u, C, 1, False, u == width - C)
-            copy = nc.vector.tensor_copy if k == len(FIRST_PARTS) - 1 else nc.scalar.copy
-            copy(y[0][:, start : start + width], y_bank[:])
+            nc.scalar.copy(y[0][:, start : start + width], y_bank[:])
 
         def listed(r, b0, nb):
             return pos_sb[r][:, b0 * P // PER_COL : (b0 + nb) * P // PER_COL]
@@ -307,7 +306,18 @@ def tile_moe_sub_silu_kernel(
 
         def slope_times_sums(b):
             da_t = ring.tile([P, H], BF16, name="da_t", align_bytes=64)
-            nc.vector.tensor_tensor(as_pairs(da_t[:]), by_pairs(sums[b][:]), as_pairs(slope[b][:]), ALU.mult)
+            if b < early:
+                nc.vector.tensor_tensor(as_pairs(da_t[:]), by_pairs(sums[b][:]), as_pairs(slope[b]), ALU.mult)
+            else:
+                for u in range(PAIRS):
+                    nc.vector.scalar_tensor_tensor(
+                        as_pairs(da_t[:])[:, u],
+                        by_pairs(sums[b][:])[:, u],
+                        -1.0,
+                        as_pairs(slope[b])[:, u],
+                        ALU.mult,
+                        ALU.mult,
+                    )
             return da_t
 
         def turn_pairs(da_t, number):
@@ -395,7 +405,7 @@ def tile_moe_sub_silu_kernel(
             da_last[:].rearrange("p (t d) -> p t d", d=PACK),
             back_last[:].rearrange("p d t -> p t d"),
             -1.0,
-            slope[SHARED][:].rearrange("p (t d) -> p t d", d=PACK),
+            slope[SHARED].rearrange("p (t d) -> p t d", d=PACK),
             ALU.mult,
             ALU.mult,
         )

@@ -26,7 +26,7 @@ HT = H // P
 BLOCKS = T // P
 PER_COL = 16
 FIRST_PARTS = ((0, 512), (512, 512), (1024, 256), (1280, 256))
-WORD_PIECES = (((0, 768), (768, 768)), FIRST_PARTS)
+WORD_PIECES = (((0, 512), (512, 512), (1024, 512)), FIRST_PARTS)
 WORD_WINDOW = 1024
 BYTE_WINDOW = 2052
 ROWS_AT = 96
@@ -64,10 +64,11 @@ def tile_moe_sub_silu_kernel(
             keep.tile([P, E * PASSES, HALF_H], U8, name="w2_s0", align_bytes=64),
             placed.tile([P, E * PASSES, HALF_H], U8, name="w2_s1", align_bytes=64, offset=0),
         ]
-        w2_w = [
-            keep.tile([P, E * PASSES, 2 * HALF_H], U8, name="w2_w0", align_bytes=64),
-            placed.tile([P, E * PASSES, 2 * HALF_H], U8, name="w2_w1", align_bytes=64, offset=picked_at),
+        w2_early = [
+            keep.tile([P, 2 * PASSES, 2 * HALF_H], U8, name="w2_early%d" % pair, align_bytes=64)
+            for pair in range(E // 2)
         ]
+        w2_late = placed.tile([P, E * PASSES, 2 * HALF_H], U8, name="w2_late", align_bytes=64, offset=picked_at)
         slot_w = [
             [keep.tile([P, n], I32, name="slot_w%d_%d" % (s, first), align_bytes=64) for first, n in WORD_PIECES[s]]
             for s in range(PASSES)
@@ -99,60 +100,55 @@ def tile_moe_sub_silu_kernel(
 
         nc.sync.dma_start(dy_s[ROWS_AT:P, 0:T].bitcast(I32), dy_scales.rearrange("s b t -> b s t").bitcast(I32))
         nc.sync.dma_start(offs_sb[:], offs)
-        word_at = (T, 0)
-
-        def load_words(s):
-            nc.sync.dma_start(
-                dy_w[:, word_at[s] : word_at[s] + T], dy_words[s].rearrange("p t d -> p (t d)").bitcast(I32)
-            )
-
         a_by_tile = a[:, 0 : SHARED * P].rearrange("(j p) t -> p j t", p=P)
         nc.sync.dma_start(a_rows[:, 0:2, :], a_by_tile[:, 0:2, :])
         nc.sync.dma_start(a_rows[:, 2:HT, :], a_by_tile[:, 2:HT, :])
-        load_words(0)
+        nc.sync.dma_start(
+            dy_w[:, 0 : PASSES * T].rearrange("p (s t) -> p s t", s=PASSES),
+            dy_words.rearrange("s p t d -> p s (t d)").bitcast(I32),
+        )
         nc.sync.dma_start(a_last[:], a[:, SHARED * P : T].rearrange("(p d) t -> p d t", d=PACK))
-        load_words(1)
 
-        def load_w2_scales(h, quads):
+        def load_w2_scales(h):
             cols = slice(h * HALF_H, (h + 1) * HALF_H)
-            for q in quads:
-                nc.sync.dma_start(
-                    w2_s[h][32 * q : 32 * q + 4, :, :].bitcast(I32),
-                    w2t_scales[:, :, 4 * q : 4 * q + 4, cols].rearrange("e s b i -> b (e s) i").bitcast(I32),
-                )
+            by_row = w2t_scales[:, :, :, cols].rearrange("e s (q r) i -> r q (e s) i", r=4)
+            for r in range(4):
+                nc.sync.dma_start(w2_s[h][r:P:32, :, :].bitcast(I32), by_row[r].bitcast(I32))
 
-        def load_w2_words(h):
+        def load_w2_words(target, experts, h):
             cols = slice(2 * h * HALF_H, 2 * (h + 1) * HALF_H)
             nc.sync.dma_start(
-                w2_w[h][:].bitcast(I32), w2t_words[:, :, :, cols].rearrange("e s p b -> p (e s) b").bitcast(I32)
+                target[:].bitcast(I32), w2t_words[experts, :, :, cols].rearrange("e s p b -> p (e s) b").bitcast(I32)
             )
 
-        for r, pos in enumerate((pos1, pos2, pos3)):
-            nc.sync.dma_start(pos_sb[r][:], pos)
-        load_w2_scales(0, range(1))
-        load_w2_words(0)
-        load_w2_scales(0, range(1, QUADS))
+        load_w2_scales(0)
+        load_w2_words(w2_early[0], slice(0, 2), 0)
 
         def gather_words(s, i):
             first, n = WORD_PIECES[s][i]
             entries = offs_sb[:, first // PER_COL : (first + n) // PER_COL]
-            window = dy_w[:, word_at[s] : word_at[s] + WORD_WINDOW].bitcast(U32)
+            window = dy_w[:, s * T : s * T + WORD_WINDOW].bitcast(U32)
             nc.vector.tensor_copy(slot_w[s][i][:].bitcast(U32), window.indirect(entries))
 
         nc.vector.tensor_copy(picked_s[:], dy_s[:].indirect(offs_sb[:]))
-        for q in range(QUADS):
+        for q in (0, 2, 1, 3):
             nc.sync.dma_start(
                 slot_s[32 * q : 32 * q + 4, :, :].bitcast(I32),
                 picked_s[ROWS_AT + 8 * q : ROWS_AT + 8 * q + 8, :].bitcast(I32),
             )
+        for pair in range(1, E // 2):
+            load_w2_words(w2_early[pair], slice(2 * pair, 2 * pair + 2), 0)
+        for r, pos in enumerate((pos1, pos2, pos3)):
+            nc.sync.dma_start(pos_sb[r][:], pos)
         gate_sb = placed.tile([P, TOP, SHARED * P], F32, name="gate_sb", align_bytes=64, offset=gate_at)
         nc.sync.dma_start(gate_sb[:], gate[:, :, 0 : SHARED * P].rearrange("r p t -> p r t"))
         nc.gpsimd.memset(w2_s[1][:].bitcast(I32), 0)
-        load_w2_scales(1, range(QUADS))
-        load_w2_words(1)
-        for s in range(PASSES):
-            for i in range(len(WORD_PIECES[s])):
-                gather_words(s, i)
+        load_w2_scales(1)
+        load_w2_words(w2_late, slice(0, E), 1)
+        for pair in range(E // 2):
+            for s in range(PASSES):
+                gather_words(s, pair)
+        gather_words(1, E // 2)
 
         banks_used = []
 
@@ -213,9 +209,10 @@ def tile_moe_sub_silu_kernel(
             e = slot // C
             piece = max(i for i, (first, n) in enumerate(WORD_PIECES[s]) if first <= slot)
             at = slot - WORD_PIECES[s][piece][0]
+            words = w2_late[:, e * PASSES + s, :] if h else w2_early[e // 2][:, (e % 2) * PASSES + s, :]
             nc.tensor.matmul_mx(
                 out=target,
-                lhsT=w2_w[h][:, e * PASSES + s, 2 * col : 2 * (col + P)].bitcast(FP4X4),
+                lhsT=words[:, 2 * col : 2 * (col + P)].bitcast(FP4X4),
                 lhsT_scale=w2_s[h][:, e * PASSES + s, col : col + P],
                 rhs=slot_w[s][piece][:, at : at + width].bitcast(FP8X4),
                 rhs_scale=slot_s[:, s, slot : slot + width],
@@ -227,8 +224,8 @@ def tile_moe_sub_silu_kernel(
             first = 2 * pair * C
             y_bank = bank(number, [P, 2 * C])
             for u in range(0, 2 * C, C):
-                for s in reversed(range(PASSES)):
-                    one_pass(j, y_bank[:, u : u + C], first + u, C, s, s == PASSES - 1, s == 0)
+                for s in range(PASSES):
+                    one_pass(j, y_bank[:, u : u + C], first + u, C, s, s == 0, s == PASSES - 1)
             nc.scalar.copy(y[j][:, first : first + 2 * C], y_bank[:])
 
         def early_pass(k):
@@ -349,13 +346,14 @@ def tile_moe_sub_silu_kernel(
             nc.sync.dma_start(out[:, b0 * P : (b0 + nb) * P], res[:])
 
         on_scalar, on_vector = nc.scalar.copy, nc.vector.tensor_copy
-        open0 = [early_pass(0)]
-        for k in range(len(FIRST_PARTS)):
-            if k + 1 < len(FIRST_PARTS):
-                open0.append(early_pass(k + 1))
-            late_pass(k, open0[k])
-        for pair, number in enumerate((3, 4, 5)):
-            product(1, pair, number)
+        product(0, 0, 4)
+        product(1, 0, 3)
+        product(0, 1, 5)
+        last_banks = [early_pass(k) for k in (2, 3)]
+        for k, y_bank in zip((2, 3), last_banks):
+            late_pass(k, y_bank)
+        product(1, 1, 4)
+        product(1, 2, 5)
         fetch_plain(0)
         for pair in range(E // 2):
             product(2, pair, pair)

@@ -25,9 +25,7 @@ QUADS = 4
 HT = H // P
 BLOCKS = T // P
 PER_COL = 16
-FIRST_PARTS = ((0, 512), (512, 512), (1024, 256), (1280, 256))
-WORD_PIECES = (((0, 512), (512, 512), (1024, 512)), FIRST_PARTS)
-WORD_WINDOW = 1024
+WORD_GATHERS = ((0, 0, 768), (1, 0, 384), (1, 384, 384), (0, 768, 768), (1, 768, 256), (1, 1024, 256), (1, 1280, 256))
 BYTE_WINDOW = 2052
 ROWS_AT = 96
 HALF_H = H // 2
@@ -49,54 +47,47 @@ def tile_moe_sub_silu_kernel(
         psum = ctx.enter_context(tc.psum_pool(name="psum", bufs=1))
 
         plane_bytes = E * PASSES * HALF_H
-        dy_s_at = plane_bytes - T
-        gate_at = plane_bytes + 64
-        dy_w_at = gate_at + TOP * SHARED * P * 4
-        shifted_at = dy_w_at + (T + WORD_WINDOW) * 4
-        a_at = shifted_at + SHARED * H * 4
-        picked_at = a_at + SHARED * H * 4
-        a_last_at = picked_at + 2 * plane_bytes
+        a_at = 0
+        tail_at = BLOCKS * H * 4
         offs_sb = keep.tile([P, SLOTS // PER_COL], U16, name="offs_sb")
         pos_sb = [keep.tile([P, T // PER_COL], U16, name="pos_sb%d" % r) for r in range(TOP)]
-        dy_s = placed.tile([P, BYTE_WINDOW], U8, name="dy_s", align_bytes=64, offset=dy_s_at)
-        dy_w = placed.tile([P, T + WORD_WINDOW], I32, name="dy_w", align_bytes=64, offset=dy_w_at)
-        w2_s = [
-            keep.tile([P, E * PASSES, HALF_H], U8, name="w2_s0", align_bytes=64),
-            placed.tile([P, E * PASSES, HALF_H], U8, name="w2_s1", align_bytes=64, offset=0),
-        ]
+        dy_s = keep.tile([P, BYTE_WINDOW], U8, name="dy_s", align_bytes=64)
+        dy_w = keep.tile([P, PASSES * T], I32, name="dy_w", align_bytes=64)
+        w2_planes = [keep.tile([P, plane_bytes + 4], U8, name="w2_plane%d" % h, align_bytes=64) for h in range(2)]
+        w2_s = [plane[:, 0:plane_bytes].rearrange("p (g i) -> p g i", i=HALF_H) for plane in w2_planes]
         w2_early = [
             keep.tile([P, 2 * PASSES, 2 * HALF_H], U8, name="w2_early%d" % pair, align_bytes=64)
             for pair in range(E // 2)
         ]
-        w2_late = placed.tile([P, E * PASSES, 2 * HALF_H], U8, name="w2_late", align_bytes=64, offset=picked_at)
-        slot_w = [
-            [keep.tile([P, n], I32, name="slot_w%d_%d" % (s, first), align_bytes=64) for first, n in WORD_PIECES[s]]
-            for s in range(PASSES)
-        ]
-        picked_s = placed.tile([P, SLOTS], U8, name="picked_s", align_bytes=64, offset=picked_at)
+        w2_late = keep.tile([P, E * PASSES, 2 * HALF_H], U8, name="w2_late", align_bytes=64)
+        slot_w = [keep.tile([P, SLOTS], I32, name="slot_w%d" % s, align_bytes=64) for s in range(PASSES)]
+        picked_s = keep.tile([P, SLOTS], U8, name="picked_s", align_bytes=64)
         slot_s = keep.tile([P, PASSES, SLOTS], U8, name="slot_s", align_bytes=64)
         y = [keep.tile([P, SLOTS], F32, name="y%d" % j, align_bytes=64) for j in range(HT)]
         a_rows = placed.tile([P, HT, SHARED * P], F32, name="a_rows", align_bytes=64, offset=a_at)
-        a_last = placed.tile([P, PACK, P], F32, name="a_last", align_bytes=64, offset=a_last_at)
-        early = BLOCKS // 2
-        sig_late = placed.tile([P, early * H], F32, name="sig_late", align_bytes=64, offset=a_at)
-        silu_late = keep.tile([P, early * H], F32, name="silu_late", align_bytes=64)
-        slope_late = keep.tile([P, early * H], F32, name="slope_late", align_bytes=64)
-        sig_first = placed.tile([P, H], F32, name="sig_first", align_bytes=64, offset=a_at + early * H * 4)
-        sig_second = keep.tile([P, H], F32, name="sig_second", align_bytes=64)
-        sig = [sig_first[:], sig_second[:], sig_late[:, 0:H], sig_late[:, H:]]
-        silu_early = [keep.tile([P, H], F32, name="silu_early%d" % b, align_bytes=64) for b in range(early)]
-        silu_neg = [silu_early[0][:], silu_early[1][:], silu_late[:, 0:H], silu_late[:, H:]]
-        slope_early = [keep.tile([P, H], F32, name="slope_early%d" % b, align_bytes=64) for b in range(early)]
-        slope = [slope_early[0][:], slope_early[1][:], slope_late[:, 0:H], slope_late[:, H:]]
+        a_last = keep.tile([P, PACK, P], F32, name="a_last", align_bytes=64)
+        sig_last = placed.tile([P, H], F32, name="sig_last", align_bytes=64, offset=a_at)
+        sig_shared = placed.tile([P, SHARED * H], F32, name="sig_shared", align_bytes=64, offset=a_at + H * 4)
+        silu_shared = keep.tile([P, SHARED * H], F32, name="silu_shared", align_bytes=64)
+        silu_last = keep.tile([P, H], F32, name="silu_last", align_bytes=64)
+        slope_shared = keep.tile([P, SHARED * H], F32, name="slope_shared", align_bytes=64)
+        slope_last = keep.tile([P, H], F32, name="slope_last", align_bytes=64)
+
+        def by_block(shared, last):
+            return [shared[:, b * H : (b + 1) * H] for b in range(SHARED)] + [last[:]]
+
+        sig, silu_neg = by_block(sig_shared, sig_last), by_block(silu_shared, silu_last)
+        slope = by_block(slope_shared, slope_last)
+        w1_s = keep.tile([P, K], U8, name="w1_s", align_bytes=64)
         ident = keep.tile([P, P], F32, name="ident")
 
+        nc.gpsimd.memset(w2_planes[0][:].bitcast(I32), 0)
+        make_identity(nc, ident[:])
         nc.gpsimd.memset(slot_s[:].bitcast(I32), 0)
-        nc.gpsimd.memset(w2_s[0][:].bitcast(I32), 0)
+        nc.gpsimd.memset(w1_s[:].bitcast(I32), 0)
         nc.vector.memset(dy_s[:, T:].bitcast(I32), 0)
         nc.vector.memset(dy_s[0:ROWS_AT, 0 : T + 4].bitcast(I32), 0)
-        make_identity(nc, ident[:])
-        nc.gpsimd.memset(dy_w[:, PASSES * T :], 0)
+        nc.vector.memset(w2_planes[1][:].bitcast(I32), 0)
 
         nc.sync.dma_start(dy_s[ROWS_AT:P, 0:T].bitcast(I32), dy_scales.rearrange("s b t -> b s t").bitcast(I32))
         nc.sync.dma_start(offs_sb[:], offs)
@@ -104,7 +95,7 @@ def tile_moe_sub_silu_kernel(
         nc.sync.dma_start(a_rows[:, 0:2, :], a_by_tile[:, 0:2, :])
         nc.sync.dma_start(a_rows[:, 2:HT, :], a_by_tile[:, 2:HT, :])
         nc.sync.dma_start(
-            dy_w[:, 0 : PASSES * T].rearrange("p (s t) -> p s t", s=PASSES),
+            dy_w[:].rearrange("p (s t) -> p s t", s=PASSES),
             dy_words.rearrange("s p t d -> p s (t d)").bitcast(I32),
         )
         nc.sync.dma_start(a_last[:], a[:, SHARED * P : T].rearrange("(p d) t -> p d t", d=PACK))
@@ -124,12 +115,6 @@ def tile_moe_sub_silu_kernel(
         load_w2_scales(0)
         load_w2_words(w2_early[0], slice(0, 2), 0)
 
-        def gather_words(s, i):
-            first, n = WORD_PIECES[s][i]
-            entries = offs_sb[:, first // PER_COL : (first + n) // PER_COL]
-            window = dy_w[:, s * T : s * T + WORD_WINDOW].bitcast(U32)
-            nc.vector.tensor_copy(slot_w[s][i][:].bitcast(U32), window.indirect(entries))
-
         nc.vector.tensor_copy(picked_s[:], dy_s[:].indirect(offs_sb[:]))
         for q in (0, 2, 1, 3):
             nc.sync.dma_start(
@@ -140,15 +125,14 @@ def tile_moe_sub_silu_kernel(
             load_w2_words(w2_early[pair], slice(2 * pair, 2 * pair + 2), 0)
         for r, pos in enumerate((pos1, pos2, pos3)):
             nc.sync.dma_start(pos_sb[r][:], pos)
-        gate_sb = placed.tile([P, TOP, SHARED * P], F32, name="gate_sb", align_bytes=64, offset=gate_at)
+        gate_sb = placed.tile([P, TOP, SHARED * P], F32, name="gate_sb", align_bytes=64, offset=tail_at)
         nc.sync.dma_start(gate_sb[:], gate[:, :, 0 : SHARED * P].rearrange("r p t -> p r t"))
-        nc.gpsimd.memset(w2_s[1][:].bitcast(I32), 0)
         load_w2_scales(1)
         load_w2_words(w2_late, slice(0, E), 1)
-        for pair in range(E // 2):
-            for s in range(PASSES):
-                gather_words(s, pair)
-        gather_words(1, E // 2)
+        for s, first, n in WORD_GATHERS:
+            entries = offs_sb[:, first // PER_COL : (first + n) // PER_COL]
+            window = dy_w[:, s * T :].bitcast(U32)
+            nc.vector.tensor_copy(slot_w[s][:, first : first + n].bitcast(U32), window.indirect(entries))
 
         banks_used = []
 
@@ -178,27 +162,17 @@ def tile_moe_sub_silu_kernel(
                     scale=scale,
                 )
 
-        shifted = [
-            placed.tile([P, H], F32, name="shifted%d" % b, align_bytes=64, offset=shifted_at + b * H * 4)
-            for b in range(early)
-        ]
         for b in range(BLOCKS):
             activate(b, silu_neg[b], ACT.Silu, -1.0)
-            if b < early:
-                nc.gpsimd.tensor_scalar(shifted[b][:], silu_neg[b], -1.0, 1.0, ALU.mult, ALU.add)
         for b in range(BLOCKS):
             activate(b, sig[b], ACT.Sigmoid, 1.0)
-            if b < early:
-                nc.gpsimd.tensor_tensor(slope[b], shifted[b][:], sig[b], ALU.mult)
-        nc.vector.scalar_tensor_tensor(slope_late[:], silu_late[:], 1.0, sig_late[:], ALU.subtract, ALU.mult)
+        nc.vector.scalar_tensor_tensor(slope_shared[:], silu_shared[:], 1.0, sig_shared[:], ALU.subtract, ALU.mult)
 
-        gate_t = placed.tile([P, TOP], F32, name="gate_t", align_bytes=64, offset=a_last_at + 2 * K)
+        gate_t = keep.tile([P, TOP], F32, name="gate_t", align_bytes=64)
         with nc.allow_non_contiguous_dma(reason="one gate value a token and partition"):
             nc.sync.dma_start(gate_t[:], gate[:, 0, SHARED * P : T].rearrange("r t -> t r"))
-        w1_w = placed.tile([P, 2 * K], U8, name="w1_w", align_bytes=64, offset=a_last_at)
+        w1_w = keep.tile([P, 2 * K], U8, name="w1_w", align_bytes=64)
         nc.sync.dma_start(w1_w[:].bitcast(I32), w1t_words[0].bitcast(I32))
-        w1_s = placed.tile([P, K], U8, name="w1_s", align_bytes=64, offset=shifted_at + H * 4)
-        nc.gpsimd.memset(w1_s[:].bitcast(I32), 0)
         for q in range(QUADS):
             nc.sync.dma_start(
                 w1_s[32 * q : 32 * q + 4, :].bitcast(I32), w1t_scales[0, 4 * q : 4 * q + 4, :].bitcast(I32)
@@ -207,39 +181,29 @@ def tile_moe_sub_silu_kernel(
         def one_pass(j, target, slot, width, s, opens, closes):
             h, col = divmod(j * P, HALF_H)
             e = slot // C
-            piece = max(i for i, (first, n) in enumerate(WORD_PIECES[s]) if first <= slot)
-            at = slot - WORD_PIECES[s][piece][0]
             words = w2_late[:, e * PASSES + s, :] if h else w2_early[e // 2][:, (e % 2) * PASSES + s, :]
             nc.tensor.matmul_mx(
                 out=target,
                 lhsT=words[:, 2 * col : 2 * (col + P)].bitcast(FP4X4),
                 lhsT_scale=w2_s[h][:, e * PASSES + s, col : col + P],
-                rhs=slot_w[s][piece][:, at : at + width].bitcast(FP8X4),
+                rhs=slot_w[s][:, slot : slot + width].bitcast(FP8X4),
                 rhs_scale=slot_s[:, s, slot : slot + width],
                 start=opens,
                 stop=closes,
             )
 
-        def product(j, pair, number):
-            first = 2 * pair * C
-            y_bank = bank(number, [P, 2 * C])
-            for u in range(0, 2 * C, C):
+        def multiply(j, first, count, number):
+            y_bank = bank(number, [P, count * C])
+            for u in range(count):
                 for s in range(PASSES):
-                    one_pass(j, y_bank[:, u : u + C], first + u, C, s, s == 0, s == PASSES - 1)
-            nc.scalar.copy(y[j][:, first : first + 2 * C], y_bank[:])
-
-        def early_pass(k):
-            start, width = FIRST_PARTS[k]
-            y_bank = bank(QUADS + k, [P, width])
-            for u in range(0, width, C):
-                one_pass(0, y_bank[:, u : u + C], start + u, C, 0, u == 0, False)
+                    one_pass(j, y_bank[:, u * C : (u + 1) * C], (first + u) * C, C, s, s == 0, s == PASSES - 1)
             return y_bank
 
-        def late_pass(k, y_bank):
-            start, width = FIRST_PARTS[k]
-            for u in range(0, width, C):
-                one_pass(0, y_bank[:, u : u + C], start + u, C, 1, False, u == width - C)
-            nc.scalar.copy(y[0][:, start : start + width], y_bank[:])
+        def fetch_sums(j, first, count, y_bank):
+            nc.scalar.copy(y[j][:, first * C : (first + count) * C], y_bank[:])
+
+        def product(j, pair, number):
+            fetch_sums(j, 2 * pair, 2, multiply(j, 2 * pair, 2, number))
 
         def listed(r, b0, nb):
             return pos_sb[r][:, b0 * P // PER_COL : (b0 + nb) * P // PER_COL]
@@ -303,18 +267,15 @@ def tile_moe_sub_silu_kernel(
 
         def slope_times_sums(b):
             da_t = ring.tile([P, H], BF16, name="da_t", align_bytes=64)
-            if b < early:
-                nc.vector.tensor_tensor(as_pairs(da_t[:]), by_pairs(sums[b][:]), as_pairs(slope[b]), ALU.mult)
-            else:
-                for u in range(PAIRS):
-                    nc.vector.scalar_tensor_tensor(
-                        as_pairs(da_t[:])[:, u],
-                        by_pairs(sums[b][:])[:, u],
-                        -1.0,
-                        as_pairs(slope[b])[:, u],
-                        ALU.mult,
-                        ALU.mult,
-                    )
+            for u in range(PAIRS):
+                nc.vector.scalar_tensor_tensor(
+                    as_pairs(da_t[:])[:, u],
+                    by_pairs(sums[b][:])[:, u],
+                    -1.0,
+                    as_pairs(slope[b])[:, u],
+                    ALU.mult,
+                    ALU.mult,
+                )
             return da_t
 
         def turn_pairs(da_t, number):
@@ -347,11 +308,20 @@ def tile_moe_sub_silu_kernel(
 
         on_scalar, on_vector = nc.scalar.copy, nc.vector.tensor_copy
         product(0, 0, 4)
-        product(1, 0, 3)
-        product(0, 1, 5)
-        last_banks = [early_pass(k) for k in (2, 3)]
-        for k, y_bank in zip((2, 3), last_banks):
-            late_pass(k, y_bank)
+        ahead = multiply(1, 0, 2, 3)
+        opened = [bank(number, [P, C]) for number in (6, 7)]
+        third = bank(5, [P, 2 * C])
+        for s in range(PASSES):
+            one_pass(0, third[:, 0:C], 2 * C, C, s, s == 0, False)
+        one_pass(0, third[:, C:], 3 * C, C, 0, False, False)
+        for u in range(2):
+            one_pass(0, opened[u][:], (4 + u) * C, C, 0, True, False)
+        one_pass(0, third[:, C:], 3 * C, C, 1, False, True)
+        fetch_sums(0, 2, 2, third)
+        for u in range(2):
+            one_pass(0, opened[u][:], (4 + u) * C, C, 1, False, True)
+            fetch_sums(0, 4 + u, 1, opened[u])
+        fetch_sums(1, 0, 2, ahead)
         product(1, 1, 4)
         product(1, 2, 5)
         fetch_plain(0)
@@ -392,6 +362,9 @@ def tile_moe_sub_silu_kernel(
         combine(3, 2, LONE, 1)
         add_back(1, back_last)
         weigh(2)
+        shifted = placed.tile([P, H], F32, name="shifted", align_bytes=64, offset=tail_at)
+        nc.gpsimd.tensor_scalar(shifted[:], silu_last[:], -1.0, 1.0, ALU.mult, ALU.add)
+        nc.gpsimd.tensor_tensor(slope_last[:], shifted[:], sig_last[:], ALU.mult)
         da_pair = keep.tile([P, LONE * H], BF16, name="da_pair", align_bytes=64)
         da_lone = keep.tile([P, H], BF16, name="da_lone", align_bytes=64)
         da_last = keep.tile([P, H], BF16, name="da_last", align_bytes=64)
@@ -399,12 +372,10 @@ def tile_moe_sub_silu_kernel(
         add_back(2, back_last)
         lay_pairs(da_pair, 1, turn_pairs(slope_times_sums(1), 5))
         lay_pairs(da_lone, 0, turn_pairs(slope_times_sums(LONE), 6))
-        nc.vector.scalar_tensor_tensor(
+        nc.vector.tensor_tensor(
             da_last[:].rearrange("p (t d) -> p t d", d=PACK),
             back_last[:].rearrange("p d t -> p t d"),
-            -1.0,
-            slope[SHARED].rearrange("p (t d) -> p t d", d=PACK),
-            ALU.mult,
+            slope_last[:].rearrange("p (t d) -> p t d", d=PACK),
             ALU.mult,
         )
         project(0, LONE, da_pair, 0, on_scalar)

@@ -25,7 +25,8 @@ QUADS = 4
 HT = H // P
 BLOCKS = T // P
 PER_COL = 16
-WORD_GATHERS = ((0, 0, 768), (1, 0, 384), (1, 384, 384), (0, 768, 768), (1, 768, 256), (1, 1024, 256), (1, 1280, 256))
+FIRST_PARTS = ((0, 2), (2, 2), (4, 1), (5, 1))
+NARROW = 384
 BYTE_WINDOW = 2052
 ROWS_AT = 96
 HALF_H = H // 2
@@ -71,7 +72,7 @@ def tile_moe_sub_silu_kernel(
         silu_shared = keep.tile([P, SHARED * H], F32, name="silu_shared", align_bytes=64)
         silu_last = keep.tile([P, H], F32, name="silu_last", align_bytes=64)
         slope_shared = keep.tile([P, SHARED * H], F32, name="slope_shared", align_bytes=64)
-        slope_last = keep.tile([P, H], F32, name="slope_last", align_bytes=64)
+        slope_last = placed.tile([P, H], F32, name="slope_last", align_bytes=64, offset=tail_at)
 
         def by_block(shared, last):
             return [shared[:, b * H : (b + 1) * H] for b in range(SHARED)] + [last[:]]
@@ -81,8 +82,10 @@ def tile_moe_sub_silu_kernel(
         w1_s = keep.tile([P, K], U8, name="w1_s", align_bytes=64)
         ident = keep.tile([P, P], F32, name="ident")
 
-        nc.gpsimd.memset(w2_planes[0][:].bitcast(I32), 0)
+        gate_rows = keep.tile([P, TOP, P], F32, name="gate_rows", align_bytes=64)
+        nc.gpsimd.memset(gate_rows[:], 0.0)
         make_identity(nc, ident[:])
+        nc.gpsimd.memset(w2_planes[0][:].bitcast(I32), 0)
         nc.gpsimd.memset(slot_s[:].bitcast(I32), 0)
         nc.gpsimd.memset(w1_s[:].bitcast(I32), 0)
         nc.vector.memset(dy_s[:, T:].bitcast(I32), 0)
@@ -91,14 +94,20 @@ def tile_moe_sub_silu_kernel(
 
         nc.sync.dma_start(dy_s[ROWS_AT:P, 0:T].bitcast(I32), dy_scales.rearrange("s b t -> b s t").bitcast(I32))
         nc.sync.dma_start(offs_sb[:], offs)
+        word_at = (T, 0)
+
+        def load_words(s):
+            nc.sync.dma_start(
+                dy_w[:, word_at[s] : word_at[s] + T], dy_words[s].rearrange("p t d -> p (t d)").bitcast(I32)
+            )
+
+        nc.sync.dma_start(a_last[:], a[:, SHARED * P : T].rearrange("(p d) t -> p d t", d=PACK))
+        nc.sync.dma_start(gate_rows[0:BLOCKS, :, :], gate[:, 0, :].rearrange("r (b t) -> b r t", t=P))
         a_by_tile = a[:, 0 : SHARED * P].rearrange("(j p) t -> p j t", p=P)
         nc.sync.dma_start(a_rows[:, 0:2, :], a_by_tile[:, 0:2, :])
+        load_words(0)
         nc.sync.dma_start(a_rows[:, 2:HT, :], a_by_tile[:, 2:HT, :])
-        nc.sync.dma_start(
-            dy_w[:].rearrange("p (s t) -> p s t", s=PASSES),
-            dy_words.rearrange("s p t d -> p s (t d)").bitcast(I32),
-        )
-        nc.sync.dma_start(a_last[:], a[:, SHARED * P : T].rearrange("(p d) t -> p d t", d=PACK))
+        load_words(1)
 
         def load_w2_scales(h):
             cols = slice(h * HALF_H, (h + 1) * HALF_H)
@@ -126,13 +135,18 @@ def tile_moe_sub_silu_kernel(
         for r, pos in enumerate((pos1, pos2, pos3)):
             nc.sync.dma_start(pos_sb[r][:], pos)
         gate_sb = placed.tile([P, TOP, SHARED * P], F32, name="gate_sb", align_bytes=64, offset=tail_at)
-        nc.sync.dma_start(gate_sb[:], gate[:, :, 0 : SHARED * P].rearrange("r p t -> p r t"))
         load_w2_scales(1)
         load_w2_words(w2_late, slice(0, E), 1)
-        for s, first, n in WORD_GATHERS:
+
+        def gather_words(s, first, n):
             entries = offs_sb[:, first // PER_COL : (first + n) // PER_COL]
-            window = dy_w[:, s * T :].bitcast(U32)
+            window = dy_w[:, word_at[s] :].bitcast(U32)
             nc.vector.tensor_copy(slot_w[s][:, first : first + n].bitcast(U32), window.indirect(entries))
+
+        for first in range(0, SLOTS, NARROW):
+            gather_words(0, first, NARROW)
+        for first, count in FIRST_PARTS:
+            gather_words(1, first * C, count * C)
 
         banks_used = []
 
@@ -146,11 +160,6 @@ def tile_moe_sub_silu_kernel(
         def as_pairs(ap):
             return ap.rearrange("t (u p e) -> t u p e", u=PAIRS, e=2)
 
-        a_turned = [bank(b, [P, H]) for b in range(SHARED)]
-        for b, j in [(b, j) for half in (0, 2) for b in range(SHARED) for j in (half, half + 1)]:
-            if True:
-                nc.tensor.transpose(a_turned[b][:, j * P : (j + 1) * P], a_rows[:, j, b * P : (b + 1) * P], ident[:])
-
         def activate(b, target, func, scale):
             if b < SHARED:
                 nc.scalar.activation(as_pairs(target), by_pairs(a_turned[b][:]), func, scale=scale)
@@ -162,15 +171,34 @@ def tile_moe_sub_silu_kernel(
                     scale=scale,
                 )
 
-        for b in range(BLOCKS):
+        a_turned = [bank(b, [P, H]) for b in range(SHARED)]
+        activate(SHARED, silu_neg[SHARED], ACT.Silu, -1.0)
+        shifted = keep.tile([P, H], F32, name="shifted", align_bytes=64)
+        nc.scalar.activation(shifted[:], silu_last[:], ACT.Copy, scale=-1.0, bias=1.0)
+        gate_turned = bank(7, [P, TOP, P])
+        for r in range(TOP):
+            nc.tensor.transpose(gate_turned[:, r, :], gate_rows[:, r, :], ident[:])
+        gate_t = keep.tile([P, TOP, BLOCKS], F32, name="gate_t", align_bytes=64)
+        nc.scalar.copy(gate_t[:], gate_turned[:, :, 0:BLOCKS])
+        for r in range(TOP):
+            spread = bank(QUADS + r, [P, SHARED, P])
+            for b in range(SHARED):
+                nc.tensor.transpose(spread[:, b, :], gate_t[:, r, b : b + 1].to_broadcast([P, P]), ident[:])
+            nc.scalar.copy(gate_sb[:, r, :], spread[:].rearrange("p b t -> p (b t)"))
+
+        for half in range(0, HT, 2):
+            for b in range(SHARED):
+                for j in (half, half + 1):
+                    nc.tensor.transpose(
+                        a_turned[b][:, j * P : (j + 1) * P], a_rows[:, j, b * P : (b + 1) * P], ident[:]
+                    )
+
+        for b in range(SHARED):
             activate(b, silu_neg[b], ACT.Silu, -1.0)
         for b in range(BLOCKS):
             activate(b, sig[b], ACT.Sigmoid, 1.0)
         nc.vector.scalar_tensor_tensor(slope_shared[:], silu_shared[:], 1.0, sig_shared[:], ALU.subtract, ALU.mult)
 
-        gate_t = keep.tile([P, TOP], F32, name="gate_t", align_bytes=64)
-        with nc.allow_non_contiguous_dma(reason="one gate value a token and partition"):
-            nc.sync.dma_start(gate_t[:], gate[:, 0, SHARED * P : T].rearrange("r t -> t r"))
         w1_w = keep.tile([P, 2 * K], U8, name="w1_w", align_bytes=64)
         nc.sync.dma_start(w1_w[:].bitcast(I32), w1t_words[0].bitcast(I32))
         for q in range(QUADS):
@@ -251,7 +279,7 @@ def tile_moe_sub_silu_kernel(
                 weighed[r][:],
                 apart[r][:].rearrange("t j (m d) -> t d (j m)", d=PACK),
                 ACT.Copy,
-                scale=gate_t[:, r : r + 1],
+                scale=gate_t[:, r, SHARED : SHARED + 1],
             )
 
         def add_back(r, back):
@@ -307,20 +335,24 @@ def tile_moe_sub_silu_kernel(
             nc.sync.dma_start(out[:, b0 * P : (b0 + nb) * P], res[:])
 
         on_scalar, on_vector = nc.scalar.copy, nc.vector.tensor_copy
-        product(0, 0, 4)
+        opened = [bank(QUADS + k, [P, count * C]) for k, (first, count) in enumerate(FIRST_PARTS)]
+
+        def first_tile(k, s):
+            first, count = FIRST_PARTS[k]
+            for u in range(count):
+                target = opened[k][:, u * C : (u + 1) * C]
+                one_pass(0, target, (first + u) * C, C, s, s == 0 and u == 0, s == PASSES - 1 and u == count - 1)
+            if s == PASSES - 1:
+                fetch_sums(0, first, count, opened[k])
+
+        first_tile(0, 0)
+        first_tile(1, 0)
+        first_tile(0, 1)
         ahead = multiply(1, 0, 2, 3)
-        opened = [bank(number, [P, C]) for number in (6, 7)]
-        third = bank(5, [P, 2 * C])
-        for s in range(PASSES):
-            one_pass(0, third[:, 0:C], 2 * C, C, s, s == 0, False)
-        one_pass(0, third[:, C:], 3 * C, C, 0, False, False)
-        for u in range(2):
-            one_pass(0, opened[u][:], (4 + u) * C, C, 0, True, False)
-        one_pass(0, third[:, C:], 3 * C, C, 1, False, True)
-        fetch_sums(0, 2, 2, third)
-        for u in range(2):
-            one_pass(0, opened[u][:], (4 + u) * C, C, 1, False, True)
-            fetch_sums(0, 4 + u, 1, opened[u])
+        for k in range(2, len(FIRST_PARTS)):
+            first_tile(k, 0)
+        for k in range(1, len(FIRST_PARTS)):
+            first_tile(k, 1)
         fetch_sums(1, 0, 2, ahead)
         product(1, 1, 4)
         product(1, 2, 5)
@@ -362,8 +394,6 @@ def tile_moe_sub_silu_kernel(
         combine(3, 2, LONE, 1)
         add_back(1, back_last)
         weigh(2)
-        shifted = placed.tile([P, H], F32, name="shifted", align_bytes=64, offset=tail_at)
-        nc.gpsimd.tensor_scalar(shifted[:], silu_last[:], -1.0, 1.0, ALU.mult, ALU.add)
         nc.gpsimd.tensor_tensor(slope_last[:], shifted[:], sig_last[:], ALU.mult)
         da_pair = keep.tile([P, LONE * H], BF16, name="da_pair", align_bytes=64)
         da_lone = keep.tile([P, H], BF16, name="da_lone", align_bytes=64)

@@ -26,7 +26,8 @@ HT = H // P
 BLOCKS = T // P
 PER_COL = 16
 FIRST_PARTS = ((0, 2), (2, 2), (4, 1), (5, 1))
-NARROW = 384
+WIDE = 768
+WORD_WINDOW = 1024
 BYTE_WINDOW = 2052
 ROWS_AT = 96
 HALF_H = H // 2
@@ -53,7 +54,7 @@ def tile_moe_sub_silu_kernel(
         offs_sb = keep.tile([P, SLOTS // PER_COL], U16, name="offs_sb")
         pos_sb = [keep.tile([P, T // PER_COL], U16, name="pos_sb%d" % r) for r in range(TOP)]
         dy_s = keep.tile([P, BYTE_WINDOW], U8, name="dy_s", align_bytes=64)
-        dy_w = keep.tile([P, PASSES * T], I32, name="dy_w", align_bytes=64)
+        dy_w = keep.tile([P, T + WORD_WINDOW + 1], I32, name="dy_w", align_bytes=64)
         w2_planes = [keep.tile([P, plane_bytes + 4], U8, name="w2_plane%d" % h, align_bytes=64) for h in range(2)]
         w2_s = [plane[:, 0:plane_bytes].rearrange("p (g i) -> p g i", i=HALF_H) for plane in w2_planes]
         w2_early = [
@@ -87,10 +88,11 @@ def tile_moe_sub_silu_kernel(
         make_identity(nc, ident[:])
         nc.gpsimd.memset(w2_planes[0][:].bitcast(I32), 0)
         nc.gpsimd.memset(slot_s[:].bitcast(I32), 0)
+        nc.gpsimd.memset(w2_planes[1][:].bitcast(I32), 0)
         nc.gpsimd.memset(w1_s[:].bitcast(I32), 0)
         nc.vector.memset(dy_s[:, T:].bitcast(I32), 0)
         nc.vector.memset(dy_s[0:ROWS_AT, 0 : T + 4].bitcast(I32), 0)
-        nc.vector.memset(w2_planes[1][:].bitcast(I32), 0)
+        nc.vector.memset(dy_w[:, PASSES * T :], 0)
 
         nc.sync.dma_start(dy_s[ROWS_AT:P, 0:T].bitcast(I32), dy_scales.rearrange("s b t -> b s t").bitcast(I32))
         nc.sync.dma_start(offs_sb[:], offs)
@@ -105,8 +107,8 @@ def tile_moe_sub_silu_kernel(
         nc.sync.dma_start(gate_rows[0:BLOCKS, :, :], gate[:, 0, :].rearrange("r (b t) -> b r t", t=P))
         a_by_tile = a[:, 0 : SHARED * P].rearrange("(j p) t -> p j t", p=P)
         nc.sync.dma_start(a_rows[:, 0:2, :], a_by_tile[:, 0:2, :])
-        load_words(0)
         nc.sync.dma_start(a_rows[:, 2:HT, :], a_by_tile[:, 2:HT, :])
+        load_words(0)
         load_words(1)
 
         def load_w2_scales(h):
@@ -140,11 +142,11 @@ def tile_moe_sub_silu_kernel(
 
         def gather_words(s, first, n):
             entries = offs_sb[:, first // PER_COL : (first + n) // PER_COL]
-            window = dy_w[:, word_at[s] :].bitcast(U32)
+            window = dy_w[:, word_at[s] : word_at[s] + WORD_WINDOW].bitcast(U32)
             nc.vector.tensor_copy(slot_w[s][:, first : first + n].bitcast(U32), window.indirect(entries))
 
-        for first in range(0, SLOTS, NARROW):
-            gather_words(0, first, NARROW)
+        for first in range(0, SLOTS, WIDE):
+            gather_words(0, first, WIDE)
         for first, count in FIRST_PARTS:
             gather_words(1, first * C, count * C)
 
@@ -195,9 +197,14 @@ def tile_moe_sub_silu_kernel(
 
         for b in range(SHARED):
             activate(b, silu_neg[b], ACT.Silu, -1.0)
+        shifted_first = keep.tile([P, H], F32, name="shifted_first", align_bytes=64)
+        nc.gpsimd.tensor_scalar(shifted_first[:], silu_neg[0], -1.0, 1.0, ALU.mult, ALU.add)
         for b in range(BLOCKS):
             activate(b, sig[b], ACT.Sigmoid, 1.0)
-        nc.vector.scalar_tensor_tensor(slope_shared[:], silu_shared[:], 1.0, sig_shared[:], ALU.subtract, ALU.mult)
+        nc.gpsimd.tensor_tensor(slope[0], shifted_first[:], sig[0], ALU.mult)
+        nc.vector.scalar_tensor_tensor(
+            slope_shared[:, H:], silu_shared[:, H:], 1.0, sig_shared[:, H:], ALU.subtract, ALU.mult
+        )
 
         w1_w = keep.tile([P, 2 * K], U8, name="w1_w", align_bytes=64)
         nc.sync.dma_start(w1_w[:].bitcast(I32), w1t_words[0].bitcast(I32))
@@ -295,6 +302,9 @@ def tile_moe_sub_silu_kernel(
 
         def slope_times_sums(b):
             da_t = ring.tile([P, H], BF16, name="da_t", align_bytes=64)
+            if b == 0:
+                nc.vector.tensor_tensor(as_pairs(da_t[:]), by_pairs(sums[b][:]), as_pairs(slope[b]), ALU.mult)
+                return da_t
             for u in range(PAIRS):
                 nc.vector.scalar_tensor_tensor(
                     as_pairs(da_t[:])[:, u],
@@ -348,12 +358,11 @@ def tile_moe_sub_silu_kernel(
         first_tile(0, 0)
         first_tile(1, 0)
         first_tile(0, 1)
-        ahead = multiply(1, 0, 2, 3)
         for k in range(2, len(FIRST_PARTS)):
             first_tile(k, 0)
         for k in range(1, len(FIRST_PARTS)):
             first_tile(k, 1)
-        fetch_sums(1, 0, 2, ahead)
+        product(1, 0, 3)
         product(1, 1, 4)
         product(1, 2, 5)
         fetch_plain(0)

@@ -50,7 +50,7 @@ def tile_moe_sub_silu_kernel(
 
         plane_bytes = E * PASSES * HALF_H
         a_at = 0
-        tail_at = BLOCKS * H * 4
+        tail_at = (BLOCKS + 1) * H * 4
         offs_sb = keep.tile([P, SLOTS // PER_COL], U16, name="offs_sb")
         pos_sb = [keep.tile([P, T // PER_COL], U16, name="pos_sb%d" % r) for r in range(TOP)]
         dy_s = keep.tile([P, BYTE_WINDOW], U8, name="dy_s", align_bytes=64)
@@ -66,10 +66,12 @@ def tile_moe_sub_silu_kernel(
         picked_s = keep.tile([P, SLOTS], U8, name="picked_s", align_bytes=64)
         slot_s = keep.tile([P, PASSES, SLOTS], U8, name="slot_s", align_bytes=64)
         y = [keep.tile([P, SLOTS], F32, name="y%d" % j, align_bytes=64) for j in range(HT)]
-        a_rows = placed.tile([P, HT, SHARED * P], F32, name="a_rows", align_bytes=64, offset=a_at)
+        a_first = placed.tile([P, HT, P], F32, name="a_first", align_bytes=64, offset=a_at)
+        a_next = placed.tile([P, HT, LONE * P], F32, name="a_next", align_bytes=64, offset=a_at + H * 4)
+        a_rows = [a_first[:], a_next[:, :, 0:P], a_next[:, :, P:]]
         a_last = keep.tile([P, PACK, P], F32, name="a_last", align_bytes=64)
-        sig_last = placed.tile([P, H], F32, name="sig_last", align_bytes=64, offset=a_at)
-        sig_shared = placed.tile([P, SHARED * H], F32, name="sig_shared", align_bytes=64, offset=a_at + H * 4)
+        sig_last = placed.tile([P, H], F32, name="sig_last", align_bytes=64, offset=a_at + H * 4)
+        sig_shared = placed.tile([P, SHARED * H], F32, name="sig_shared", align_bytes=64, offset=a_at + 2 * H * 4)
         silu_shared = keep.tile([P, SHARED * H], F32, name="silu_shared", align_bytes=64)
         silu_last = keep.tile([P, H], F32, name="silu_last", align_bytes=64)
         slope_shared = keep.tile([P, SHARED * H], F32, name="slope_shared", align_bytes=64)
@@ -105,9 +107,8 @@ def tile_moe_sub_silu_kernel(
 
         nc.sync.dma_start(a_last[:], a[:, SHARED * P : T].rearrange("(p d) t -> p d t", d=PACK))
         nc.sync.dma_start(gate_rows[0:BLOCKS, :, :], gate[:, 0, :].rearrange("r (b t) -> b r t", t=P))
-        a_by_tile = a[:, 0 : SHARED * P].rearrange("(j p) t -> p j t", p=P)
-        nc.sync.dma_start(a_rows[:, 0:2, :], a_by_tile[:, 0:2, :])
-        nc.sync.dma_start(a_rows[:, 2:HT, :], a_by_tile[:, 2:HT, :])
+        nc.sync.dma_start(a_first[:], a[:, 0:P].rearrange("(j p) t -> p j t", p=P))
+        nc.sync.dma_start(a_next[:], a[:, P : SHARED * P].rearrange("(j p) t -> p j t", p=P))
         load_words(0)
         load_words(1)
 
@@ -176,27 +177,30 @@ def tile_moe_sub_silu_kernel(
         a_turned = [bank(b, [P, H]) for b in range(SHARED)]
         activate(SHARED, silu_neg[SHARED], ACT.Silu, -1.0)
         shifted = keep.tile([P, H], F32, name="shifted", align_bytes=64)
-        nc.scalar.activation(shifted[:], silu_last[:], ACT.Copy, scale=-1.0, bias=1.0)
+        nc.gpsimd.tensor_scalar(shifted[:], silu_last[:], -1.0, 1.0, ALU.mult, ALU.add)
         gate_turned = bank(7, [P, TOP, P])
         for r in range(TOP):
             nc.tensor.transpose(gate_turned[:, r, :], gate_rows[:, r, :], ident[:])
         gate_t = keep.tile([P, TOP, BLOCKS], F32, name="gate_t", align_bytes=64)
         nc.scalar.copy(gate_t[:], gate_turned[:, :, 0:BLOCKS])
-        for r in range(TOP):
+
+        def spread_gate(r):
             spread = bank(QUADS + r, [P, SHARED, P])
             for b in range(SHARED):
                 nc.tensor.transpose(spread[:, b, :], gate_t[:, r, b : b + 1].to_broadcast([P, P]), ident[:])
             nc.scalar.copy(gate_sb[:, r, :], spread[:].rearrange("p b t -> p (b t)"))
 
-        for half in range(0, HT, 2):
-            for b in range(SHARED):
-                for j in (half, half + 1):
-                    nc.tensor.transpose(
-                        a_turned[b][:, j * P : (j + 1) * P], a_rows[:, j, b * P : (b + 1) * P], ident[:]
-                    )
-
-        for b in range(SHARED):
+        def turn_a(b):
+            for j in range(HT):
+                nc.tensor.transpose(a_turned[b][:, j * P : (j + 1) * P], a_rows[b][:, j, :], ident[:])
             activate(b, silu_neg[b], ACT.Silu, -1.0)
+
+        turn_a(0)
+        spread_gate(0)
+        spread_gate(1)
+        turn_a(1)
+        turn_a(2)
+        spread_gate(2)
         shifted_first = keep.tile([P, H], F32, name="shifted_first", align_bytes=64)
         nc.gpsimd.tensor_scalar(shifted_first[:], silu_neg[0], -1.0, 1.0, ALU.mult, ALU.add)
         for b in range(BLOCKS):

from contextlib import ExitStack

import concourse.mybir as mybir
from concourse.masks import make_identity

K, T, E, C, H, N, TOP = 128, 512, 6, 256, 512, 1024, 3
SLOTS = E * C
FLOPS = 2 * N * H * SLOTS + 2 * H * K * T

F32 = mybir.dt.float32
BF16 = mybir.dt.bfloat16
I32 = mybir.dt.int32
U32 = mybir.dt.uint32
U16 = mybir.dt.uint16
U8 = mybir.dt.uint8
FP8X4 = mybir.dt.float8_e4m3fn_x4
FP4X4 = mybir.dt.float4_e2m1fn_x4
ACT = mybir.ActivationFunctionType
ALU = mybir.AluOpType

P = 128
PACK = 4
PASSES = N // (P * PACK)
QUADS = 4
HT = H // P
BLOCKS = T // P
PER_COL = 16
FIRST_PARTS = ((0, 2), (2, 2), (4, 1), (5, 1))
WIDE = 768
WORD_WINDOW = 1024
BYTE_WINDOW = 2052
ROWS_AT = 96
HALF_H = H // 2
BANK = 2048
SHARED = BLOCKS - 1
LONE = SHARED - 1
PAIRS = PACK // 2


def tile_moe_sub_silu_kernel(
    tc, dy_words, dy_scales, w2t_words, w2t_scales, w1t_words, w1t_scales, a, gate, offs, pos1, pos2, pos3, out
):
    nc = tc.nc
    with ExitStack() as ctx:
        keep = ctx.enter_context(tc.tile_pool(name="keep", bufs=1))
        placed = ctx.enter_context(tc.tile_pool(name="placed", bufs=1))
        ring = ctx.enter_context(tc.tile_pool(name="ring", bufs=3))
        picks = ctx.enter_context(tc.tile_pool(name="picks", bufs=15))
        psum = ctx.enter_context(tc.psum_pool(name="psum", bufs=1))

        plane_bytes = E * PASSES * HALF_H
        a_at = 0
        tail_at = (BLOCKS + 1) * H * 4
        offs_sb = keep.tile([P, SLOTS // PER_COL], U16, name="offs_sb")
        pos_sb = [keep.tile([P, T // PER_COL], U16, name="pos_sb%d" % r) for r in range(TOP)]
        dy_s = keep.tile([P, BYTE_WINDOW], U8, name="dy_s", align_bytes=64)
        dy_w = keep.tile([P, T + WORD_WINDOW + 1], I32, name="dy_w", align_bytes=64)
        w2_planes = [keep.tile([P, plane_bytes + 4], U8, name="w2_plane%d" % h, align_bytes=64) for h in range(2)]
        w2_s = [plane[:, 0:plane_bytes].rearrange("p (g i) -> p g i", i=HALF_H) for plane in w2_planes]
        w2_early = [
            keep.tile([P, 2 * PASSES, 2 * HALF_H], U8, name="w2_early%d" % pair, align_bytes=64)
            for pair in range(E // 2)
        ]
        w2_late = keep.tile([P, E * PASSES, 2 * HALF_H], U8, name="w2_late", align_bytes=64)
        slot_w = [keep.tile([P, SLOTS], I32, name="slot_w%d" % s, align_bytes=64) for s in range(PASSES)]
        picked_s = keep.tile([P, SLOTS], U8, name="picked_s", align_bytes=64)
        slot_s = keep.tile([P, PASSES, SLOTS], U8, name="slot_s", align_bytes=64)
        y = [keep.tile([P, SLOTS], F32, name="y%d" % j, align_bytes=64) for j in range(HT)]
        a_first = placed.tile([P, HT, P], F32, name="a_first", align_bytes=64, offset=a_at)
        a_next = placed.tile([P, HT, LONE * P], F32, name="a_next", align_bytes=64, offset=a_at + H * 4)
        a_rows = [a_first[:], a_next[:, :, 0:P], a_next[:, :, P:]]
        a_last = keep.tile([P, PACK, P], F32, name="a_last", align_bytes=64)
        sig_last = placed.tile([P, H], F32, name="sig_last", align_bytes=64, offset=a_at + H * 4)
        sig_shared = placed.tile([P, SHARED * H], F32, name="sig_shared", align_bytes=64, offset=a_at + 2 * H * 4)
        silu_shared = keep.tile([P, SHARED * H], F32, name="silu_shared", align_bytes=64)
        silu_last = keep.tile([P, H], F32, name="silu_last", align_bytes=64)
        slope_shared = keep.tile([P, SHARED * H], F32, name="slope_shared", align_bytes=64)
        slope_last = placed.tile([P, H], F32, name="slope_last", align_bytes=64, offset=tail_at)

        def by_block(shared, last):
            return [shared[:, b * H : (b + 1) * H] for b in range(SHARED)] + [last[:]]

        sig, silu_neg = by_block(sig_shared, sig_last), by_block(silu_shared, silu_last)
        slope = by_block(slope_shared, slope_last)
        w1_s = keep.tile([P, K], U8, name="w1_s", align_bytes=64)
        ident = keep.tile([P, P], F32, name="ident")

        gate_rows = keep.tile([P, TOP, P], F32, name="gate_rows", align_bytes=64)
        nc.gpsimd.memset(gate_rows[:], 0.0)
        make_identity(nc, ident[:])
        nc.gpsimd.memset(w2_planes[0][:].bitcast(I32), 0)
        nc.gpsimd.memset(slot_s[:].bitcast(I32), 0)
        nc.gpsimd.memset(w2_planes[1][:].bitcast(I32), 0)
        nc.gpsimd.memset(w1_s[:].bitcast(I32), 0)
        nc.vector.memset(dy_s[:, T:].bitcast(I32), 0)
        nc.vector.memset(dy_s[0:ROWS_AT, 0 : T + 4].bitcast(I32), 0)
        nc.vector.memset(dy_w[:, PASSES * T :], 0)

        nc.sync.dma_start(dy_s[ROWS_AT:P, 0:T].bitcast(I32), dy_scales.rearrange("s b t -> b s t").bitcast(I32))
        nc.sync.dma_start(offs_sb[:], offs)
        word_at = (T, 0)

        def load_words(s):
            nc.sync.dma_start(
                dy_w[:, word_at[s] : word_at[s] + T], dy_words[s].rearrange("p t d -> p (t d)").bitcast(I32)
            )

        nc.sync.dma_start(a_last[:], a[:, SHARED * P : T].rearrange("(p d) t -> p d t", d=PACK))
        nc.sync.dma_start(gate_rows[0:BLOCKS, :, :], gate[:, 0, :].rearrange("r (b t) -> b r t", t=P))
        nc.sync.dma_start(a_first[:], a[:, 0:P].rearrange("(j p) t -> p j t", p=P))
        nc.sync.dma_start(a_next[:], a[:, P : SHARED * P].rearrange("(j p) t -> p j t", p=P))
        load_words(0)
        load_words(1)

        def load_w2_scales(h):
            cols = slice(h * HALF_H, (h + 1) * HALF_H)
            by_row = w2t_scales[:, :, :, cols].rearrange("e s (q r) i -> r q (e s) i", r=4)
            for r in range(4):
                nc.sync.dma_start(w2_s[h][r:P:32, :, :].bitcast(I32), by_row[r].bitcast(I32))

        def load_w2_words(target, experts, h):
            cols = slice(2 * h * HALF_H, 2 * (h + 1) * HALF_H)
            nc.sync.dma_start(
                target[:].bitcast(I32), w2t_words[experts, :, :, cols].rearrange("e s p b -> p (e s) b").bitcast(I32)
            )

        load_w2_scales(0)
        load_w2_words(w2_early[0], slice(0, 2), 0)

        nc.vector.tensor_copy(picked_s[:], dy_s[:].indirect(offs_sb[:]))
        for q in (0, 2, 1, 3):
            nc.sync.dma_start(
                slot_s[32 * q : 32 * q + 4, :, :].bitcast(I32),
                picked_s[ROWS_AT + 8 * q : ROWS_AT + 8 * q + 8, :].bitcast(I32),
            )
        for pair in range(1, E // 2):
            load_w2_words(w2_early[pair], slice(2 * pair, 2 * pair + 2), 0)
        for r, pos in enumerate((pos1, pos2, pos3)):
            nc.sync.dma_start(pos_sb[r][:], pos)
        gate_sb = placed.tile([P, TOP, SHARED * P], F32, name="gate_sb", align_bytes=64, offset=tail_at)
        load_w2_scales(1)
        load_w2_words(w2_late, slice(0, E), 1)

        def gather_words(s, first, n):
            entries = offs_sb[:, first // PER_COL : (first + n) // PER_COL]
            window = dy_w[:, word_at[s] : word_at[s] + WORD_WINDOW].bitcast(U32)
            nc.vector.tensor_copy(slot_w[s][:, first : first + n].bitcast(U32), window.indirect(entries))

        for first in range(0, SLOTS, WIDE):
            gather_words(0, first, WIDE)
        for first, count in FIRST_PARTS:
            gather_words(1, first * C, count * C)

        banks_used = []

        def bank(number, shape):
            banks_used.append(number)
            return psum.tile(shape, F32, name="bank%d" % len(banks_used), offset=number * BANK)

        def by_pairs(ap):
            return ap.rearrange("t (p u e) -> t u p e", u=PAIRS, e=2)

        def as_pairs(ap):
            return ap.rearrange("t (u p e) -> t u p e", u=PAIRS, e=2)

        def activate(b, target, func, scale):
            if b < SHARED:
                nc.scalar.activation(as_pairs(target), by_pairs(a_turned[b][:]), func, scale=scale)
            else:
                nc.scalar.activation(
                    target.rearrange("p (c i d) -> p c d i", i=PACK, d=PACK),
                    a_last[:].rearrange("p d (c i) -> p c d i", i=PACK),
                    func,
                    scale=scale,
                )

        a_turned = [bank(b, [P, H]) for b in range(SHARED)]
        activate(SHARED, silu_neg[SHARED], ACT.Silu, -1.0)
        shifted = keep.tile([P, H], F32, name="shifted", align_bytes=64)
        nc.gpsimd.tensor_scalar(shifted[:], silu_last[:], -1.0, 1.0, ALU.mult, ALU.add)
        gate_turned = bank(7, [P, TOP, P])
        for r in range(TOP):
            nc.tensor.transpose(gate_turned[:, r, :], gate_rows[:, r, :], ident[:])
        gate_t = keep.tile([P, TOP, BLOCKS], F32, name="gate_t", align_bytes=64)
        nc.scalar.copy(gate_t[:], gate_turned[:, :, 0:BLOCKS])

        def spread_gate(r):
            spread = bank(QUADS + r, [P, SHARED, P])
            for b in range(SHARED):
                nc.tensor.transpose(spread[:, b, :], gate_t[:, r, b : b + 1].to_broadcast([P, P]), ident[:])
            nc.scalar.copy(gate_sb[:, r, :], spread[:].rearrange("p b t -> p (b t)"))

        def turn_a(b):
            for j in range(HT):
                nc.tensor.transpose(a_turned[b][:, j * P : (j + 1) * P], a_rows[b][:, j, :], ident[:])
            activate(b, silu_neg[b], ACT.Silu, -1.0)

        turn_a(0)
        spread_gate(0)
        spread_gate(1)
        turn_a(1)
        turn_a(2)
        spread_gate(2)
        shifted_first = keep.tile([P, H], F32, name="shifted_first", align_bytes=64)
        nc.gpsimd.tensor_scalar(shifted_first[:], silu_neg[0], -1.0, 1.0, ALU.mult, ALU.add)
        for b in range(BLOCKS):
            activate(b, sig[b], ACT.Sigmoid, 1.0)
        nc.gpsimd.tensor_tensor(slope[0], shifted_first[:], sig[0], ALU.mult)
        nc.vector.scalar_tensor_tensor(
            slope_shared[:, H:], silu_shared[:, H:], 1.0, sig_shared[:, H:], ALU.subtract, ALU.mult
        )

        w1_w = keep.tile([P, 2 * K], U8, name="w1_w", align_bytes=64)
        nc.sync.dma_start(w1_w[:].bitcast(I32), w1t_words[0].bitcast(I32))
        for q in range(QUADS):
            nc.sync.dma_start(
                w1_s[32 * q : 32 * q + 4, :].bitcast(I32), w1t_scales[0, 4 * q : 4 * q + 4, :].bitcast(I32)
            )

        def one_pass(j, target, slot, width, s, opens, closes):
            h, col = divmod(j * P, HALF_H)
            e = slot // C
            words = w2_late[:, e * PASSES + s, :] if h else w2_early[e // 2][:, (e % 2) * PASSES + s, :]
            nc.tensor.matmul_mx(
                out=target,
                lhsT=words[:, 2 * col : 2 * (col + P)].bitcast(FP4X4),
                lhsT_scale=w2_s[h][:, e * PASSES + s, col : col + P],
                rhs=slot_w[s][:, slot : slot + width].bitcast(FP8X4),
                rhs_scale=slot_s[:, s, slot : slot + width],
                start=opens,
                stop=closes,
            )

        def multiply(j, first, count, number):
            y_bank = bank(number, [P, count * C])
            for u in range(count):
                for s in range(PASSES):
                    one_pass(j, y_bank[:, u * C : (u + 1) * C], (first + u) * C, C, s, s == 0, s == PASSES - 1)
            return y_bank

        def fetch_sums(j, first, count, y_bank):
            nc.scalar.copy(y[j][:, first * C : (first + count) * C], y_bank[:])

        def product(j, pair, number):
            fetch_sums(j, 2 * pair, 2, multiply(j, 2 * pair, 2, number))

        def listed(r, b0, nb):
            return pos_sb[r][:, b0 * P // PER_COL : (b0 + nb) * P // PER_COL]

        gated = {}

        def fetch_gated(j, r, b0, nb):
            picked = picks.tile([P, nb * P], F32, name="gated")
            nc.vector.tensor_tensor(
                picked[:], y[j][:].indirect(listed(r, b0, nb)), gate_sb[:, r, b0 * P : (b0 + nb) * P], ALU.mult
            )
            for b in range(nb):
                gated[j, r, b0 + b] = picked[:, b * P : (b + 1) * P]

        def turn_gated(j, r, b):
            nc.tensor.matmul(
                sums[b][:, j * P : (j + 1) * P],
                lhsT=gated[j, r, b],
                rhs=ident[:],
                is_transpose=True,
                start=(r == 0),
                stop=(r == TOP - 1),
            )

        def combine(j, r, b0, nb):
            fetch_gated(j, r, b0, nb)
            for b in range(b0, b0 + nb):
                turn_gated(j, r, b)

        plains = {}

        def fetch_plain(j, choices=range(TOP)):
            for r in choices:
                plains[j, r] = picks.tile([P, P], F32, name="plain")
                nc.scalar.activation(plains[j, r][:], y[j][:].indirect(listed(r, SHARED, 1)), ACT.Copy)

        def turn_plain(j, choices=range(TOP)):
            for r in choices:
                nc.tensor.transpose(apart[r][:, j, :], plains[j, r][:], ident[:])

        weighed = [keep.tile([P, PACK, P], F32, name="weighed%d" % r, align_bytes=64) for r in range(TOP)]

        def weigh(r):
            nc.scalar.activation(
                weighed[r][:],
                apart[r][:].rearrange("t j (m d) -> t d (j m)", d=PACK),
                ACT.Copy,
                scale=gate_t[:, r, SHARED : SHARED + 1],
            )

        def add_back(r, back):
            for d in range(PACK):
                nc.tensor.matmul(
                    back[:, d, :],
                    lhsT=weighed[r][:, d, :],
                    rhs=ident[:],
                    is_transpose=True,
                    start=(r == 0 and d == 0),
                    stop=(r == TOP - 1 and d == PACK - 1),
                )

        def slope_times_sums(b):
            da_t = ring.tile([P, H], BF16, name="da_t", align_bytes=64)
            if b == 0:
                nc.vector.tensor_tensor(as_pairs(da_t[:]), by_pairs(sums[b][:]), as_pairs(slope[b]), ALU.mult)
                return da_t
            for u in range(PAIRS):
                nc.vector.scalar_tensor_tensor(
                    as_pairs(da_t[:])[:, u],
                    by_pairs(sums[b][:])[:, u],
                    -1.0,
                    as_pairs(slope[b])[:, u],
                    ALU.mult,
                    ALU.mult,
                )
            return da_t

        def turn_pairs(da_t, number):
            back = bank(number, [P, PAIRS, P])
            for u in range(PAIRS):
                nc.tensor.transpose(back[:, u, :], da_t[:].bitcast(F32)[:, u * P : (u + 1) * P], ident[:])
            return back

        def lay_pairs(da, k, back):
            words = da[:].bitcast(F32)[:, k * P * PAIRS : (k + 1) * P * PAIRS]
            nc.scalar.copy(words.rearrange("p (t u) -> p t u", u=PAIRS), back[:].rearrange("p u t -> p t u"))

        def project(b0, nb, da, number, copy):
            da_w = ring.tile([P, nb * P], U32, name="da_w", align_bytes=64)
            da_s = ring.tile([P, nb * P], U8, name="da_s", align_bytes=64)
            nc.vector.quantize_mx(out=da_w[:].bitcast(FP8X4), scales=da_s[:], in_=da[:])
            res_bank = bank(number, [P, nb * P])
            nc.tensor.matmul_mx(
                out=res_bank[:],
                lhsT=w1_w[:].bitcast(FP4X4),
                lhsT_scale=w1_s[:],
                rhs=da_w[:].bitcast(FP8X4),
                rhs_scale=da_s[:],
                start=True,
                stop=True,
            )
            res = ring.tile([P, nb * P], F32, name="res")
            copy(res[:], res_bank[:])
            nc.sync.dma_start(out[:, b0 * P : (b0 + nb) * P], res[:])

        on_scalar, on_vector = nc.scalar.copy, nc.vector.tensor_copy
        opened = [bank(QUADS + k, [P, count * C]) for k, (first, count) in enumerate(FIRST_PARTS)]

        def first_tile(k, s):
            first, count = FIRST_PARTS[k]
            for u in range(count):
                target = opened[k][:, u * C : (u + 1) * C]
                one_pass(0, target, (first + u) * C, C, s, s == 0 and u == 0, s == PASSES - 1 and u == count - 1)
            if s == PASSES - 1:
                fetch_sums(0, first, count, opened[k])

        first_tile(0, 0)
        first_tile(1, 0)
        first_tile(0, 1)
        for k in range(2, len(FIRST_PARTS)):
            first_tile(k, 0)
        for k in range(1, len(FIRST_PARTS)):
            first_tile(k, 1)
        product(1, 0, 3)
        product(1, 1, 4)
        product(1, 2, 5)
        fetch_plain(0)
        for pair in range(E // 2):
            product(2, pair, pair)
        for pair, number in enumerate((6, 7, 5)):
            product(3, pair, number)
        sums = [bank(b, [P, H]) for b in range(SHARED)]
        apart = [bank(number, [P, HT, P]) for number in (5, 6, 7)]
        for r in range(TOP):
            combine(0, r, 0, SHARED)
        turn_plain(0)
        for r in range(TOP):
            combine(1, r, 0, SHARED)
        fetch_plain(1)
        turn_plain(1)

        def late_plain(r):
            for j in (2, 3):
                fetch_plain(j, [r])
                turn_plain(j, [r])

        combine(2, 0, 0, SHARED)
        combine(2, 1, 0, SHARED)
        late_plain(0)
        combine(2, 2, 0, SHARED)
        late_plain(1)
        combine(3, 0, 0, LONE)
        late_plain(2)
        combine(3, 1, 0, LONE)
        back_last = bank(4, [P, PACK, P])
        weigh(0)
        combine(3, 2, 0, LONE)
        add_back(0, back_last)
        combine(3, 0, LONE, 1)
        weigh(1)
        combine(3, 1, LONE, 1)
        combine(3, 2, LONE, 1)
        add_back(1, back_last)
        weigh(2)
        nc.gpsimd.tensor_tensor(slope_last[:], shifted[:], sig_last[:], ALU.mult)
        da_pair = keep.tile([P, LONE * H], BF16, name="da_pair", align_bytes=64)
        da_lone = keep.tile([P, H], BF16, name="da_lone", align_bytes=64)
        da_last = keep.tile([P, H], BF16, name="da_last", align_bytes=64)
        lay_pairs(da_pair, 0, turn_pairs(slope_times_sums(0), 3))
        add_back(2, back_last)
        lay_pairs(da_pair, 1, turn_pairs(slope_times_sums(1), 5))
        lay_pairs(da_lone, 0, turn_pairs(slope_times_sums(LONE), 6))
        nc.vector.tensor_tensor(
            da_last[:].rearrange("p (t d) -> p t d", d=PACK),
            back_last[:].rearrange("p d t -> p t d"),
            slope_last[:].rearrange("p (t d) -> p t d", d=PACK),
            ALU.mult,
        )
        project(0, LONE, da_pair, 0, on_scalar)
        project(SHARED, 1, da_last, 1, on_scalar)
        project(LONE, 1, da_lone, 2, on_vector)
